import numpy as np
import ml_dtypes


def mxq(x, axis, fmt="e4m3"):
    dtype, down = {"e4m3": (ml_dtypes.float8_e4m3fn, 7), "e5m2": (ml_dtypes.float8_e5m2, 14)}[fmt]
    v = np.moveaxis(np.asarray(x, np.float32).astype(ml_dtypes.bfloat16).astype(np.float64), axis, -1)
    blocks = v.reshape(v.shape[:-1] + (-1, 32))
    amax = np.abs(blocks).max(-1, keepdims=True)
    byte = np.maximum(np.where(amax > 0, np.frexp(amax)[1] - 1 + 127, 0) - down, 1)
    scale = np.exp2(byte - 127.0)
    codes = (blocks / scale).astype(np.float32).astype(dtype).astype(np.float64)
    return np.moveaxis((codes * scale).reshape(v.shape), -1, axis)


WIDE = False


def mx_kscale(k):
    if not WIDE:
        return np.ones(k)
    levels = np.array([10, -10, 5, -5, 0])
    if k % 512:
        return np.exp2(np.random.permutation(np.resize(levels, k // 32))).repeat(32)
    a = np.empty((k // 512, 16))
    for p in range(k // 512):
        a[p, :8] = np.random.permutation(np.resize(levels, 8))
        for g in range(8):
            far = levels[np.abs(levels - a[p, g]) >= 10]
            a[p, g + 8] = far[np.random.randint(len(far))]
    return np.exp2(a.ravel()).repeat(32)


BF16 = ml_dtypes.bfloat16


def bf(x):
    return np.asarray(x, np.float32).astype(BF16)


def f64(x):
    return np.asarray(x).astype(np.float64)

def planes(Y):
    n, m = Y.shape
    b = f64(bf(Y)).reshape(n // 32, 32, m)
    amax = np.abs(b).max(1)
    byte = np.clip(np.where(amax > 0, np.frexp(amax)[1] - 1 + 127 - 7, 1), 1, 254)
    codes = (b * np.exp2(127.0 - byte)[:, None, :]).reshape(n, m).astype(np.float32).astype(ml_dtypes.float8_e4m3fn).view(np.uint8)
    words = codes.reshape(n // 512, 128, 4, m).transpose(0, 1, 3, 2)
    return np.ascontiguousarray(words), np.ascontiguousarray(byte.astype(np.uint8).reshape(n // 512, 16, m))


N, M, D = 1024, 1024, 1024


def sigmoid(a):
    return 1.0 / (1.0 + np.exp(-a))


def setup_inputs():
    s, t = mx_kscale(D), mx_kscale(M)
    return {"z": bf(np.random.standard_normal((N, D)) * s[None, :]),
            "y": bf(np.random.standard_normal((M, D))),
            "adj": bf(np.random.uniform(0.0, 1.0, (N, M))),
            "g": bf((1.0 + 0.1 * np.random.standard_normal(D)) / s),
            "bj": bf(0.5 * np.random.standard_normal(M)),
            "v": bf((1.0 + 0.1 * np.random.standard_normal(M)) * t),
            "r": bf((1.0 + 0.1 * np.random.standard_normal(M)) / t)}


def core(z, y, adj, g, bj, v, r):
    z, y, adj, g, bj, v, r = f64(z), f64(y), f64(adj), f64(g), f64(bj), f64(v), f64(r)
    d = z.shape[1]
    m = y.shape[0]
    yg = y * g[None, :]
    sc = mxq(z, 1, "e4m3") @ mxq(yg, 1, "e4m3").T
    pr = sigmoid(sc / np.sqrt(d) + bj[None, :])
    res = (pr - adj) * v[None, :]
    yr = y * r[:, None]
    return (mxq(res, 1, "e4m3") @ mxq(yr, 0, "e4m3")) / np.sqrt(m)


def reference(z, y, adj, g, bj, v, r):
    R_out = core(z, y, adj, g, bj, v, r)
    words, scales = planes(R_out.T)
    return R_out, words, scales

@@ -1,0 +1,330 @@
+from contextlib import ExitStack
+
+import concourse.mybir as mybir
+from concourse.masks import make_identity
+
+N, M, D = 1024, 1024, 1024
+FLOPS = 2 * N * M * D + 2 * N * M * D
+
+F32 = mybir.dt.float32
+BF16 = mybir.dt.bfloat16
+U32 = mybir.dt.uint32
+I32 = mybir.dt.int32
+U8 = mybir.dt.uint8
+FP8X4 = mybir.dt.float8_e4m3fn_x4
+ACT = mybir.ActivationFunctionType
+ALU = mybir.AluOpType
+
+P = 128
+CH = 256
+NCH = N // CH
+WIDE = (False, True)
+
+
+def tile_innerproductsigmoidresidualprojection_kernel(tc, z, y, adj, g, bj, v, r, out_0, out_1, out_2):
+    nc = tc.nc
+    with ExitStack() as ctx:
+        keep = ctx.enter_context(tc.tile_pool(name="keep", bufs=1))
+        work = ctx.enter_context(tc.tile_pool(name="work", bufs=2))
+        psum = ctx.enter_context(tc.psum_pool(name="psum", bufs=2))
+
+        y_raw = {}
+        z_raw = {}
+        a_raw = {}
+        vecs = {}
+        for name in ("r", "g", "bj", "v"):
+            vecs[name] = keep.tile([P, 2, 4], BF16, name="vec_" + name)
+        y_scaled = {}
+        yr_bf = {}
+        yr_codes = {}
+        yr_scales = {}
+        yg_bf = {}
+        yg_codes = {}
+        yg_scales = {}
+        for G in range(2):
+            y_scaled[G] = keep.tile([P, 4, D], BF16, name="y_scaled_%d" % G, align_bytes=64)
+            yr_bf[G] = keep.tile([P, D, 4], BF16, name="yr_bf_%d" % G, align_bytes=64)
+            yr_codes[G] = keep.tile([P, D], U32, name="yr_codes_%d" % G, align_bytes=64)
+            yr_scales[G] = keep.tile([P, D], U8, name="yr_scales_%d" % G, align_bytes=64)
+            yg_codes[G] = keep.tile([P, M], U32, name="yg_codes_%d" % G, align_bytes=64)
+            yg_scales[G] = keep.tile([P, M], U8, name="yg_scales_%d" % G, align_bytes=64)
+        out_scales = keep.tile([P, 2, N], U8, name="out_scales", align_bytes=64)
+        ident = keep.tile([P, P], F32, name="ident")
+        r_f32 = keep.tile([P, 2, 4], F32, name="r_f32")
+        warm = keep.tile([P, 1], F32, name="warm")
+
+        def new_raw():
+            return work.tile([P, 2, D], BF16, name="raw", align_bytes=64, bufs=10)
+
+        def load_y(G, jp):
+            y_raw[G, jp] = new_raw()
+            src = y[512 * G : 512 * G + 512, :].rearrange("(p j) d -> p j d", j=4)
+            nc.sync.dma_start(out=y_raw[G, jp][:], in_=src[:, 2 * jp : 2 * jp + 2, :])
+
+        def load_rows(dst, src, c):
+            dst[c] = new_raw()
+            nc.sync.dma_start(out=dst[c][:], in_=src[CH * c : CH * c + CH, :].rearrange("(p i) k -> p i k", i=2))
+
+        t_y = {}
+        t_z = {}
+        t_a = {}
+        t_s = {}
+        t_o = {}
+        t_p = {}
+        z_bf = {}
+        z_codes = {}
+        z_scales = {}
+        pr = {}
+        dd = {}
+        res_bf = {}
+        res_codes = {}
+        res_scales = {}
+        of = {}
+        cast = {}
+        p_bf = {}
+        p_codes = {}
+
+        def Y(G, jp):
+            for f in range(2):
+                bank = psum.tile([P, 2, CH], F32, name="bank_tr", tag="tr")
+                t_y[G, jp, f] = bank
+                for k in range(2):
+                    words = y_raw[G, jp][:, k, :].bitcast(F32)
+                    for u in range(2):
+                        nc.tensor.transpose(bank[:, u, P * k : P * k + P], words[:, 256 * f + u : 256 * f + 256 : 2], ident[:])
+
+        def Ye(G, jp):
+            for f in range(2):
+                if jp == 0:
+                    yg_bf[G, f] = work.tile([P, 512, 4], BF16, name="yg_bf", tag="f4k", align_bytes=64, bufs=4)
+                src = t_y[G, jp, f][:].rearrange("p u m -> p (u m)").bitcast(BF16).rearrange("p (u m e) -> p m u e", u=2, e=2)
+                dst = yg_bf[G, f][:, CH * jp : CH * jp + CH, :].rearrange("p m (u e) -> p m u e", u=2)
+                fac = vecs["g"][:, f, :].unsqueeze(1).to_broadcast([P, CH, 4]).rearrange("p m (u e) -> p m u e", u=2)
+                nc.vector.tensor_tensor(out=dst, in0=src, in1=fac, op=ALU.mult)
+
+        def Yq(G):
+            cols = slice(512 * G, 512 * G + 512)
+            for f in range(2):
+                nc.vector.quantize_mx(out=yg_codes[f][:, cols].bitcast(FP8X4), scales=yg_scales[f][:, cols], in_=yg_bf[G, f][:].rearrange("p m t -> p (m t)"))
+
+        def rows_to_banks(raw, store, c, tag):
+            for f in range(2):
+                bank = psum.tile([P, 2, CH], F32, name="bank_" + tag, tag=tag)
+                store[c, f] = bank
+                for i in range(2):
+                    words = raw[c][:, i, :].bitcast(F32)
+                    for u in range(2):
+                        nc.tensor.transpose(bank[:, u, P * i : P * i + P], words[:, 256 * f + u : 256 * f + 256 : 2], ident[:])
+
+        def Z(c):
+            rows_to_banks(z_raw, t_z, c, "tr")
+
+        def A(c):
+            rows_to_banks(a_raw, t_a, c, "a")
+
+        def z_slot(c, f):
+            h, k = divmod(c, 2)
+            return 2 * f + k if WIDE[h] else 2 * k + f
+
+        def Zc(c):
+            h, k = divmod(c, 2)
+            if k == 0:
+                z_bf[h] = work.tile([P, 4, CH, 4], BF16, name="z_bf", align_bytes=64, bufs=2)
+            for f in range(2):
+                nc.scalar.copy(out=z_bf[h][:, z_slot(c, f), :, :].rearrange("p n t -> p (n t)").bitcast(F32).rearrange("p (n u) -> p n u", u=2), in_=t_z[c, f][:].rearrange("p u n -> p n u"))
+
+        def Zq(c):
+            h, k = divmod(c, 2)
+            if k == 0:
+                z_codes[h] = work.tile([P, 4 * CH], U32, name="z_codes", align_bytes=64, bufs=2)
+                z_scales[h] = work.tile([P, 4 * CH], U8, name="z_scales", align_bytes=64, bufs=2)
+            cols = slice(2 * CH * k, 2 * CH * k + 2 * CH)
+            nc.vector.quantize_mx(out=z_codes[h][:, cols].bitcast(FP8X4), scales=z_scales[h][:, cols], in_=z_bf[h][:, 2 * k : 2 * k + 2, :, :].rearrange("p s n t -> p (s n t)"))
+
+        def YRs(G, slots, engine="V"):
+            for j in slots:
+                dst = y_scaled[G][:, j, :]
+                src = y_raw[G, j // 2][:, j % 2, :]
+                if engine == "V":
+                    nc.vector.tensor_scalar_mul(dst, src, vecs["r"][:, G, j : j + 1])
+                elif engine == "S":
+                    nc.scalar.activation(out=dst, in_=src, func=ACT.Copy, scale=r_f32[:, G, j : j + 1])
+                else:
+                    nc.gpsimd.tensor_scalar(out=dst, in0=src, scalar1=r_f32[:, G, j : j + 1], scalar2=0.0, op0=ALU.mult, op1=ALU.add)
+
+        def YRi(G, h, k, engine="S"):
+                cols = slice(512 * h + 256 * k, 512 * h + 256 * k + 256)
+                copy = nc.scalar.copy if engine == "S" else nc.vector.tensor_copy
+                copy(out=yr_bf[G][:, cols, :].rearrange("p (c i) t -> p c t i", i=4), in_=y_scaled[G][:, :, cols].rearrange("p t (c i) -> p c t i", i=4))
+
+        def YRq(G, h):
+            cols = slice(512 * h, 512 * h + 512)
+            nc.vector.quantize_mx(out=yr_codes[G][:, cols].bitcast(FP8X4), scales=yr_scales[G][:, cols], in_=yr_bf[G][:, cols, :].rearrange("p d t -> p (d t)"))
+
+        def S1(c, G):
+            h = c // 2
+            if WIDE[h]:
+                if c % 2 == 1:
+                    return
+                pr[h, G] = work.tile([P, 4, 2 * CH], F32, name="pr_wide", bufs=2)
+                for t in range(4):
+                    bank = psum.tile([P, 2 * CH], F32, name="bank_s", tag="s")
+                    m0 = 512 * G + P * t
+                    for f in range(2):
+                        nc.tensor.matmul_mx(out=bank[:], lhsT=yg_codes[f][:, m0 : m0 + P].bitcast(FP8X4), lhsT_scale=yg_scales[f][:, m0 : m0 + P], rhs=z_codes[h][:, 512 * f : 512 * f + 512].bitcast(FP8X4), rhs_scale=z_scales[h][:, 512 * f : 512 * f + 512], start=(f == 0), stop=(f == 1))
+                    nc.scalar.activation(out=pr[h, G][:, t, :], in_=bank[:], func=ACT.Sigmoid, bias=vecs["bj"][:, G, t : t + 1], scale=1.0 / 32.0)
+                return
+            for tp in range(2):
+                bank = psum.tile([P, 2, CH], F32, name="bank_s", tag="s")
+                t_s[c, G, tp] = bank
+                for k in range(2):
+                    m0 = 512 * G + P * (2 * tp + k)
+                    for f in range(2):
+                        nc.tensor.matmul_mx(out=bank[:, k, :], lhsT=yg_codes[f][:, m0 : m0 + P].bitcast(FP8X4), lhsT_scale=yg_scales[f][:, m0 : m0 + P], rhs=z_codes[h][:, CH * z_slot(c, f) : CH * z_slot(c, f) + CH].bitcast(FP8X4), rhs_scale=z_scales[h][:, CH * z_slot(c, f) : CH * z_slot(c, f) + CH], start=(f == 0), stop=(f == 1))
+
+        def Pr(c, G):
+            if WIDE[c // 2]:
+                return
+            pr[c, G, "n"] = work.tile([P, 4, CH], F32, name="pr", bufs=4)
+            for t in range(4):
+                nc.scalar.activation(out=pr[c, G, "n"][:, t, :], in_=t_s[c, G, t // 2][:, t % 2, :], func=ACT.Sigmoid, bias=vecs["bj"][:, G, t : t + 1], scale=1.0 / 32.0)
+
+        def R(c, G):
+            prob = pr[c // 2, G][:, :, CH * (c % 2) : CH * (c % 2) + CH] if WIDE[c // 2] else pr[c, G, "n"][:]
+            dd[c, G] = work.tile([P, 4, CH], F32, name="dd", bufs=3)
+            nc.vector.tensor_tensor(
+                out=dd[c, G][:].rearrange("p (u e) n -> p u e n", u=2),
+                in0=prob.rearrange("p (u e) n -> p u e n", u=2),
+                in1=t_a[c, G][:].rearrange("p u n -> p (u n)").bitcast(BF16).rearrange("p (u n e) -> p u e n", u=2, e=2),
+                op=ALU.subtract,
+            )
+
+        def Mu(c, G):
+            if c not in res_bf:
+                res_bf[c] = work.tile([P, 2, CH, 4], BF16, name="res_bf", align_bytes=64, bufs=2)
+            nc.vector.tensor_tensor(
+                out=res_bf[c][:, G, :, :].rearrange("p (c i) t -> p c t i", i=4),
+                in0=dd[c, G][:].rearrange("p t (c i) -> p c t i", i=4),
+                in1=vecs["v"][:, G, :].unsqueeze(1).unsqueeze(3).to_broadcast([P, CH // 4, 4, 4]),
+                op=ALU.mult,
+            )
+
+        def Rq(c):
+            res_codes[c] = work.tile([P, 2 * CH], U32, name="res_codes", align_bytes=64, bufs=4)
+            res_scales[c] = work.tile([P, 2 * CH], U8, name="res_scales", align_bytes=64, bufs=4)
+            nc.vector.quantize_mx(out=res_codes[c][:].bitcast(FP8X4), scales=res_scales[c][:], in_=res_bf[c][:].rearrange("p f n t -> p (f n t)"))
+
+        def O(c, i):
+            for h in range(2):
+                bank = psum.tile([P, 512], F32, name="bank_o", tag="o")
+                t_o[c, i, h] = bank
+                for G in range(2):
+                    nc.tensor.matmul_mx(out=bank[:], lhsT=res_codes[c][:, CH * G + P * i : CH * G + P * i + P].bitcast(FP8X4), lhsT_scale=res_scales[c][:, CH * G + P * i : CH * G + P * i + P], rhs=yr_codes[G][:, 512 * h : 512 * h + 512].bitcast(FP8X4), rhs_scale=yr_scales[G][:, 512 * h : 512 * h + 512], start=(G == 0), stop=(G == 1))
+
+        def Oe(c, i, engines="SS"):
+            of[c, i] = work.tile([P, D], F32, name="of", tag="f4k", align_bytes=64, bufs=4)
+            for h in range(2):
+                dst = of[c, i][:, 512 * h : 512 * h + 512]
+                if engines[h] == "S":
+                    nc.scalar.mul(dst, t_o[c, i, h][:], 1.0 / 32.0)
+                else:
+                    nc.vector.tensor_scalar_mul(dst, t_o[c, i, h][:], 1.0 / 32.0)
+            nc.sync.dma_start(out=out_0[CH * c : CH * c + CH, :].rearrange("(p i) d -> p i d", i=2)[:, i, :], in_=of[c, i][:])
+
+        def C(c, i, engine="V"):
+            cast[c, i] = work.tile([P, D], BF16, name="cast", align_bytes=64, bufs=4)
+            if engine == "S":
+                for h in range(2):
+                    nc.scalar.mul(cast[c, i][:].rearrange("p (u h q e) -> p h u q e", u=2, h=2, e=2)[:, h, :, :, :], t_o[c, i, h][:].rearrange("p (q u e) -> p u q e", u=2, e=2), 1.0 / 32.0)
+                return
+            dst = cast[c, i][:].rearrange("p (u q e) -> p u q e", u=2, e=2)
+            src = of[c, i][:].rearrange("p (q u e) -> p u q e", u=2, e=2)
+            if engine == "V":
+                nc.vector.tensor_copy(out=dst, in_=src)
+            else:
+                nc.gpsimd.tensor_scalar(out=dst, in0=src, scalar1=1.0, scalar2=0.0, op0=ALU.mult, op1=ALU.add)
+
+        def Pt(c):
+            for f in range(2):
+                bank = psum.tile([P, 2, CH], F32, name="bank_tr", tag="tr")
+                t_p[c, f] = bank
+                for i in range(2):
+                    words = cast[c, i][:].bitcast(F32)
+                    for u in range(2):
+                        w0 = 256 * u + P * f
+                        nc.tensor.transpose(bank[:, u, P * i : P * i + P], words[:, w0 : w0 + P], ident[:])
+
+        def Pc(c, engines="SS"):
+            if c % 2 == 0:
+                p_bf[c // 2] = keep.tile([P, 2, 2 * CH, 4], BF16, name="p_bf_%d" % (c // 2), align_bytes=64)
+                p_codes[c // 2] = keep.tile([P, 2, 2 * CH], U32, name="p_codes_%d" % (c // 2), align_bytes=64)
+            n0 = CH * (c % 2)
+            for f in range(2):
+                dst = p_bf[c // 2][:, f, n0 : n0 + CH, :].rearrange("p n t -> p (n t)").bitcast(F32).rearrange("p (q i u) -> p q i u", i=2, u=2)
+                src = t_p[c, f][:].rearrange("p u (i q) -> p q i u", i=2)
+                if engines[f] == "S":
+                    nc.scalar.copy(out=dst, in_=src)
+                else:
+                    nc.vector.tensor_copy(out=dst, in_=src)
+
+        def Pq(c):
+            if c == 0:
+                return
+            h = c // 2
+            width = 2 * CH if c == 1 else CH
+            n0 = 0 if c == 1 else CH * (c % 2)
+            for f in range(2):
+                nc.vector.quantize_mx(out=p_codes[h][:, f, n0 : n0 + width].bitcast(FP8X4), scales=out_scales[:, f, 512 * h + n0 : 512 * h + n0 + width], in_=p_bf[h][:, f, n0 : n0 + width, :].rearrange("p n t -> p (n t)"))
+                if c == 3:
+                    nc.sync.dma_start(out=out_1[f, :, 512 * h + n0 : 512 * h + n0 + width, :].rearrange("p n t -> p (n t)").bitcast(I32), in_=p_codes[h][:, f, n0 : n0 + width].bitcast(I32))
+            if c != 3:
+                nc.sync.dma_start(out=out_1[:, :, 512 * h + n0 : 512 * h + n0 + width, :].rearrange("f p n t -> p f (n t)").bitcast(I32), in_=p_codes[h][:, :, n0 : n0 + width].bitcast(I32))
+            if c == 3:
+                for Q in range(4):
+                    queue = nc.scalar if Q % 2 == 0 else nc.sync
+                    queue.dma_start(out=out_2[:, 4 * Q : 4 * Q + 4, :].rearrange("f q n -> q f n").bitcast(I32), in_=out_scales[32 * Q : 32 * Q + 4, :, :].bitcast(I32))
+
+        with tc.manual_schedule():
+            for name, src in (("r", r), ("g", g), ("bj", bj), ("v", v)):
+                nc.scalar.dma_start(out=vecs[name][:], in_=src.rearrange("(G p t) -> p G t", p=P, t=4))
+            make_identity(nc, ident[:])
+            y_raw[0, 0] = new_raw()
+            for f in range(2):
+                cols = slice(512 * f, 512 * f + 512)
+                nc.sync.dma_start(out=y_raw[0, 0][:, :, cols], in_=y[0:512, cols].rearrange("(p j) d -> p j d", j=4)[:, 0:2, :])
+            load_y(0, 1)
+            load_y(1, 0)
+            load_y(1, 1)
+            load_rows(z_raw, z, 0)
+            load_rows(z_raw, z, 1)
+            load_rows(a_raw, adj, 0)
+            load_rows(z_raw, z, 2)
+            load_rows(a_raw, adj, 1)
+            load_rows(z_raw, z, 3)
+            load_rows(a_raw, adj, 2)
+            load_rows(a_raw, adj, 3)
+            nc.scalar.copy(out=r_f32[:], in_=vecs["r"][:])
+            nc.scalar.activation(out=warm[:], in_=r_f32[:, 0, 0:1], func=ACT.Sigmoid)
+            bank = psum.tile([P, 512], F32, name="bank_o", tag="o")
+            for k in range(14):
+                nc.tensor.transpose(bank[:, P * (k % 4) : P * (k % 4) + P], ident[:], ident[:])
+
+            Y(0, 0); Ye(0, 0); Y(0, 1); YRs(0, (0, 1), "S"); YRs(0, (2, 3)); Ye(0, 1)
+            Y(1, 0); YRi(0, 0, 1); Ye(1, 0); YRi(0, 1, 0, "V"); Y(1, 1); Ye(1, 1)
+            YRs(1, (2, 3)); Z(0); A(0); Pq(0); YRi(0, 1, 1); YRs(1, (0, 1), "G")
+            Yq(0); YRi(0, 0, 0); S1(3, 1); Zc(0); Z(1); Zq(0)
+            YRi(1, 0, 1); YRq(0, 1); Zc(1); S1(0, 0); Yq(1); Pr(0, 0)
+            Z(2); YRi(1, 1, 1, "V"); S1(0, 1); Zc(2); YRq(0, 0); R(0, 0)
+            Pr(0, 1); Zq(1); Z(3); Zc(3); Mu(0, 0); Zq(2)
+            R(0, 1); S1(1, 1); Pr(1, 1); S1(1, 0); Pr(1, 0); Zq(3)
+            A(1); YRi(1, 0, 0); Mu(0, 1); Pr(2, 0); S1(2, 0); R(1, 0)
+            R(1, 1); YRq(1, 0); YRi(1, 1, 0); Rq(0); Mu(1, 0); A(2)
+            R(2, 0); S1(2, 1); YRq(1, 1); O(0, 0); S1(3, 0); Oe(0, 0)
+            O(0, 1); Mu(2, 0); Mu(1, 1); Pr(3, 1); Oe(0, 1); R(2, 1)
+            C(0, 1, "S"); Rq(1); A(3); O(1, 0); Oe(1, 0); O(1, 1)
+            Oe(1, 1); Mu(2, 1); Pr(2, 1); C(0, 0, "G"); R(3, 0); Rq(2)
+            O(2, 0); Pt(0); Oe(2, 0); O(2, 1); C(1, 0, "G"); R(3, 1)
+            Pc(0); Mu(3, 0); Mu(3, 1); C(1, 1); Pt(1); Oe(2, 1)
+            Pc(1); Rq(3); C(2, 0); O(3, 0); Oe(3, 0, "VS"); C(2, 1, "G")
+            Pq(1); O(3, 1); Pt(2); C(3, 0); Oe(3, 1); C(3, 1)
+            Pc(2); Pt(3); Pc(3); Pq(2); Pq(3); Pr(3, 0)

@@ -18,313 +18,256 @@ ALU = mybir.AluOpType
 P = 128
 CH = 256
 NCH = N // CH
-WIDE = (False, True)
+RING = 5
+ADJ_BANKS = 3
 
 
 def tile_innerproductsigmoidresidualprojection_kernel(tc, z, y, adj, g, bj, v, r, out_0, out_1, out_2):
     nc = tc.nc
     with ExitStack() as ctx:
-        keep = ctx.enter_context(tc.tile_pool(name="keep", bufs=1))
-        work = ctx.enter_context(tc.tile_pool(name="work", bufs=2))
-        psum = ctx.enter_context(tc.psum_pool(name="psum", bufs=2))
+        sb = ctx.enter_context(tc.tile_pool(name="sb", bufs=1))
+        psum = ctx.enter_context(tc.psum_pool(name="psum", bufs=1))
 
-        y_raw = {}
-        z_raw = {}
-        a_raw = {}
-        vecs = {}
-        for name in ("r", "g", "bj", "v"):
-            vecs[name] = keep.tile([P, 2, 4], BF16, name="vec_" + name)
-        y_scaled = {}
-        yr_bf = {}
-        yr_codes = {}
-        yr_scales = {}
-        yg_bf = {}
-        yg_codes = {}
-        yg_scales = {}
-        for G in range(2):
-            y_scaled[G] = keep.tile([P, 4, D], BF16, name="y_scaled_%d" % G, align_bytes=64)
-            yr_bf[G] = keep.tile([P, D, 4], BF16, name="yr_bf_%d" % G, align_bytes=64)
-            yr_codes[G] = keep.tile([P, D], U32, name="yr_codes_%d" % G, align_bytes=64)
-            yr_scales[G] = keep.tile([P, D], U8, name="yr_scales_%d" % G, align_bytes=64)
-            yg_codes[G] = keep.tile([P, M], U32, name="yg_codes_%d" % G, align_bytes=64)
-            yg_scales[G] = keep.tile([P, M], U8, name="yg_scales_%d" % G, align_bytes=64)
-        out_scales = keep.tile([P, 2, N], U8, name="out_scales", align_bytes=64)
-        ident = keep.tile([P, P], F32, name="ident")
-        r_f32 = keep.tile([P, 2, 4], F32, name="r_f32")
-        warm = keep.tile([P, 1], F32, name="warm")
+        def tile(shape, dtype, tag):
+            return sb.tile(shape, dtype, name=tag, tag=tag, align_bytes=64)
 
-        def new_raw():
-            return work.tile([P, 2, D], BF16, name="raw", align_bytes=64, bufs=10)
+        taken = []
 
-        def load_y(G, jp):
-            y_raw[G, jp] = new_raw()
-            src = y[512 * G : 512 * G + 512, :].rearrange("(p j) d -> p j d", j=4)
-            nc.sync.dma_start(out=y_raw[G, jp][:], in_=src[:, 2 * jp : 2 * jp + 2, :])
+        def ring_bank():
+            tag = "ring_%d" % (len(taken) % RING)
+            taken.append(tag)
+            return psum.tile([P, 512], F32, name=tag, tag=tag)
 
-        def load_rows(dst, src, c):
-            dst[c] = new_raw()
+        side = []
+
+        def side_bank():
+            tag = "side_%d" % (len(side) % ADJ_BANKS)
+            side.append(tag)
+            return psum.tile([P, 512], F32, name=tag, tag=tag)
+
+        vecs = {name: tile([P, 2, 4], BF16, "vec_" + name) for name in ("r", "g", "bj", "v")}
+        y_scaled = [tile([P, 4, D], BF16, "y_scaled_%d" % G) for G in range(2)]
+        yr_bf = [tile([P, D, 4], BF16, "yr_bf_%d" % G) for G in range(2)]
+        yr_codes = [tile([P, D], U32, "yr_codes_%d" % G) for G in range(2)]
+        yr_scales = [tile([P, D], U8, "yr_scales_%d" % G) for G in range(2)]
+        yg_codes = [tile([P, M], U32, "yg_codes_%d" % f) for f in range(2)]
+        yg_scales = [tile([P, M], U8, "yg_scales_%d" % f) for f in range(2)]
+        out_scales = tile([P, 2, N], U8, "out_scales")
+        ident = tile([P, P], F32, "ident")
+        r_f32 = tile([P, 2, 4], F32, "r_f32")
+        warm = tile([P, 1], F32, "warm")
+
+        y_raw, y_rows, z_raw, a_raw = {}, {}, {}, {}
+        t_y, t_z, t_a, t_o, t_p = {}, {}, {}, {}, {}
+        yg_bf, z_bf, z_codes, z_scales, pr = {}, {}, {}, {}, {}
+        res_bf, res_codes, res_scales, of, cast, p_bf, p_codes = {}, {}, {}, {}, {}, {}, {}
+
+        def load_y(G, jp, halves=1):
+            src = y[512 * G : 512 * G + 512, :].rearrange("(p j) d -> p j d", j=4)[:, 2 * jp : 2 * jp + 2, :]
+            if halves == 1:
+                whole = tile([P, 2, D], BF16, "raw_y%d" % (2 * G + jp))
+                nc.sync.dma_start(out=whole[:], in_=src)
+                for f in range(2):
+                    y_raw[G, jp, f] = whole[:, :, 512 * f : 512 * f + 512]
+                y_rows[G, jp] = [(whole[:], slice(0, D))]
+                return
+            for f in range(2):
+                half = tile([P, 2, 512], BF16, "raw_half%d" % f)
+                nc.sync.dma_start(out=half[:], in_=src[:, :, 512 * f : 512 * f + 512])
+                y_raw[G, jp, f] = half[:]
+            y_rows[G, jp] = [(y_raw[G, jp, f], slice(512 * f, 512 * f + 512)) for f in range(2)]
+
+        def load_rows(dst, src, c, name):
+            dst[c] = tile([P, 2, D], BF16, "raw_%s%d" % (name, c))
             nc.sync.dma_start(out=dst[c][:], in_=src[CH * c : CH * c + CH, :].rearrange("(p i) k -> p i k", i=2))
 
-        t_y = {}
-        t_z = {}
-        t_a = {}
-        t_s = {}
-        t_o = {}
-        t_p = {}
-        z_bf = {}
-        z_codes = {}
-        z_scales = {}
-        pr = {}
-        dd = {}
-        res_bf = {}
-        res_codes = {}
-        res_scales = {}
-        of = {}
-        cast = {}
-        p_bf = {}
-        p_codes = {}
+        def turn(bank, rows):
+            for i in range(2):
+                words = rows[:, i, :].bitcast(F32)
+                for u in range(2):
+                    nc.tensor.transpose(bank[:, CH * u + P * i : CH * u + P * i + P], words[:, u:256:2], ident[:])
 
-        def Y(G, jp):
-            for f in range(2):
-                bank = psum.tile([P, 2, CH], F32, name="bank_tr", tag="tr")
-                t_y[G, jp, f] = bank
-                for k in range(2):
-                    words = y_raw[G, jp][:, k, :].bitcast(F32)
-                    for u in range(2):
-                        nc.tensor.transpose(bank[:, u, P * k : P * k + P], words[:, 256 * f + u : 256 * f + 256 : 2], ident[:])
+        def Y(G, jp, f):
+            t_y[G, jp, f] = ring_bank()
+            turn(t_y[G, jp, f], y_raw[G, jp, f])
 
-        def Ye(G, jp):
-            for f in range(2):
-                if jp == 0:
-                    yg_bf[G, f] = work.tile([P, 512, 4], BF16, name="yg_bf", tag="f4k", align_bytes=64, bufs=4)
-                src = t_y[G, jp, f][:].rearrange("p u m -> p (u m)").bitcast(BF16).rearrange("p (u m e) -> p m u e", u=2, e=2)
-                dst = yg_bf[G, f][:, CH * jp : CH * jp + CH, :].rearrange("p m (u e) -> p m u e", u=2)
-                fac = vecs["g"][:, f, :].unsqueeze(1).to_broadcast([P, CH, 4]).rearrange("p m (u e) -> p m u e", u=2)
-                nc.vector.tensor_tensor(out=dst, in0=src, in1=fac, op=ALU.mult)
+        def Ye(G, jp, f):
+            if jp == 0:
+                yg_bf[G, f] = tile([P, 512, 4], BF16, "yg_bf_%d" % (2 * G + f))
+            src = t_y[G, jp, f][:].bitcast(BF16).rearrange("p (u m e) -> p m u e", u=2, e=2)
+            dst = yg_bf[G, f][:, CH * jp : CH * jp + CH, :].rearrange("p m (u e) -> p m u e", u=2)
+            fac = vecs["g"][:, f, :].unsqueeze(1).to_broadcast([P, CH, 4]).rearrange("p m (u e) -> p m u e", u=2)
+            nc.vector.tensor_tensor(out=dst, in0=src, in1=fac, op=ALU.mult)
 
-        def Yq(G):
+        def Yq(G, f):
             cols = slice(512 * G, 512 * G + 512)
-            for f in range(2):
-                nc.vector.quantize_mx(out=yg_codes[f][:, cols].bitcast(FP8X4), scales=yg_scales[f][:, cols], in_=yg_bf[G, f][:].rearrange("p m t -> p (m t)"))
+            nc.vector.quantize_mx(out=yg_codes[f][:, cols].bitcast(FP8X4), scales=yg_scales[f][:, cols], in_=yg_bf[G, f][:].rearrange("p m t -> p (m t)"))
 
-        def rows_to_banks(raw, store, c, tag):
-            for f in range(2):
-                bank = psum.tile([P, 2, CH], F32, name="bank_" + tag, tag=tag)
-                store[c, f] = bank
-                for i in range(2):
-                    words = raw[c][:, i, :].bitcast(F32)
-                    for u in range(2):
-                        nc.tensor.transpose(bank[:, u, P * i : P * i + P], words[:, 256 * f + u : 256 * f + 256 : 2], ident[:])
+        def Z(c, f):
+            t_z[c, f] = ring_bank()
+            turn(t_z[c, f], z_raw[c][:, :, 512 * f : 512 * f + 512])
 
-        def Z(c):
-            rows_to_banks(z_raw, t_z, c, "tr")
+        def A(c, G):
+            t_a[c, G] = side_bank()
+            turn(t_a[c, G], a_raw[c][:, :, 512 * G : 512 * G + 512])
 
-        def A(c):
-            rows_to_banks(a_raw, t_a, c, "a")
+        def Zc(c, f):
+            H, k = divmod(c, 2)
+            if (H, f) not in z_bf:
+                z_bf[H, f] = tile([P, 512, 4], BF16, "turned_%d" % (2 * H + f))
+            dst = z_bf[H, f][:, CH * k : CH * k + CH, :].rearrange("p n t -> p (n t)").bitcast(F32).rearrange("p (n u) -> p n u", u=2)
+            nc.scalar.copy(out=dst, in_=t_z[c, f][:].rearrange("p (u n) -> p n u", u=2))
 
-        def z_slot(c, f):
-            h, k = divmod(c, 2)
-            return 2 * f + k if WIDE[h] else 2 * k + f
+        def Zq(H, f):
+            z_codes[H, f] = tile([P, 512], U32, "z_codes_%d" % (2 * H + f))
+            z_scales[H, f] = tile([P, 512], U8, "z_scales_%d" % (2 * H + f))
+            nc.vector.quantize_mx(out=z_codes[H, f][:].bitcast(FP8X4), scales=z_scales[H, f][:], in_=z_bf[H, f][:].rearrange("p n t -> p (n t)"))
 
-        def Zc(c):
-            h, k = divmod(c, 2)
-            if k == 0:
-                z_bf[h] = work.tile([P, 4, CH, 4], BF16, name="z_bf", align_bytes=64, bufs=2)
-            for f in range(2):
-                nc.scalar.copy(out=z_bf[h][:, z_slot(c, f), :, :].rearrange("p n t -> p (n t)").bitcast(F32).rearrange("p (n u) -> p n u", u=2), in_=t_z[c, f][:].rearrange("p u n -> p n u"))
-
-        def Zq(c):
-            h, k = divmod(c, 2)
-            if k == 0:
-                z_codes[h] = work.tile([P, 4 * CH], U32, name="z_codes", align_bytes=64, bufs=2)
-                z_scales[h] = work.tile([P, 4 * CH], U8, name="z_scales", align_bytes=64, bufs=2)
-            cols = slice(2 * CH * k, 2 * CH * k + 2 * CH)
-            nc.vector.quantize_mx(out=z_codes[h][:, cols].bitcast(FP8X4), scales=z_scales[h][:, cols], in_=z_bf[h][:, 2 * k : 2 * k + 2, :, :].rearrange("p s n t -> p (s n t)"))
-
-        def YRs(G, slots, engine="V"):
-            for j in slots:
-                dst = y_scaled[G][:, j, :]
-                src = y_raw[G, j // 2][:, j % 2, :]
+        def YRs(G, j, engine="V"):
+            for src, cols in y_rows[G, j // 2]:
+                dst = y_scaled[G][:, j, cols]
                 if engine == "V":
-                    nc.vector.tensor_scalar_mul(dst, src, vecs["r"][:, G, j : j + 1])
+                    nc.vector.tensor_scalar_mul(dst, src[:, j % 2, :], vecs["r"][:, G, j : j + 1])
                 elif engine == "S":
-                    nc.scalar.activation(out=dst, in_=src, func=ACT.Copy, scale=r_f32[:, G, j : j + 1])
+                    nc.scalar.activation(out=dst, in_=src[:, j % 2, :], func=ACT.Copy, scale=r_f32[:, G, j : j + 1])
                 else:
-                    nc.gpsimd.tensor_scalar(out=dst, in0=src, scalar1=r_f32[:, G, j : j + 1], scalar2=0.0, op0=ALU.mult, op1=ALU.add)
+                    nc.gpsimd.tensor_scalar(out=dst, in0=src[:, j % 2, :], scalar1=r_f32[:, G, j : j + 1], scalar2=0.0, op0=ALU.mult, op1=ALU.add)
 
-        def YRi(G, h, k, engine="S"):
-                cols = slice(512 * h + 256 * k, 512 * h + 256 * k + 256)
-                copy = nc.scalar.copy if engine == "S" else nc.vector.tensor_copy
-                copy(out=yr_bf[G][:, cols, :].rearrange("p (c i) t -> p c t i", i=4), in_=y_scaled[G][:, :, cols].rearrange("p t (c i) -> p c t i", i=4))
+        def YRi(G, q, engine="S"):
+            cols = slice(CH * q, CH * q + CH)
+            copy = nc.scalar.copy if engine == "S" else nc.vector.tensor_copy
+            copy(out=yr_bf[G][:, cols, :].rearrange("p (c i) t -> p c t i", i=4), in_=y_scaled[G][:, :, cols].rearrange("p t (c i) -> p c t i", i=4))
 
         def YRq(G, h):
             cols = slice(512 * h, 512 * h + 512)
             nc.vector.quantize_mx(out=yr_codes[G][:, cols].bitcast(FP8X4), scales=yr_scales[G][:, cols], in_=yr_bf[G][:, cols, :].rearrange("p d t -> p (d t)"))
 
-        def S1(c, G):
-            h = c // 2
-            if WIDE[h]:
-                if c % 2 == 1:
-                    return
-                pr[h, G] = work.tile([P, 4, 2 * CH], F32, name="pr_wide", bufs=2)
-                for t in range(4):
-                    bank = psum.tile([P, 2 * CH], F32, name="bank_s", tag="s")
-                    m0 = 512 * G + P * t
-                    for f in range(2):
-                        nc.tensor.matmul_mx(out=bank[:], lhsT=yg_codes[f][:, m0 : m0 + P].bitcast(FP8X4), lhsT_scale=yg_scales[f][:, m0 : m0 + P], rhs=z_codes[h][:, 512 * f : 512 * f + 512].bitcast(FP8X4), rhs_scale=z_scales[h][:, 512 * f : 512 * f + 512], start=(f == 0), stop=(f == 1))
-                    nc.scalar.activation(out=pr[h, G][:, t, :], in_=bank[:], func=ACT.Sigmoid, bias=vecs["bj"][:, G, t : t + 1], scale=1.0 / 32.0)
-                return
-            for tp in range(2):
-                bank = psum.tile([P, 2, CH], F32, name="bank_s", tag="s")
-                t_s[c, G, tp] = bank
-                for k in range(2):
-                    m0 = 512 * G + P * (2 * tp + k)
-                    for f in range(2):
-                        nc.tensor.matmul_mx(out=bank[:, k, :], lhsT=yg_codes[f][:, m0 : m0 + P].bitcast(FP8X4), lhsT_scale=yg_scales[f][:, m0 : m0 + P], rhs=z_codes[h][:, CH * z_slot(c, f) : CH * z_slot(c, f) + CH].bitcast(FP8X4), rhs_scale=z_scales[h][:, CH * z_slot(c, f) : CH * z_slot(c, f) + CH], start=(f == 0), stop=(f == 1))
+        def S1(H, G, t):
+            if t == 0:
+                pr[H, G] = tile([P, 4, 512], F32, "pr_%d" % (2 * H + G))
+            bank = ring_bank()
+            m0 = 512 * G + P * t
+            for f in range(2):
+                nc.tensor.matmul_mx(out=bank[:], lhsT=yg_codes[f][:, m0 : m0 + P].bitcast(FP8X4), lhsT_scale=yg_scales[f][:, m0 : m0 + P], rhs=z_codes[H, f][:].bitcast(FP8X4), rhs_scale=z_scales[H, f][:], start=(f == 0), stop=(f == 1))
+            nc.scalar.activation(out=pr[H, G][:, t, :], in_=bank[:], func=ACT.Sigmoid, bias=vecs["bj"][:, G, t : t + 1], scale=1.0 / 32.0)
 
-        def Pr(c, G):
-            if WIDE[c // 2]:
-                return
-            pr[c, G, "n"] = work.tile([P, 4, CH], F32, name="pr", bufs=4)
-            for t in range(4):
-                nc.scalar.activation(out=pr[c, G, "n"][:, t, :], in_=t_s[c, G, t // 2][:, t % 2, :], func=ACT.Sigmoid, bias=vecs["bj"][:, G, t : t + 1], scale=1.0 / 32.0)
+        def probs(c, G):
+            return pr[c // 2, G][:, :, CH * (c % 2) : CH * (c % 2) + CH]
 
         def R(c, G):
-            prob = pr[c // 2, G][:, :, CH * (c % 2) : CH * (c % 2) + CH] if WIDE[c // 2] else pr[c, G, "n"][:]
-            dd[c, G] = work.tile([P, 4, CH], F32, name="dd", bufs=3)
-            nc.vector.tensor_tensor(
-                out=dd[c, G][:].rearrange("p (u e) n -> p u e n", u=2),
-                in0=prob.rearrange("p (u e) n -> p u e n", u=2),
-                in1=t_a[c, G][:].rearrange("p u n -> p (u n)").bitcast(BF16).rearrange("p (u n e) -> p u e n", u=2, e=2),
-                op=ALU.subtract,
-            )
+            view = probs(c, G).rearrange("p (u e) n -> p u e n", u=2)
+            nc.vector.tensor_tensor(out=view, in0=view, in1=t_a[c, G][:].bitcast(BF16).rearrange("p (u n e) -> p u e n", u=2, e=2), op=ALU.subtract)
 
         def Mu(c, G):
-            if c not in res_bf:
-                res_bf[c] = work.tile([P, 2, CH, 4], BF16, name="res_bf", align_bytes=64, bufs=2)
+            if G == 0:
+                res_bf[c] = tile([P, 2, CH, 4], BF16, "res_bf_%d" % (c % 2))
             nc.vector.tensor_tensor(
                 out=res_bf[c][:, G, :, :].rearrange("p (c i) t -> p c t i", i=4),
-                in0=dd[c, G][:].rearrange("p t (c i) -> p c t i", i=4),
+                in0=probs(c, G).rearrange("p t (c i) -> p c t i", i=4),
                 in1=vecs["v"][:, G, :].unsqueeze(1).unsqueeze(3).to_broadcast([P, CH // 4, 4, 4]),
                 op=ALU.mult,
             )
 
         def Rq(c):
-            res_codes[c] = work.tile([P, 2 * CH], U32, name="res_codes", align_bytes=64, bufs=4)
-            res_scales[c] = work.tile([P, 2 * CH], U8, name="res_scales", align_bytes=64, bufs=4)
+            res_codes[c] = tile([P, 2 * CH], U32, "res_codes_%d" % c)
+            res_scales[c] = tile([P, 2 * CH], U8, "res_scales_%d" % c)
             nc.vector.quantize_mx(out=res_codes[c][:].bitcast(FP8X4), scales=res_scales[c][:], in_=res_bf[c][:].rearrange("p f n t -> p (f n t)"))
 
-        def O(c, i):
-            for h in range(2):
-                bank = psum.tile([P, 512], F32, name="bank_o", tag="o")
-                t_o[c, i, h] = bank
-                for G in range(2):
-                    nc.tensor.matmul_mx(out=bank[:], lhsT=res_codes[c][:, CH * G + P * i : CH * G + P * i + P].bitcast(FP8X4), lhsT_scale=res_scales[c][:, CH * G + P * i : CH * G + P * i + P], rhs=yr_codes[G][:, 512 * h : 512 * h + 512].bitcast(FP8X4), rhs_scale=yr_scales[G][:, 512 * h : 512 * h + 512], start=(G == 0), stop=(G == 1))
+        def O(c, i, h):
+            bank = ring_bank()
+            t_o[c, i, h] = bank
+            for G in range(2):
+                cols = slice(CH * G + P * i, CH * G + P * i + P)
+                nc.tensor.matmul_mx(out=bank[:], lhsT=res_codes[c][:, cols].bitcast(FP8X4), lhsT_scale=res_scales[c][:, cols], rhs=yr_codes[G][:, 512 * h : 512 * h + 512].bitcast(FP8X4), rhs_scale=yr_scales[G][:, 512 * h : 512 * h + 512], start=(G == 0), stop=(G == 1))
 
-        def Oe(c, i, engines="SS"):
-            of[c, i] = work.tile([P, D], F32, name="of", tag="f4k", align_bytes=64, bufs=4)
-            for h in range(2):
-                dst = of[c, i][:, 512 * h : 512 * h + 512]
-                if engines[h] == "S":
-                    nc.scalar.mul(dst, t_o[c, i, h][:], 1.0 / 32.0)
-                else:
-                    nc.vector.tensor_scalar_mul(dst, t_o[c, i, h][:], 1.0 / 32.0)
-            nc.sync.dma_start(out=out_0[CH * c : CH * c + CH, :].rearrange("(p i) d -> p i d", i=2)[:, i, :], in_=of[c, i][:])
-
-        def C(c, i, engine="V"):
-            cast[c, i] = work.tile([P, D], BF16, name="cast", align_bytes=64, bufs=4)
+        def Oe(c, i, h, engine="S"):
+            if h == 0:
+                of[c, i] = tile([P, D], F32, ("raw_z%d" % c) if i == 0 else ("yg_bf_%d" % c))
+            dst = of[c, i][:, 512 * h : 512 * h + 512]
             if engine == "S":
-                for h in range(2):
-                    nc.scalar.mul(cast[c, i][:].rearrange("p (u h q e) -> p h u q e", u=2, h=2, e=2)[:, h, :, :, :], t_o[c, i, h][:].rearrange("p (q u e) -> p u q e", u=2, e=2), 1.0 / 32.0)
+                nc.scalar.mul(dst, t_o[c, i, h][:], 1.0 / 32.0)
+            else:
+                nc.vector.tensor_scalar_mul(dst, t_o[c, i, h][:], 1.0 / 32.0)
+            if h == 1:
+                nc.sync.dma_start(out=out_0[CH * c : CH * c + CH, :].rearrange("(p i) d -> p i d", i=2)[:, i, :], in_=of[c, i][:])
+
+        def C(c, i, h, engine="V"):
+            cast[c, i, h] = tile([P, 512], BF16, "cast_%d" % (4 * c + 2 * i + h))
+            dst = cast[c, i, h][:].rearrange("p (u q e) -> p u q e", u=2, e=2)
+            if engine in ("PS", "PV"):
+                src = t_o[c, i, h][:].rearrange("p (q u e) -> p u q e", u=2, e=2)
+                if engine == "PS":
+                    nc.scalar.mul(dst, src, 1.0 / 32.0)
+                else:
+                    nc.vector.tensor_scalar_mul(dst, src, 1.0 / 32.0)
                 return
-            dst = cast[c, i][:].rearrange("p (u q e) -> p u q e", u=2, e=2)
-            src = of[c, i][:].rearrange("p (q u e) -> p u q e", u=2, e=2)
+            src = of[c, i][:, 512 * h : 512 * h + 512].rearrange("p (q u e) -> p u q e", u=2, e=2)
             if engine == "V":
                 nc.vector.tensor_copy(out=dst, in_=src)
             else:
                 nc.gpsimd.tensor_scalar(out=dst, in0=src, scalar1=1.0, scalar2=0.0, op0=ALU.mult, op1=ALU.add)
 
-        def Pt(c):
-            for f in range(2):
-                bank = psum.tile([P, 2, CH], F32, name="bank_tr", tag="tr")
-                t_p[c, f] = bank
-                for i in range(2):
-                    words = cast[c, i][:].bitcast(F32)
-                    for u in range(2):
-                        w0 = 256 * u + P * f
-                        nc.tensor.transpose(bank[:, u, P * i : P * i + P], words[:, w0 : w0 + P], ident[:])
+        def Pt(c, f):
+            bank = side_bank()
+            t_p[c, f] = bank
+            for i in range(2):
+                words = cast[c, i, f][:].bitcast(F32)
+                for u in range(2):
+                    nc.tensor.transpose(bank[:, CH * u + P * i : CH * u + P * i + P], words[:, P * u : P * u + P], ident[:])
 
-        def Pc(c, engines="SS"):
-            if c % 2 == 0:
-                p_bf[c // 2] = keep.tile([P, 2, 2 * CH, 4], BF16, name="p_bf_%d" % (c // 2), align_bytes=64)
-                p_codes[c // 2] = keep.tile([P, 2, 2 * CH], U32, name="p_codes_%d" % (c // 2), align_bytes=64)
-            n0 = CH * (c % 2)
-            for f in range(2):
-                dst = p_bf[c // 2][:, f, n0 : n0 + CH, :].rearrange("p n t -> p (n t)").bitcast(F32).rearrange("p (q i u) -> p q i u", i=2, u=2)
-                src = t_p[c, f][:].rearrange("p u (i q) -> p q i u", i=2)
-                if engines[f] == "S":
-                    nc.scalar.copy(out=dst, in_=src)
-                else:
-                    nc.vector.tensor_copy(out=dst, in_=src)
-
-        def Pq(c):
+        def Pc(c, f, engine="S"):
             if c == 0:
-                return
-            h = c // 2
-            width = 2 * CH if c == 1 else CH
-            n0 = 0 if c == 1 else CH * (c % 2)
-            for f in range(2):
-                nc.vector.quantize_mx(out=p_codes[h][:, f, n0 : n0 + width].bitcast(FP8X4), scales=out_scales[:, f, 512 * h + n0 : 512 * h + n0 + width], in_=p_bf[h][:, f, n0 : n0 + width, :].rearrange("p n t -> p (n t)"))
-                if c == 3:
-                    nc.sync.dma_start(out=out_1[f, :, 512 * h + n0 : 512 * h + n0 + width, :].rearrange("p n t -> p (n t)").bitcast(I32), in_=p_codes[h][:, f, n0 : n0 + width].bitcast(I32))
-            if c != 3:
-                nc.sync.dma_start(out=out_1[:, :, 512 * h + n0 : 512 * h + n0 + width, :].rearrange("f p n t -> p f (n t)").bitcast(I32), in_=p_codes[h][:, :, n0 : n0 + width].bitcast(I32))
-            if c == 3:
-                for Q in range(4):
-                    queue = nc.scalar if Q % 2 == 0 else nc.sync
-                    queue.dma_start(out=out_2[:, 4 * Q : 4 * Q + 4, :].rearrange("f q n -> q f n").bitcast(I32), in_=out_scales[32 * Q : 32 * Q + 4, :, :].bitcast(I32))
+                p_bf[0, f] = tile([P, 2 * CH, 4], BF16, "turned_%d" % f)
+            elif c > 1:
+                p_bf[c, f] = tile([P, CH, 4], BF16, "p_bf_%d" % (2 * c + f))
+            rows = p_bf[0, f][:, CH * c : CH * c + CH, :] if c < 2 else p_bf[c, f][:]
+            dst = rows.rearrange("p n t -> p (n t)").bitcast(F32).rearrange("p (q i u) -> p q i u", i=2, u=2)
+            src = t_p[c, f][:].rearrange("p (u i q) -> p q i u", u=2, i=2)
+            if engine == "S":
+                nc.scalar.copy(out=dst, in_=src)
+            else:
+                nc.vector.tensor_copy(out=dst, in_=src)
+
+        def Pq(c, f):
+            n0, width = CH * c, 2 * CH if c == 0 else CH
+            p_codes[c, f] = tile([P, width], U32, "p_codes_%d" % (2 * c + f))
+            nc.vector.quantize_mx(out=p_codes[c, f][:].bitcast(FP8X4), scales=out_scales[:, f, n0 : n0 + width], in_=p_bf[c, f][:].rearrange("p n t -> p (n t)"))
+            nc.sync.dma_start(out=out_1[f, :, n0 : n0 + width, :].rearrange("p n t -> p (n t)").bitcast(I32), in_=p_codes[c, f][:].bitcast(I32))
+
+        def store_scales():
+            for Q in range(4):
+                queue = nc.scalar if Q % 2 == 0 else nc.sync
+                queue.dma_start(out=out_2[:, 4 * Q : 4 * Q + 4, :].rearrange("f q n -> q f n").bitcast(I32), in_=out_scales[32 * Q : 32 * Q + 4, :, :].bitcast(I32))
 
         with tc.manual_schedule():
             for name, src in (("r", r), ("g", g), ("bj", bj), ("v", v)):
                 nc.scalar.dma_start(out=vecs[name][:], in_=src.rearrange("(G p t) -> p G t", p=P, t=4))
             make_identity(nc, ident[:])
-            y_raw[0, 0] = new_raw()
-            for f in range(2):
-                cols = slice(512 * f, 512 * f + 512)
-                nc.sync.dma_start(out=y_raw[0, 0][:, :, cols], in_=y[0:512, cols].rearrange("(p j) d -> p j d", j=4)[:, 0:2, :])
+            nc.scalar.activation(out=warm[:], in_=ident[:, 0:1], func=ACT.Sigmoid)
+            load_y(0, 0, halves=2)
             load_y(0, 1)
+            load_rows(z_raw, z, 0, "z")
+            load_rows(z_raw, z, 1, "z")
             load_y(1, 0)
             load_y(1, 1)
-            load_rows(z_raw, z, 0)
-            load_rows(z_raw, z, 1)
-            load_rows(a_raw, adj, 0)
-            load_rows(z_raw, z, 2)
-            load_rows(a_raw, adj, 1)
-            load_rows(z_raw, z, 3)
-            load_rows(a_raw, adj, 2)
-            load_rows(a_raw, adj, 3)
+            load_rows(a_raw, adj, 0, "a")
+            load_rows(a_raw, adj, 1, "a")
+            load_rows(z_raw, z, 2, "z")
+            load_rows(z_raw, z, 3, "z")
+            for c in range(2, NCH):
+                load_rows(a_raw, adj, c, "a")
             nc.scalar.copy(out=r_f32[:], in_=vecs["r"][:])
-            nc.scalar.activation(out=warm[:], in_=r_f32[:, 0, 0:1], func=ACT.Sigmoid)
-            bank = psum.tile([P, 512], F32, name="bank_o", tag="o")
-            for k in range(14):
-                nc.tensor.transpose(bank[:, P * (k % 4) : P * (k % 4) + P], ident[:], ident[:])
-
-            Y(0, 0); Ye(0, 0); Y(0, 1); YRs(0, (0, 1), "S"); YRs(0, (2, 3)); Ye(0, 1)
-            Y(1, 0); YRi(0, 0, 1); Ye(1, 0); YRi(0, 1, 0, "V"); Y(1, 1); Ye(1, 1)
-            YRs(1, (2, 3)); Z(0); A(0); Pq(0); YRi(0, 1, 1); YRs(1, (0, 1), "G")
-            Yq(0); YRi(0, 0, 0); S1(3, 1); Zc(0); Z(1); Zq(0)
-            YRi(1, 0, 1); YRq(0, 1); Zc(1); S1(0, 0); Yq(1); Pr(0, 0)
-            Z(2); YRi(1, 1, 1, "V"); S1(0, 1); Zc(2); YRq(0, 0); R(0, 0)
-            Pr(0, 1); Zq(1); Z(3); Zc(3); Mu(0, 0); Zq(2)
-            R(0, 1); S1(1, 1); Pr(1, 1); S1(1, 0); Pr(1, 0); Zq(3)
-            A(1); YRi(1, 0, 0); Mu(0, 1); Pr(2, 0); S1(2, 0); R(1, 0)
-            R(1, 1); YRq(1, 0); YRi(1, 1, 0); Rq(0); Mu(1, 0); A(2)
-            R(2, 0); S1(2, 1); YRq(1, 1); O(0, 0); S1(3, 0); Oe(0, 0)
-            O(0, 1); Mu(2, 0); Mu(1, 1); Pr(3, 1); Oe(0, 1); R(2, 1)
-            C(0, 1, "S"); Rq(1); A(3); O(1, 0); Oe(1, 0); O(1, 1)
-            Oe(1, 1); Mu(2, 1); Pr(2, 1); C(0, 0, "G"); R(3, 0); Rq(2)
-            O(2, 0); Pt(0); Oe(2, 0); O(2, 1); C(1, 0, "G"); R(3, 1)
-            Pc(0); Mu(3, 0); Mu(3, 1); C(1, 1); Pt(1); Oe(2, 1)
-            Pc(1); Rq(3); C(2, 0); O(3, 0); Oe(3, 0, "VS"); C(2, 1, "G")
-            Pq(1); O(3, 1); Pt(2); C(3, 0); Oe(3, 1); C(3, 1)
-            Pc(2); Pt(3); Pc(3); Pq(2); Pq(3); Pr(3, 0)
+            Y(0,0,0); Ye(0,0,0); Y(0,0,1); Ye(0,0,1); YRs(0,0,"S"); YRs(0,1,"S")
+            Y(0,1,0); Y(0,1,1); YRs(0,2); YRs(0,3); Ye(0,1,0); Ye(0,1,1); YRi(0,0)
+            Z(0,0); Zc(0,0); Z(0,1); Zc(0,1); Yq(0,0); Yq(0,1); Z(1,0); Zc(1,0); Z(1,1); Zc(1,1)
+            Y(1,0,0); YRs(1,0); YRs(1,1); Zq(0,0); Ye(1,0,0); Y(1,0,1); Zq(0,1); Ye(1,0,1); YRi(0,1); YRi(0,2)
+            Y(1,1,0); Ye(1,1,0); Y(1,1,1); Ye(1,1,1)
+            S1(0,0,0); S1(0,0,1); S1(0,0,2); S1(0,0,3); Yq(1,0); Yq(1,1); YRs(1,2); YRs(1,3); YRq(0,0)
+            A(0,0); A(1,0); YRi(0,3); Z(2,0); Zc(2,0); Z(2,1); Zc(2,1); Z(3,0); Zc(3,0); Z(3,1); Zc(3,1); R(0,0); R(1,0); Mu(0,0); YRq(0,1); Mu(1,0)
+            YRi(1,0); S1(0,1,0); S1(0,1,1); S1(0,1,2); S1(0,1,3); A(0,1); A(1,1); Zq(1,0); Zq(1,1); YRi(1,1,"V"); R(0,1); R(1,1); YRq(1,0); Mu(0,1); Mu(1,1)
+            YRi(1,2); S1(1,0,0); S1(1,0,1); S1(1,0,2); S1(1,0,3); A(2,0); YRi(1,3); S1(1,1,0); S1(1,1,1); S1(1,1,2); S1(1,1,3); A(2,1); Rq(0); R(2,0); YRq(1,1); Rq(1); Mu(2,0); A(3,0)
+            O(0,0,0); C(0,0,0,"PS"); Oe(0,0,0); O(0,0,1); C(0,0,1,"PS"); Oe(0,0,1); R(2,1); A(3,1); O(0,1,0); C(0,1,0,"PS"); Oe(0,1,0); O(0,1,1); C(0,1,1,"PS"); Oe(0,1,1); R(3,0); Mu(2,1); R(3,1); Rq(2); O(1,0,0); C(1,0,0,"PS"); Oe(1,0,0); O(1,0,1); Oe(1,0,1,"S"); O(1,1,0); C(1,1,0,"PS"); Oe(1,1,0); O(1,1,1); Oe(1,1,1,"S")
+            Pt(0,0); Pt(0,1); Mu(3,0); Mu(3,1); C(1,0,1); Rq(3); C(1,1,1); Pt(1,0); Pc(0,0); O(2,0,0); Oe(2,0,0,"S"); O(2,0,1); Oe(2,0,1,"S"); O(2,1,0); Oe(2,1,0,"S"); O(2,1,1); Oe(2,1,1,"S"); Pc(0,1,"V"); Pt(1,1); Pc(1,0,"V")
+            O(3,0,0); Oe(3,0,0); O(3,1,0); Oe(3,1,0); O(3,0,1); Oe(3,0,1); O(3,1,1); Oe(3,1,1); C(2,0,0,"V"); C(2,1,0,"V"); C(2,0,1,"V"); C(2,1,1,"V"); Pc(1,1,"V"); Pt(2,0); Pt(2,1); Pq(0,0); C(3,0,0); C(3,1,0); Pt(3,0); Pq(0,1); C(3,0,1); C(3,1,1); Pc(2,0); Pt(3,1); Pc(2,1)
+            Pc(3,0); Pq(2,0); Pq(2,1); Pc(3,1); Pq(3,0); Pq(3,1)
+            store_scales()

@@ -46,36 +46,40 @@ def tile_innerproductsigmoidresidualprojection_kernel(tc, z, y, adj, g, bj, v, r
             return psum.tile([P, 512], F32, name=tag, tag=tag)
 
         vecs = {name: tile([P, 2, 4], BF16, "vec_" + name) for name in ("r", "g", "bj", "v")}
-        y_scaled = [tile([P, 4, D], BF16, "y_scaled_%d" % G) for G in range(2)]
-        yr_bf = [tile([P, D, 4], BF16, "yr_bf_%d" % G) for G in range(2)]
-        yr_codes = [tile([P, D], U32, "yr_codes_%d" % G) for G in range(2)]
-        yr_scales = [tile([P, D], U8, "yr_scales_%d" % G) for G in range(2)]
-        yg_codes = [tile([P, M], U32, "yg_codes_%d" % f) for f in range(2)]
-        yg_scales = [tile([P, M], U8, "yg_scales_%d" % f) for f in range(2)]
+        pairs = [(a, b) for a in range(2) for b in range(2)]
+        y_scaled_halves = [tile([P, 4, 512], BF16, "y_scaled_0%d" % f) for f in range(2)]
+        y_scaled_whole = tile([P, 4, D], BF16, "y_scaled_1")
+        yr_bf = {(G, h): tile([P, 512, 4], BF16, "yr_bf_%d%d" % (G, h)) for G, h in pairs}
+        yr_codes = {(G, h): tile([P, 512], U32, "yr_codes_%d%d" % (G, h)) for G, h in pairs}
+        yr_scales = {(G, h): tile([P, 512], U8, "yr_scales_%d%d" % (G, h)) for G, h in pairs}
+        yg_codes = {(G, f): tile([P, 512], U32, "yg_codes_%d%d" % (G, f)) for G, f in pairs}
+        yg_scales = {(G, f): tile([P, 512], U8, "yg_scales_%d%d" % (G, f)) for G, f in pairs}
         out_scales = tile([P, 2, N], U8, "out_scales")
         ident = tile([P, P], F32, "ident")
-        r_f32 = tile([P, 2, 4], F32, "r_f32")
         warm = tile([P, 1], F32, "warm")
 
-        y_raw, y_rows, z_raw, a_raw = {}, {}, {}, {}
+        y_raw, y_whole, z_raw, a_raw = {}, {}, {}, {}
         t_y, t_z, t_a, t_o, t_p = {}, {}, {}, {}, {}
         yg_bf, z_bf, z_codes, z_scales, pr = {}, {}, {}, {}, {}
-        res_bf, res_codes, res_scales, of, cast, p_bf, p_codes = {}, {}, {}, {}, {}, {}, {}
+        res_bf, res_mx, of, cast, p_bf, p_codes = {}, {}, {}, {}, {}, {}
 
-        def load_y(G, jp, halves=1):
-            src = y[512 * G : 512 * G + 512, :].rearrange("(p j) d -> p j d", j=4)[:, 2 * jp : 2 * jp + 2, :]
-            if halves == 1:
-                whole = tile([P, 2, D], BF16, "raw_y%d" % (2 * G + jp))
-                nc.sync.dma_start(out=whole[:], in_=src)
-                for f in range(2):
-                    y_raw[G, jp, f] = whole[:, :, 512 * f : 512 * f + 512]
-                y_rows[G, jp] = [(whole[:], slice(0, D))]
-                return
+        def y_pair(G, jp):
+            return y[512 * G : 512 * G + 512, :].rearrange("(p j) d -> p j d", j=4)[:, 2 * jp : 2 * jp + 2, :]
+
+        def load_y(G, jp):
+            whole = tile([P, 2, D], BF16, "raw_y%d" % (2 * G + jp))
+            nc.sync.dma_start(out=whole[:], in_=y_pair(G, jp))
             for f in range(2):
-                half = tile([P, 2, 512], BF16, "raw_half%d" % f)
-                nc.sync.dma_start(out=half[:], in_=src[:, :, 512 * f : 512 * f + 512])
-                y_raw[G, jp, f] = half[:]
-            y_rows[G, jp] = [(y_raw[G, jp, f], slice(512 * f, 512 * f + 512)) for f in range(2)]
+                y_raw[G, jp, f] = whole[:, :, 512 * f : 512 * f + 512]
+            y_whole[G, jp] = whole
+
+        def load_y_half(G, jp, f):
+            half = tile([P, 2, 512], BF16, "raw_half%d" % (2 * jp + f))
+            nc.sync.dma_start(out=half[:], in_=y_pair(G, jp)[:, :, 512 * f : 512 * f + 512])
+            y_raw[G, jp, f] = half[:]
+
+        def load_vec(name, src, queue):
+            queue.dma_start(out=vecs[name][:], in_=src.rearrange("(G p t) -> p G t", p=P, t=4))
 
         def load_rows(dst, src, c, name):
             dst[c] = tile([P, 2, D], BF16, "raw_%s%d" % (name, c))
@@ -100,8 +104,7 @@ def tile_innerproductsigmoidresidualprojection_kernel(tc, z, y, adj, g, bj, v, r
             nc.vector.tensor_tensor(out=dst, in0=src, in1=fac, op=ALU.mult)
 
         def Yq(G, f):
-            cols = slice(512 * G, 512 * G + 512)
-            nc.vector.quantize_mx(out=yg_codes[f][:, cols].bitcast(FP8X4), scales=yg_scales[f][:, cols], in_=yg_bf[G, f][:].rearrange("p m t -> p (m t)"))
+            nc.vector.quantize_mx(out=yg_codes[G, f][:].bitcast(FP8X4), scales=yg_scales[G, f][:], in_=yg_bf[G, f][:].rearrange("p m t -> p (m t)"))
 
         def Z(c, f):
             t_z[c, f] = ring_bank()
@@ -123,32 +126,34 @@ def tile_innerproductsigmoidresidualprojection_kernel(tc, z, y, adj, g, bj, v, r
             z_scales[H, f] = tile([P, 512], U8, "z_scales_%d" % (2 * H + f))
             nc.vector.quantize_mx(out=z_codes[H, f][:].bitcast(FP8X4), scales=z_scales[H, f][:], in_=z_bf[H, f][:].rearrange("p n t -> p (n t)"))
 
-        def YRs(G, j, engine="V"):
-            for src, cols in y_rows[G, j // 2]:
-                dst = y_scaled[G][:, j, cols]
-                if engine == "V":
-                    nc.vector.tensor_scalar_mul(dst, src[:, j % 2, :], vecs["r"][:, G, j : j + 1])
-                elif engine == "S":
-                    nc.scalar.activation(out=dst, in_=src[:, j % 2, :], func=ACT.Copy, scale=r_f32[:, G, j : j + 1])
-                else:
-                    nc.gpsimd.tensor_scalar(out=dst, in0=src[:, j % 2, :], scalar1=r_f32[:, G, j : j + 1], scalar2=0.0, op0=ALU.mult, op1=ALU.add)
+        def YRs(G, j):
+            nc.vector.tensor_scalar_mul(y_scaled_whole[:, j, :], y_whole[G, j // 2][:, j % 2, :], vecs["r"][:, G, j : j + 1])
+
+        def YRh(G, j, f):
+            nc.vector.tensor_scalar_mul(y_scaled_halves[f][:, j, :], y_raw[G, j // 2, f][:, j % 2, :], vecs["r"][:, G, j : j + 1])
 
         def YRi(G, q, engine="S"):
-            cols = slice(CH * q, CH * q + CH)
-            copy = nc.scalar.copy if engine == "S" else nc.vector.tensor_copy
-            copy(out=yr_bf[G][:, cols, :].rearrange("p (c i) t -> p c t i", i=4), in_=y_scaled[G][:, :, cols].rearrange("p t (c i) -> p c t i", i=4))
+            h, k = divmod(q, 2)
+            src = y_scaled_halves[h][:, :, CH * k : CH * k + CH] if G == 0 else y_scaled_whole[:, :, CH * q : CH * q + CH]
+            src = src.rearrange("p t (c i) -> p c t i", i=4)
+            dst = yr_bf[G, h][:, CH * k : CH * k + CH, :].rearrange("p (c i) t -> p c t i", i=4)
+            if engine == "S":
+                nc.scalar.copy(out=dst, in_=src)
+            elif engine == "V":
+                nc.vector.tensor_copy(out=dst, in_=src)
+            else:
+                nc.gpsimd.tensor_scalar(out=dst, in0=src, scalar1=1.0, scalar2=0.0, op0=ALU.mult, op1=ALU.add)
 
         def YRq(G, h):
-            cols = slice(512 * h, 512 * h + 512)
-            nc.vector.quantize_mx(out=yr_codes[G][:, cols].bitcast(FP8X4), scales=yr_scales[G][:, cols], in_=yr_bf[G][:, cols, :].rearrange("p d t -> p (d t)"))
+            nc.vector.quantize_mx(out=yr_codes[G, h][:].bitcast(FP8X4), scales=yr_scales[G, h][:], in_=yr_bf[G, h][:].rearrange("p d t -> p (d t)"))
 
         def S1(H, G, t):
             if t == 0:
                 pr[H, G] = tile([P, 4, 512], F32, "pr_%d" % (2 * H + G))
             bank = ring_bank()
-            m0 = 512 * G + P * t
+            m0 = P * t
             for f in range(2):
-                nc.tensor.matmul_mx(out=bank[:], lhsT=yg_codes[f][:, m0 : m0 + P].bitcast(FP8X4), lhsT_scale=yg_scales[f][:, m0 : m0 + P], rhs=z_codes[H, f][:].bitcast(FP8X4), rhs_scale=z_scales[H, f][:], start=(f == 0), stop=(f == 1))
+                nc.tensor.matmul_mx(out=bank[:], lhsT=yg_codes[G, f][:, m0 : m0 + P].bitcast(FP8X4), lhsT_scale=yg_scales[G, f][:, m0 : m0 + P], rhs=z_codes[H, f][:].bitcast(FP8X4), rhs_scale=z_scales[H, f][:], start=(f == 0), stop=(f == 1))
             nc.scalar.activation(out=pr[H, G][:, t, :], in_=bank[:], func=ACT.Sigmoid, bias=vecs["bj"][:, G, t : t + 1], scale=1.0 / 32.0)
 
         def probs(c, G):
@@ -158,27 +163,45 @@ def tile_innerproductsigmoidresidualprojection_kernel(tc, z, y, adj, g, bj, v, r
             view = probs(c, G).rearrange("p (u e) n -> p u e n", u=2)
             nc.vector.tensor_tensor(out=view, in0=view, in1=t_a[c, G][:].bitcast(BF16).rearrange("p (u n e) -> p u e n", u=2, e=2), op=ALU.subtract)
 
-        def Mu(c, G):
-            if G == 0:
-                res_bf[c] = tile([P, 2, CH, 4], BF16, "res_bf_%d" % (c % 2))
+        def times_v(dst, src, G, width):
             nc.vector.tensor_tensor(
-                out=res_bf[c][:, G, :, :].rearrange("p (c i) t -> p c t i", i=4),
-                in0=probs(c, G).rearrange("p t (c i) -> p c t i", i=4),
-                in1=vecs["v"][:, G, :].unsqueeze(1).unsqueeze(3).to_broadcast([P, CH // 4, 4, 4]),
+                out=dst.rearrange("p (c i) t -> p c t i", i=4),
+                in0=src.rearrange("p t (c i) -> p c t i", i=4),
+                in1=vecs["v"][:, G, :].unsqueeze(1).unsqueeze(3).to_broadcast([P, width // 4, 4, 4]),
                 op=ALU.mult,
             )
 
+        def quantize_res(key, src, width):
+            codes = tile([P, 2, width], U32, "res_codes_%s" % key)
+            scales = tile([P, 2, width], U8, "res_scales_%s" % key)
+            nc.vector.quantize_mx(out=codes[:].rearrange("p G n -> p (G n)").bitcast(FP8X4), scales=scales[:].rearrange("p G n -> p (G n)"), in_=src.rearrange("p G n t -> p (G n t)"))
+            return codes, scales
+
+        def Mu(c, G):
+            if G == 0:
+                res_bf[c] = tile([P, 2, CH, 4], BF16, "res_bf_%d" % (c % 2))
+            times_v(res_bf[c][:, G, :, :], probs(c, G), G, CH)
+
         def Rq(c):
-            res_codes[c] = tile([P, 2 * CH], U32, "res_codes_%d" % c)
-            res_scales[c] = tile([P, 2 * CH], U8, "res_scales_%d" % c)
-            nc.vector.quantize_mx(out=res_codes[c][:].bitcast(FP8X4), scales=res_scales[c][:], in_=res_bf[c][:].rearrange("p f n t -> p (f n t)"))
+            codes, scales = quantize_res(str(c), res_bf[c][:], CH)
+            for i in range(2):
+                res_mx[c, i] = (codes[:, :, P * i : P * i + P], scales[:, :, P * i : P * i + P])
+
+        def Mh(c, G, i):
+            if G == 0:
+                res_bf[c, i] = tile([P, 2, P, 4], BF16, "res_half_%d" % i)
+            times_v(res_bf[c, i][:, G, :, :], probs(c, G)[:, :, P * i : P * i + P], G, P)
+
+        def Rh(c, i):
+            codes, scales = quantize_res("half_%d" % i, res_bf[c, i][:], P)
+            res_mx[c, i] = (codes[:], scales[:])
 
         def O(c, i, h):
             bank = ring_bank()
             t_o[c, i, h] = bank
+            codes, scales = res_mx[c, i]
             for G in range(2):
-                cols = slice(CH * G + P * i, CH * G + P * i + P)
-                nc.tensor.matmul_mx(out=bank[:], lhsT=res_codes[c][:, cols].bitcast(FP8X4), lhsT_scale=res_scales[c][:, cols], rhs=yr_codes[G][:, 512 * h : 512 * h + 512].bitcast(FP8X4), rhs_scale=yr_scales[G][:, 512 * h : 512 * h + 512], start=(G == 0), stop=(G == 1))
+                nc.tensor.matmul_mx(out=bank[:], lhsT=codes[:, G, :].bitcast(FP8X4), lhsT_scale=scales[:, G, :], rhs=yr_codes[G, h][:].bitcast(FP8X4), rhs_scale=yr_scales[G, h][:], start=(G == 0), stop=(G == 1))
 
         def Oe(c, i, h, engine="S"):
             if h == 0:
@@ -188,8 +211,11 @@ def tile_innerproductsigmoidresidualprojection_kernel(tc, z, y, adj, g, bj, v, r
                 nc.scalar.mul(dst, t_o[c, i, h][:], 1.0 / 32.0)
             else:
                 nc.vector.tensor_scalar_mul(dst, t_o[c, i, h][:], 1.0 / 32.0)
-            if h == 1:
-                nc.sync.dma_start(out=out_0[CH * c : CH * c + CH, :].rearrange("(p i) d -> p i d", i=2)[:, i, :], in_=of[c, i][:])
+            rows = out_0[CH * c : CH * c + CH, :].rearrange("(p i) d -> p i d", i=2)[:, i, :]
+            if (c, i) == (NCH - 1, 1):
+                nc.sync.dma_start(out=rows[:, 512 * h : 512 * h + 512], in_=dst)
+            elif h == 1:
+                nc.sync.dma_start(out=rows, in_=of[c, i][:])
 
         def C(c, i, h, engine="V"):
             cast[c, i, h] = tile([P, 512], BF16, "cast_%d" % (4 * c + 2 * i + h))
@@ -216,12 +242,8 @@ def tile_innerproductsigmoidresidualprojection_kernel(tc, z, y, adj, g, bj, v, r
                     nc.tensor.transpose(bank[:, CH * u + P * i : CH * u + P * i + P], words[:, P * u : P * u + P], ident[:])
 
         def Pc(c, f, engine="S"):
-            if c == 0:
-                p_bf[0, f] = tile([P, 2 * CH, 4], BF16, "turned_%d" % f)
-            elif c > 1:
-                p_bf[c, f] = tile([P, CH, 4], BF16, "p_bf_%d" % (2 * c + f))
-            rows = p_bf[0, f][:, CH * c : CH * c + CH, :] if c < 2 else p_bf[c, f][:]
-            dst = rows.rearrange("p n t -> p (n t)").bitcast(F32).rearrange("p (q i u) -> p q i u", i=2, u=2)
+            p_bf[c, f] = tile([P, CH, 4], BF16, "turned_%d" % (2 * (c % 2) + f))
+            dst = p_bf[c, f][:].rearrange("p n t -> p (n t)").bitcast(F32).rearrange("p (q i u) -> p q i u", i=2, u=2)
             src = t_p[c, f][:].rearrange("p (u i q) -> p q i u", u=2, i=2)
             if engine == "S":
                 nc.scalar.copy(out=dst, in_=src)
@@ -229,10 +251,12 @@ def tile_innerproductsigmoidresidualprojection_kernel(tc, z, y, adj, g, bj, v, r
                 nc.vector.tensor_copy(out=dst, in_=src)
 
         def Pq(c, f):
-            n0, width = CH * c, 2 * CH if c == 0 else CH
-            p_codes[c, f] = tile([P, width], U32, "p_codes_%d" % (2 * c + f))
-            nc.vector.quantize_mx(out=p_codes[c, f][:].bitcast(FP8X4), scales=out_scales[:, f, n0 : n0 + width], in_=p_bf[c, f][:].rearrange("p n t -> p (n t)"))
-            nc.sync.dma_start(out=out_1[f, :, n0 : n0 + width, :].rearrange("p n t -> p (n t)").bitcast(I32), in_=p_codes[c, f][:].bitcast(I32))
+            cols = slice(CH * c, CH * c + CH)
+            if f == 0:
+                p_codes[c] = tile([P, 2, CH], U32, "p_codes_%d" % c)
+            nc.vector.quantize_mx(out=p_codes[c][:, f, :].bitcast(FP8X4), scales=out_scales[:, f, cols], in_=p_bf[c, f][:].rearrange("p n t -> p (n t)"))
+            if f == 1:
+                nc.sync.dma_start(out=out_1[:, :, cols, :].rearrange("f p n t -> p f (n t)").bitcast(I32), in_=p_codes[c][:].bitcast(I32))
 
         def store_scales():
             for Q in range(4):
@@ -240,34 +264,34 @@ def tile_innerproductsigmoidresidualprojection_kernel(tc, z, y, adj, g, bj, v, r
                 queue.dma_start(out=out_2[:, 4 * Q : 4 * Q + 4, :].rearrange("f q n -> q f n").bitcast(I32), in_=out_scales[32 * Q : 32 * Q + 4, :, :].bitcast(I32))
 
         with tc.manual_schedule():
-            for name, src in (("r", r), ("g", g), ("bj", bj), ("v", v)):
-                nc.scalar.dma_start(out=vecs[name][:], in_=src.rearrange("(G p t) -> p G t", p=P, t=4))
+            load_vec("r", r, nc.scalar)
+            load_vec("g", g, nc.scalar)
             make_identity(nc, ident[:])
             nc.scalar.activation(out=warm[:], in_=ident[:, 0:1], func=ACT.Sigmoid)
-            load_y(0, 0, halves=2)
-            load_y(0, 1)
+            for f in range(2):
+                for jp in range(2):
+                    load_y_half(0, jp, f)
             load_rows(z_raw, z, 0, "z")
             load_rows(z_raw, z, 1, "z")
             load_y(1, 0)
             load_y(1, 1)
+            load_vec("bj", bj, nc.sync)
+            load_vec("v", v, nc.sync)
             load_rows(a_raw, adj, 0, "a")
             load_rows(a_raw, adj, 1, "a")
             load_rows(z_raw, z, 2, "z")
             load_rows(z_raw, z, 3, "z")
             for c in range(2, NCH):
                 load_rows(a_raw, adj, c, "a")
-            nc.scalar.copy(out=r_f32[:], in_=vecs["r"][:])
-            Y(0,0,0); Ye(0,0,0); Y(0,0,1); Ye(0,0,1); YRs(0,0,"S"); YRs(0,1,"S")
-            Y(0,1,0); Y(0,1,1); YRs(0,2); YRs(0,3); Ye(0,1,0); Ye(0,1,1); YRi(0,0)
-            Z(0,0); Zc(0,0); Z(0,1); Zc(0,1); Yq(0,0); Yq(0,1); Z(1,0); Zc(1,0); Z(1,1); Zc(1,1)
-            Y(1,0,0); YRs(1,0); YRs(1,1); Zq(0,0); Ye(1,0,0); Y(1,0,1); Zq(0,1); Ye(1,0,1); YRi(0,1); YRi(0,2)
-            Y(1,1,0); Ye(1,1,0); Y(1,1,1); Ye(1,1,1)
-            S1(0,0,0); S1(0,0,1); S1(0,0,2); S1(0,0,3); Yq(1,0); Yq(1,1); YRs(1,2); YRs(1,3); YRq(0,0)
-            A(0,0); A(1,0); YRi(0,3); Z(2,0); Zc(2,0); Z(2,1); Zc(2,1); Z(3,0); Zc(3,0); Z(3,1); Zc(3,1); R(0,0); R(1,0); Mu(0,0); YRq(0,1); Mu(1,0)
-            YRi(1,0); S1(0,1,0); S1(0,1,1); S1(0,1,2); S1(0,1,3); A(0,1); A(1,1); Zq(1,0); Zq(1,1); YRi(1,1,"V"); R(0,1); R(1,1); YRq(1,0); Mu(0,1); Mu(1,1)
-            YRi(1,2); S1(1,0,0); S1(1,0,1); S1(1,0,2); S1(1,0,3); A(2,0); YRi(1,3); S1(1,1,0); S1(1,1,1); S1(1,1,2); S1(1,1,3); A(2,1); Rq(0); R(2,0); YRq(1,1); Rq(1); Mu(2,0); A(3,0)
-            O(0,0,0); C(0,0,0,"PS"); Oe(0,0,0); O(0,0,1); C(0,0,1,"PS"); Oe(0,0,1); R(2,1); A(3,1); O(0,1,0); C(0,1,0,"PS"); Oe(0,1,0); O(0,1,1); C(0,1,1,"PS"); Oe(0,1,1); R(3,0); Mu(2,1); R(3,1); Rq(2); O(1,0,0); C(1,0,0,"PS"); Oe(1,0,0); O(1,0,1); Oe(1,0,1,"S"); O(1,1,0); C(1,1,0,"PS"); Oe(1,1,0); O(1,1,1); Oe(1,1,1,"S")
-            Pt(0,0); Pt(0,1); Mu(3,0); Mu(3,1); C(1,0,1); Rq(3); C(1,1,1); Pt(1,0); Pc(0,0); O(2,0,0); Oe(2,0,0,"S"); O(2,0,1); Oe(2,0,1,"S"); O(2,1,0); Oe(2,1,0,"S"); O(2,1,1); Oe(2,1,1,"S"); Pc(0,1,"V"); Pt(1,1); Pc(1,0,"V")
-            O(3,0,0); Oe(3,0,0); O(3,1,0); Oe(3,1,0); O(3,0,1); Oe(3,0,1); O(3,1,1); Oe(3,1,1); C(2,0,0,"V"); C(2,1,0,"V"); C(2,0,1,"V"); C(2,1,1,"V"); Pc(1,1,"V"); Pt(2,0); Pt(2,1); Pq(0,0); C(3,0,0); C(3,1,0); Pt(3,0); Pq(0,1); C(3,0,1); C(3,1,1); Pc(2,0); Pt(3,1); Pc(2,1)
-            Pc(3,0); Pq(2,0); Pq(2,1); Pc(3,1); Pq(3,0); Pq(3,1)
+            Y(0,0,0); YRh(0,0,0); YRh(0,1,0); Y(0,1,0); YRh(0,2,0); YRh(0,3,0); Ye(0,0,0); YRi(0,0); YRi(0,1); Y(0,0,1); Y(0,1,1); Ye(0,1,0); YRh(0,0,1); YRh(0,1,1); Ye(0,0,1); Yq(0,0); YRh(0,2,1); YRh(0,3,1); Ye(0,1,1)
+            Z(0,0); Zc(0,0); Z(0,1); Zc(0,1); YRq(0,0); Yq(0,1); Z(1,0); Zc(1,0); Z(1,1); Zc(1,1); YRi(0,2); YRi(0,3)
+            Y(1,0,0); YRs(1,0); YRs(1,1); Zq(0,0); Ye(1,0,0); Y(1,0,1); Zq(0,1); Ye(1,0,1)
+            Y(1,1,0); Y(1,1,1); YRs(1,2); YRs(1,3); Ye(1,1,0); Ye(1,1,1)
+            S1(0,0,0); S1(0,0,1); S1(0,0,2); S1(0,0,3); Yq(1,0); Yq(1,1); YRq(0,1); YRi(1,0)
+            A(0,0); A(1,0); S1(0,1,0); Z(2,0); Zc(2,0); Z(2,1); Zc(2,1); S1(0,1,1); Z(3,0); Zc(3,0); Z(3,1); Zc(3,1); S1(0,1,2); S1(0,1,3); A(0,1); R(0,0); A(1,1); R(1,0); Mu(0,0); Mu(1,0); Zq(1,0); Zq(1,1); YRi(1,1,"V"); YRi(1,2); YRi(1,3)
+            R(0,1); R(1,1); YRq(1,0); Mu(0,1); YRq(1,1); Rq(0); S1(1,0,0); S1(1,0,1); S1(1,0,2); S1(1,0,3); A(2,0); Mu(1,1); S1(1,1,0); S1(1,1,1); S1(1,1,2); S1(1,1,3); A(2,1); R(2,0); Rq(1); R(2,1)
+            O(0,0,0); C(0,0,0,"PS"); Oe(0,0,0); O(0,0,1); C(0,0,1,"PS"); Oe(0,0,1); O(0,1,0); C(0,1,0,"PS"); Oe(0,1,0); O(0,1,1); C(0,1,1,"PS"); Oe(0,1,1); A(3,0); A(3,1); Mu(2,0); R(3,0); Mu(2,1); Mh(3,0,0); Rq(2); O(1,0,0); C(1,0,0,"PS"); Oe(1,0,0); O(1,0,1); Oe(1,0,1,"S"); Pt(0,0); Pt(0,1); O(1,1,0); C(1,1,0,"PS"); Oe(1,1,0); O(1,1,1); Oe(1,1,1,"S"); R(3,1)
+            Pc(0,0); Pc(0,1); Mh(3,0,1); Mh(3,1,0); C(1,0,1); C(1,1,1); O(2,0,0); Oe(2,0,0,"S"); O(2,0,1); Oe(2,0,1,"S"); Pt(1,0); O(2,1,0); Oe(2,1,0,"S"); O(2,1,1); Oe(2,1,1,"S"); Pt(1,1); Rh(3,0); Mh(3,1,1); Pq(0,0); Rh(3,1); Pq(0,1); Pc(1,0); Pc(1,1)
+            O(3,0,0); Oe(3,0,0,"S"); O(3,0,1); Oe(3,0,1,"S"); C(2,0,0,"V"); C(2,1,0,"V"); C(2,0,1,"V"); C(2,1,1,"V"); O(3,1,0); O(3,1,1); Pt(2,0); Pt(2,1); Pq(1,0); Pq(1,1); C(3,1,0,"PS"); C(3,0,0); Pt(3,0); C(3,1,1,"PS"); C(3,0,1); Pt(3,1); Oe(3,1,0)
+            Pc(2,0,"V"); Pc(2,1,"V"); Pc(3,0); Pc(3,1); Pq(2,0); Pq(2,1); Oe(3,1,1,"V"); Pq(3,0); Pq(3,1)
             store_scales()

@@ -20,6 +20,8 @@ CH = 256
 NCH = N // CH
 RING = 5
 ADJ_BANKS = 3
+SCALED_TAG = "turned_0"
+LAST_TAG = "turned_1"
 
 
 def tile_innerproductsigmoidresidualprojection_kernel(tc, z, y, adj, g, bj, v, r, out_0, out_1, out_2):
@@ -46,21 +48,21 @@ def tile_innerproductsigmoidresidualprojection_kernel(tc, z, y, adj, g, bj, v, r
             return psum.tile([P, 512], F32, name=tag, tag=tag)
 
         vecs = {name: tile([P, 2, 4], BF16, "vec_" + name) for name in ("r", "g", "bj", "v")}
-        pairs = [(a, b) for a in range(2) for b in range(2)]
         y_scaled_halves = [tile([P, 4, 512], BF16, "y_scaled_0%d" % f) for f in range(2)]
-        y_scaled_whole = tile([P, 4, D], BF16, "y_scaled_1")
-        yr_bf = {(G, h): tile([P, 512, 4], BF16, "yr_bf_%d%d" % (G, h)) for G, h in pairs}
-        yr_codes = {(G, h): tile([P, 512], U32, "yr_codes_%d%d" % (G, h)) for G, h in pairs}
-        yr_scales = {(G, h): tile([P, 512], U8, "yr_scales_%d%d" % (G, h)) for G, h in pairs}
-        yg_codes = {(G, f): tile([P, 512], U32, "yg_codes_%d%d" % (G, f)) for G, f in pairs}
-        yg_scales = {(G, f): tile([P, 512], U8, "yg_scales_%d%d" % (G, f)) for G, f in pairs}
+        y_scaled_late, yr_bf = {}, {}
+        yr_codes = [tile([P, D], U32, "yr_codes_%d" % G) for G in range(2)]
+        yr_scales = [tile([P, D], U8, "yr_scales_%d" % G) for G in range(2)]
+        yg_bf = [tile([P, 2, 512, 4], BF16, "yg_bf_%d" % G) for G in range(2)]
+        yg_codes = [tile([P, 2, 512], U32, "yg_codes_%d" % G) for G in range(2)]
+        yg_scales = [tile([P, 2, 512], U8, "yg_scales_%d" % G) for G in range(2)]
         out_scales = tile([P, 2, N], U8, "out_scales")
         ident = tile([P, P], F32, "ident")
+        r_f32 = tile([P, 2, 4], F32, "r_f32")
         warm = tile([P, 1], F32, "warm")
 
         y_raw, y_whole, z_raw, a_raw = {}, {}, {}, {}
         t_y, t_z, t_a, t_o, t_p = {}, {}, {}, {}, {}
-        yg_bf, z_bf, z_codes, z_scales, pr = {}, {}, {}, {}, {}
+        z_bf, z_codes, z_scales, pr = {}, {}, {}, {}
         res_bf, res_mx, of, cast, p_bf, p_codes = {}, {}, {}, {}, {}, {}
 
         def y_pair(G, jp):
@@ -92,19 +94,23 @@ def tile_innerproductsigmoidresidualprojection_kernel(tc, z, y, adj, g, bj, v, r
                     nc.tensor.transpose(bank[:, CH * u + P * i : CH * u + P * i + P], words[:, u:256:2], ident[:])
 
         def Y(G, jp, f):
-            t_y[G, jp, f] = ring_bank()
+            t_y[G, jp, f] = side_bank() if G == 1 and (jp, f) != (1, 1) else ring_bank()
             turn(t_y[G, jp, f], y_raw[G, jp, f])
 
         def Ye(G, jp, f):
-            if jp == 0:
-                yg_bf[G, f] = tile([P, 512, 4], BF16, "yg_bf_%d" % (2 * G + f))
             src = t_y[G, jp, f][:].bitcast(BF16).rearrange("p (u m e) -> p m u e", u=2, e=2)
-            dst = yg_bf[G, f][:, CH * jp : CH * jp + CH, :].rearrange("p m (u e) -> p m u e", u=2)
+            dst = yg_bf[G][:, f, CH * jp : CH * jp + CH, :].rearrange("p m (u e) -> p m u e", u=2)
             fac = vecs["g"][:, f, :].unsqueeze(1).to_broadcast([P, CH, 4]).rearrange("p m (u e) -> p m u e", u=2)
             nc.vector.tensor_tensor(out=dst, in0=src, in1=fac, op=ALU.mult)
 
-        def Yq(G, f):
-            nc.vector.quantize_mx(out=yg_codes[G, f][:].bitcast(FP8X4), scales=yg_scales[G, f][:], in_=yg_bf[G, f][:].rearrange("p m t -> p (m t)"))
+        def quantize(codes, scales, src):
+            nc.vector.quantize_mx(out=codes.bitcast(FP8X4), scales=scales, in_=src)
+
+        def quantize_pair(codes, scales, src):
+            quantize(codes[:].rearrange("p a n -> p (a n)"), scales[:].rearrange("p a n -> p (a n)"), src[:].rearrange("p a n t -> p (a n t)"))
+
+        def Yq(G):
+            quantize_pair(yg_codes[G], yg_scales[G], yg_bf[G])
 
         def Z(c, f):
             t_z[c, f] = ring_bank()
@@ -116,36 +122,46 @@ def tile_innerproductsigmoidresidualprojection_kernel(tc, z, y, adj, g, bj, v, r
 
         def Zc(c, f):
             H, k = divmod(c, 2)
-            if (H, f) not in z_bf:
-                z_bf[H, f] = tile([P, 512, 4], BF16, "turned_%d" % (2 * H + f))
-            dst = z_bf[H, f][:, CH * k : CH * k + CH, :].rearrange("p n t -> p (n t)").bitcast(F32).rearrange("p (n u) -> p n u", u=2)
+            if H not in z_bf:
+                z_bf[H] = tile([P, 2, 512, 4], BF16, "turned_%d" % H)
+            dst = z_bf[H][:, f, CH * k : CH * k + CH, :].rearrange("p n t -> p (n t)").bitcast(F32).rearrange("p (n u) -> p n u", u=2)
             nc.scalar.copy(out=dst, in_=t_z[c, f][:].rearrange("p (u n) -> p n u", u=2))
 
-        def Zq(H, f):
-            z_codes[H, f] = tile([P, 512], U32, "z_codes_%d" % (2 * H + f))
-            z_scales[H, f] = tile([P, 512], U8, "z_scales_%d" % (2 * H + f))
-            nc.vector.quantize_mx(out=z_codes[H, f][:].bitcast(FP8X4), scales=z_scales[H, f][:], in_=z_bf[H, f][:].rearrange("p n t -> p (n t)"))
+        def Zq(H, f=None):
+            if H not in z_codes:
+                z_codes[H] = tile([P, 2, 512], U32, "z_codes_%d" % H)
+                z_scales[H] = tile([P, 2, 512], U8, "z_scales_%d" % H)
+            if f is None:
+                quantize_pair(z_codes[H], z_scales[H], z_bf[H])
+            else:
+                quantize(z_codes[H][:, f, :], z_scales[H][:, f, :], z_bf[H][:, f, :, :].rearrange("p n t -> p (n t)"))
 
-        def YRs(G, j):
-            nc.vector.tensor_scalar_mul(y_scaled_whole[:, j, :], y_whole[G, j // 2][:, j % 2, :], vecs["r"][:, G, j : j + 1])
+        def YRs(G, j, engine="V"):
+            if G not in y_scaled_late:
+                y_scaled_late[G] = tile([P, 4, D], BF16, SCALED_TAG)
+            dst, src = y_scaled_late[G][:, j, :], y_whole[G, j // 2][:, j % 2, :]
+            if engine == "V":
+                nc.vector.tensor_scalar_mul(dst, src, vecs["r"][:, G, j : j + 1])
+            else:
+                nc.gpsimd.tensor_scalar(out=dst, in0=src, scalar1=r_f32[:, G, j : j + 1], scalar2=0.0, op0=ALU.mult, op1=ALU.add)
 
         def YRh(G, j, f):
             nc.vector.tensor_scalar_mul(y_scaled_halves[f][:, j, :], y_raw[G, j // 2, f][:, j % 2, :], vecs["r"][:, G, j : j + 1])
 
-        def YRi(G, q, engine="S"):
-            h, k = divmod(q, 2)
-            src = y_scaled_halves[h][:, :, CH * k : CH * k + CH] if G == 0 else y_scaled_whole[:, :, CH * q : CH * q + CH]
-            src = src.rearrange("p t (c i) -> p c t i", i=4)
-            dst = yr_bf[G, h][:, CH * k : CH * k + CH, :].rearrange("p (c i) t -> p c t i", i=4)
+        def YRi(G, d0, width, engine="S"):
+            src = y_scaled_halves[d0 // 512][:, :, d0 % 512 : d0 % 512 + width] if G == 0 else y_scaled_late[G][:, :, d0 : d0 + width]
+            h, k0 = divmod(d0, 512)
+            if (G, h) not in yr_bf:
+                yr_bf[G, h] = tile([P, 512, 4], BF16, LAST_TAG if (G, h) == (1, 1) else "yr_bf_%d%d" % (G, h))
+            dst = yr_bf[G, h][:, k0 : k0 + width, :]
             if engine == "S":
-                nc.scalar.copy(out=dst, in_=src)
-            elif engine == "V":
-                nc.vector.tensor_copy(out=dst, in_=src)
+                nc.scalar.copy(out=dst.rearrange("p (c i) t -> p c t i", i=4), in_=src.rearrange("p t (c i) -> p c t i", i=4))
             else:
-                nc.gpsimd.tensor_scalar(out=dst, in0=src, scalar1=1.0, scalar2=0.0, op0=ALU.mult, op1=ALU.add)
+                nc.gpsimd.tensor_scalar(out=dst, in0=src.rearrange("p t d -> p d t"), scalar1=1.0, scalar2=0.0, op0=ALU.mult, op1=ALU.add)
 
         def YRq(G, h):
-            nc.vector.quantize_mx(out=yr_codes[G, h][:].bitcast(FP8X4), scales=yr_scales[G, h][:], in_=yr_bf[G, h][:].rearrange("p d t -> p (d t)"))
+            cols = slice(512 * h, 512 * h + 512)
+            quantize(yr_codes[G][:, cols], yr_scales[G][:, cols], yr_bf[G, h][:].rearrange("p d t -> p (d t)"))
 
         def S1(H, G, t):
             if t == 0:
@@ -153,7 +169,7 @@ def tile_innerproductsigmoidresidualprojection_kernel(tc, z, y, adj, g, bj, v, r
             bank = ring_bank()
             m0 = P * t
             for f in range(2):
-                nc.tensor.matmul_mx(out=bank[:], lhsT=yg_codes[G, f][:, m0 : m0 + P].bitcast(FP8X4), lhsT_scale=yg_scales[G, f][:, m0 : m0 + P], rhs=z_codes[H, f][:].bitcast(FP8X4), rhs_scale=z_scales[H, f][:], start=(f == 0), stop=(f == 1))
+                nc.tensor.matmul_mx(out=bank[:], lhsT=yg_codes[G][:, f, m0 : m0 + P].bitcast(FP8X4), lhsT_scale=yg_scales[G][:, f, m0 : m0 + P], rhs=z_codes[H][:, f, :].bitcast(FP8X4), rhs_scale=z_scales[H][:, f, :], start=(f == 0), stop=(f == 1))
             nc.scalar.activation(out=pr[H, G][:, t, :], in_=bank[:], func=ACT.Sigmoid, bias=vecs["bj"][:, G, t : t + 1], scale=1.0 / 32.0)
 
         def probs(c, G):
@@ -174,7 +190,7 @@ def tile_innerproductsigmoidresidualprojection_kernel(tc, z, y, adj, g, bj, v, r
         def quantize_res(key, src, width):
             codes = tile([P, 2, width], U32, "res_codes_%s" % key)
             scales = tile([P, 2, width], U8, "res_scales_%s" % key)
-            nc.vector.quantize_mx(out=codes[:].rearrange("p G n -> p (G n)").bitcast(FP8X4), scales=scales[:].rearrange("p G n -> p (G n)"), in_=src.rearrange("p G n t -> p (G n t)"))
+            quantize_pair(codes, scales, src)
             return codes, scales
 
         def Mu(c, G):
@@ -183,9 +199,19 @@ def tile_innerproductsigmoidresidualprojection_kernel(tc, z, y, adj, g, bj, v, r
             times_v(res_bf[c][:, G, :, :], probs(c, G), G, CH)
 
         def Rq(c):
-            codes, scales = quantize_res(str(c), res_bf[c][:], CH)
+            codes, scales = quantize_res(str(c), res_bf[c], CH)
             for i in range(2):
                 res_mx[c, i] = (codes[:, :, P * i : P * i + P], scales[:, :, P * i : P * i + P])
+
+        def Mw(G):
+            if G == 0:
+                res_bf["wide"] = tile([P, 2, 512, 4], BF16, "yg_bf_0")
+            times_v(res_bf["wide"][:, G, :, :], pr[0, G][:], G, 512)
+
+        def Rw():
+            codes, scales = quantize_res("wide", res_bf["wide"], 512)
+            for k in range(4):
+                res_mx[k // 2, k % 2] = (codes[:, :, P * k : P * k + P], scales[:, :, P * k : P * k + P])
 
         def Mh(c, G, i):
             if G == 0:
@@ -193,7 +219,7 @@ def tile_innerproductsigmoidresidualprojection_kernel(tc, z, y, adj, g, bj, v, r
             times_v(res_bf[c, i][:, G, :, :], probs(c, G)[:, :, P * i : P * i + P], G, P)
 
         def Rh(c, i):
-            codes, scales = quantize_res("half_%d" % i, res_bf[c, i][:], P)
+            codes, scales = quantize_res("half_%d" % i, res_bf[c, i], P)
             res_mx[c, i] = (codes[:], scales[:])
 
         def O(c, i, h):
@@ -201,11 +227,11 @@ def tile_innerproductsigmoidresidualprojection_kernel(tc, z, y, adj, g, bj, v, r
             t_o[c, i, h] = bank
             codes, scales = res_mx[c, i]
             for G in range(2):
-                nc.tensor.matmul_mx(out=bank[:], lhsT=codes[:, G, :].bitcast(FP8X4), lhsT_scale=scales[:, G, :], rhs=yr_codes[G, h][:].bitcast(FP8X4), rhs_scale=yr_scales[G, h][:], start=(G == 0), stop=(G == 1))
+                nc.tensor.matmul_mx(out=bank[:], lhsT=codes[:, G, :].bitcast(FP8X4), lhsT_scale=scales[:, G, :], rhs=yr_codes[G][:, 512 * h : 512 * h + 512].bitcast(FP8X4), rhs_scale=yr_scales[G][:, 512 * h : 512 * h + 512], start=(G == 0), stop=(G == 1))
 
         def Oe(c, i, h, engine="S"):
             if h == 0:
-                of[c, i] = tile([P, D], F32, ("raw_z%d" % c) if i == 0 else ("yg_bf_%d" % c))
+                of[c, i] = tile([P, D], F32, ("raw_z%d" % c) if i == 0 else ("raw_a%d" % c))
             dst = of[c, i][:, 512 * h : 512 * h + 512]
             if engine == "S":
                 nc.scalar.mul(dst, t_o[c, i, h][:], 1.0 / 32.0)
@@ -217,9 +243,13 @@ def tile_innerproductsigmoidresidualprojection_kernel(tc, z, y, adj, g, bj, v, r
             elif h == 1:
                 nc.sync.dma_start(out=rows, in_=of[c, i][:])
 
+        def cast_tile(c, i):
+            if (c, i) not in cast:
+                cast[c, i] = tile([P, D], BF16, "cast_%d" % (2 * c + i))
+            return cast[c, i]
+
         def C(c, i, h, engine="V"):
-            cast[c, i, h] = tile([P, 512], BF16, "cast_%d" % (4 * c + 2 * i + h))
-            dst = cast[c, i, h][:].rearrange("p (u q e) -> p u q e", u=2, e=2)
+            dst = cast_tile(c, i)[:, 512 * h : 512 * h + 512].rearrange("p (u q e) -> p u q e", u=2, e=2)
             if engine in ("PS", "PV"):
                 src = t_o[c, i, h][:].rearrange("p (q u e) -> p u q e", u=2, e=2)
                 if engine == "PS":
@@ -233,16 +263,21 @@ def tile_innerproductsigmoidresidualprojection_kernel(tc, z, y, adj, g, bj, v, r
             else:
                 nc.gpsimd.tensor_scalar(out=dst, in0=src, scalar1=1.0, scalar2=0.0, op0=ALU.mult, op1=ALU.add)
 
+        def Cw(c, i):
+            dst = cast_tile(c, i)[:].rearrange("p (h u q e) -> p h u q e", h=2, u=2, e=2)
+            nc.vector.tensor_copy(out=dst, in_=of[c, i][:].rearrange("p (h q u e) -> p h u q e", h=2, u=2, e=2))
+
         def Pt(c, f):
             bank = side_bank()
             t_p[c, f] = bank
             for i in range(2):
-                words = cast[c, i, f][:].bitcast(F32)
+                words = cast[c, i][:].bitcast(F32)
                 for u in range(2):
-                    nc.tensor.transpose(bank[:, CH * u + P * i : CH * u + P * i + P], words[:, P * u : P * u + P], ident[:])
+                    w0 = CH * f + P * u
+                    nc.tensor.transpose(bank[:, CH * u + P * i : CH * u + P * i + P], words[:, w0 : w0 + P], ident[:])
 
         def Pc(c, f, engine="S"):
-            p_bf[c, f] = tile([P, CH, 4], BF16, "turned_%d" % (2 * (c % 2) + f))
+            p_bf[c, f] = tile([P, CH, 4], BF16, "p_bf_%d" % (2 * (c % 2) + f))
             dst = p_bf[c, f][:].rearrange("p n t -> p (n t)").bitcast(F32).rearrange("p (q i u) -> p q i u", i=2, u=2)
             src = t_p[c, f][:].rearrange("p (u i q) -> p q i u", u=2, i=2)
             if engine == "S":
@@ -250,13 +285,15 @@ def tile_innerproductsigmoidresidualprojection_kernel(tc, z, y, adj, g, bj, v, r
             else:
                 nc.vector.tensor_copy(out=dst, in_=src)
 
+        def store_codes(codes, n0, width):
+            nc.sync.dma_start(out=out_1[:, :, n0 : n0 + width, :].rearrange("f p n t -> p f (n t)").bitcast(I32), in_=codes[:].bitcast(I32))
+
         def Pq(c, f):
-            cols = slice(CH * c, CH * c + CH)
             if f == 0:
                 p_codes[c] = tile([P, 2, CH], U32, "p_codes_%d" % c)
-            nc.vector.quantize_mx(out=p_codes[c][:, f, :].bitcast(FP8X4), scales=out_scales[:, f, cols], in_=p_bf[c, f][:].rearrange("p n t -> p (n t)"))
+            quantize(p_codes[c][:, f, :], out_scales[:, f, CH * c : CH * c + CH], p_bf[c, f][:].rearrange("p n t -> p (n t)"))
             if f == 1:
-                nc.sync.dma_start(out=out_1[:, :, cols, :].rearrange("f p n t -> p f (n t)").bitcast(I32), in_=p_codes[c][:].bitcast(I32))
+                store_codes(p_codes[c], CH * c, CH)
 
         def store_scales():
             for Q in range(4):
@@ -283,15 +320,16 @@ def tile_innerproductsigmoidresidualprojection_kernel(tc, z, y, adj, g, bj, v, r
             load_rows(z_raw, z, 3, "z")
             for c in range(2, NCH):
                 load_rows(a_raw, adj, c, "a")
-            Y(0,0,0); YRh(0,0,0); YRh(0,1,0); Y(0,1,0); YRh(0,2,0); YRh(0,3,0); Ye(0,0,0); YRi(0,0); YRi(0,1); Y(0,0,1); Y(0,1,1); Ye(0,1,0); YRh(0,0,1); YRh(0,1,1); Ye(0,0,1); Yq(0,0); YRh(0,2,1); YRh(0,3,1); Ye(0,1,1)
-            Z(0,0); Zc(0,0); Z(0,1); Zc(0,1); YRq(0,0); Yq(0,1); Z(1,0); Zc(1,0); Z(1,1); Zc(1,1); YRi(0,2); YRi(0,3)
-            Y(1,0,0); YRs(1,0); YRs(1,1); Zq(0,0); Ye(1,0,0); Y(1,0,1); Zq(0,1); Ye(1,0,1)
-            Y(1,1,0); Y(1,1,1); YRs(1,2); YRs(1,3); Ye(1,1,0); Ye(1,1,1)
-            S1(0,0,0); S1(0,0,1); S1(0,0,2); S1(0,0,3); Yq(1,0); Yq(1,1); YRq(0,1); YRi(1,0)
-            A(0,0); A(1,0); S1(0,1,0); Z(2,0); Zc(2,0); Z(2,1); Zc(2,1); S1(0,1,1); Z(3,0); Zc(3,0); Z(3,1); Zc(3,1); S1(0,1,2); S1(0,1,3); A(0,1); R(0,0); A(1,1); R(1,0); Mu(0,0); Mu(1,0); Zq(1,0); Zq(1,1); YRi(1,1,"V"); YRi(1,2); YRi(1,3)
-            R(0,1); R(1,1); YRq(1,0); Mu(0,1); YRq(1,1); Rq(0); S1(1,0,0); S1(1,0,1); S1(1,0,2); S1(1,0,3); A(2,0); Mu(1,1); S1(1,1,0); S1(1,1,1); S1(1,1,2); S1(1,1,3); A(2,1); R(2,0); Rq(1); R(2,1)
-            O(0,0,0); C(0,0,0,"PS"); Oe(0,0,0); O(0,0,1); C(0,0,1,"PS"); Oe(0,0,1); O(0,1,0); C(0,1,0,"PS"); Oe(0,1,0); O(0,1,1); C(0,1,1,"PS"); Oe(0,1,1); A(3,0); A(3,1); Mu(2,0); R(3,0); Mu(2,1); Mh(3,0,0); Rq(2); O(1,0,0); C(1,0,0,"PS"); Oe(1,0,0); O(1,0,1); Oe(1,0,1,"S"); Pt(0,0); Pt(0,1); O(1,1,0); C(1,1,0,"PS"); Oe(1,1,0); O(1,1,1); Oe(1,1,1,"S"); R(3,1)
-            Pc(0,0); Pc(0,1); Mh(3,0,1); Mh(3,1,0); C(1,0,1); C(1,1,1); O(2,0,0); Oe(2,0,0,"S"); O(2,0,1); Oe(2,0,1,"S"); Pt(1,0); O(2,1,0); Oe(2,1,0,"S"); O(2,1,1); Oe(2,1,1,"S"); Pt(1,1); Rh(3,0); Mh(3,1,1); Pq(0,0); Rh(3,1); Pq(0,1); Pc(1,0); Pc(1,1)
-            O(3,0,0); Oe(3,0,0,"S"); O(3,0,1); Oe(3,0,1,"S"); C(2,0,0,"V"); C(2,1,0,"V"); C(2,0,1,"V"); C(2,1,1,"V"); O(3,1,0); O(3,1,1); Pt(2,0); Pt(2,1); Pq(1,0); Pq(1,1); C(3,1,0,"PS"); C(3,0,0); Pt(3,0); C(3,1,1,"PS"); C(3,0,1); Pt(3,1); Oe(3,1,0)
-            Pc(2,0,"V"); Pc(2,1,"V"); Pc(3,0); Pc(3,1); Pq(2,0); Pq(2,1); Oe(3,1,1,"V"); Pq(3,0); Pq(3,1)
+            nc.scalar.copy(out=r_f32[:], in_=vecs["r"][:])
+            Y(0,0,0); YRh(0,0,0); YRh(0,1,0); Y(0,1,0); YRh(0,2,0); YRh(0,3,0); Ye(0,0,0); YRi(0,0,512); Y(0,0,1); Y(0,1,1); Ye(0,1,0); YRh(0,0,1); YRh(0,1,1); Ye(0,0,1); YRh(0,2,1); YRh(0,3,1); Ye(0,1,1)
+            Z(0,0); Zc(0,0); Z(0,1); Zc(0,1); YRq(0,0); Yq(0); Z(1,0); Zc(1,0); Z(1,1); Zc(1,1); YRi(0,512,512); Zq(0,0); Zq(0,1)
+            Y(1,0,0); YRs(1,0,"G"); YRs(1,1,"G"); Ye(1,0,0); Y(1,0,1); Ye(1,0,1)
+            Y(1,1,0); Y(1,1,1); Ye(1,1,0); Ye(1,1,1)
+            S1(0,0,0); S1(0,0,1); S1(0,0,2); S1(0,0,3); YRq(0,1); Yq(1); YRs(1,2); YRs(1,3); YRi(1,0,320,"G")
+            A(0,0); A(1,0); S1(0,1,0); Z(2,0); Zc(2,0); Z(2,1); Zc(2,1); S1(0,1,1); Z(3,0); Zc(3,0); Z(3,1); Zc(3,1); S1(0,1,2); S1(0,1,3); A(0,1); R(0,0); A(1,1); R(1,0); Mu(0,0); Mu(1,0); Zq(1); YRi(1,512,320,"G"); YRi(1,320,192); YRi(1,832,192)
+            R(0,1); R(1,1); Mu(0,1); YRq(1,0); Rq(0); S1(1,0,0); S1(1,0,1); S1(1,0,2); S1(1,0,3); A(2,0); Mu(1,1); YRq(1,1); S1(1,1,0); S1(1,1,1); S1(1,1,2); S1(1,1,3); A(2,1); R(2,0); Rq(1); R(2,1); Mu(2,0)
+            O(0,0,0); C(0,0,0,"PS"); Oe(0,0,0); O(0,0,1); C(0,0,1,"PS"); Oe(0,0,1); O(0,1,0); C(0,1,0,"PS"); Oe(0,1,0); O(0,1,1); C(0,1,1,"PS"); Oe(0,1,1); A(3,0); Mu(2,1); R(3,0); Rq(2); O(1,0,0); Oe(1,0,0,"S"); O(1,0,1); Oe(1,0,1,"S"); A(3,1); O(1,1,0); Oe(1,1,0,"S"); O(1,1,1); Oe(1,1,1,"S"); Pt(0,0); Pt(0,1); R(3,1)
+            Pc(0,0); Pc(0,1); Cw(1,0); Cw(1,1); Mh(3,0,0); Mh(3,1,0); Mh(3,0,1); O(2,0,0); Oe(2,0,0,"S"); O(2,0,1); Oe(2,0,1,"S"); O(2,1,0); Oe(2,1,0,"S"); O(2,1,1); Oe(2,1,1,"S"); Pt(1,0); Pt(1,1); Rh(3,0); Mh(3,1,1); Pq(0,0); Rh(3,1); Pq(0,1); Pc(1,0); Pc(1,1)
+            O(3,0,0); Oe(3,0,0,"S"); O(3,0,1); Oe(3,0,1,"S"); Cw(2,0); Cw(2,1); O(3,1,0); O(3,1,1); Pt(2,0); Pt(2,1); C(3,1,0,"PS"); C(3,1,1,"PS"); Pq(1,0); Pq(1,1); Cw(3,0); Pt(3,0)
+            Pc(2,0); Pt(3,1); Oe(3,1,0,"V"); Pc(2,1); Pc(3,0); Pc(3,1); Oe(3,1,1,"V"); Pq(2,0); Pq(2,1); Pq(3,0); Pq(3,1)
             store_scales()

@@ -62,7 +62,7 @@ def tile_innerproductsigmoidresidualprojection_kernel(tc, z, y, adj, g, bj, v, r
 
         y_raw, y_whole, z_raw, a_raw = {}, {}, {}, {}
         t_y, t_z, t_a, t_o, t_p = {}, {}, {}, {}, {}
-        z_bf, z_codes, z_scales, pr = {}, {}, {}, {}
+        z_bf, z_codes, z_scales, pr, diff = {}, {}, {}, {}, {}
         res_bf, res_mx, of, cast, p_bf, p_codes = {}, {}, {}, {}, {}, {}
 
         def y_pair(G, jp):
@@ -176,14 +176,14 @@ def tile_innerproductsigmoidresidualprojection_kernel(tc, z, y, adj, g, bj, v, r
             return pr[c // 2, G][:, :, CH * (c % 2) : CH * (c % 2) + CH]
 
         def R(c, G):
-            view = probs(c, G).rearrange("p (u e) n -> p u e n", u=2)
-            nc.vector.tensor_tensor(out=view, in0=view, in1=t_a[c, G][:].bitcast(BF16).rearrange("p (u n e) -> p u e n", u=2, e=2), op=ALU.subtract)
+            diff[c, G] = tile([P, 2, CH, 2], F32, "diff_%d" % (len(diff) % 2))
+            nc.vector.tensor_tensor(out=diff[c, G][:], in0=probs(c, G).rearrange("p (u e) n -> p u n e", u=2), in1=t_a[c, G][:].bitcast(BF16).rearrange("p (u n e) -> p u n e", u=2, e=2), op=ALU.subtract)
 
         def times_v(dst, src, G, width):
             nc.vector.tensor_tensor(
-                out=dst.rearrange("p (c i) t -> p c t i", i=4),
-                in0=src.rearrange("p t (c i) -> p c t i", i=4),
-                in1=vecs["v"][:, G, :].unsqueeze(1).unsqueeze(3).to_broadcast([P, width // 4, 4, 4]),
+                out=dst.rearrange("p n (u e) -> p n u e", u=2),
+                in0=src.rearrange("p u n e -> p n u e"),
+                in1=vecs["v"][:, G, :].unsqueeze(1).to_broadcast([P, width, 4]).rearrange("p n (u e) -> p n u e", u=2),
                 op=ALU.mult,
             )
 
@@ -196,27 +196,17 @@ def tile_innerproductsigmoidresidualprojection_kernel(tc, z, y, adj, g, bj, v, r
         def Mu(c, G):
             if G == 0:
                 res_bf[c] = tile([P, 2, CH, 4], BF16, "res_bf_%d" % (c % 2))
-            times_v(res_bf[c][:, G, :, :], probs(c, G), G, CH)
+            times_v(res_bf[c][:, G, :, :], diff[c, G][:], G, CH)
 
         def Rq(c):
             codes, scales = quantize_res(str(c), res_bf[c], CH)
             for i in range(2):
                 res_mx[c, i] = (codes[:, :, P * i : P * i + P], scales[:, :, P * i : P * i + P])
 
-        def Mw(G):
-            if G == 0:
-                res_bf["wide"] = tile([P, 2, 512, 4], BF16, "yg_bf_0")
-            times_v(res_bf["wide"][:, G, :, :], pr[0, G][:], G, 512)
-
-        def Rw():
-            codes, scales = quantize_res("wide", res_bf["wide"], 512)
-            for k in range(4):
-                res_mx[k // 2, k % 2] = (codes[:, :, P * k : P * k + P], scales[:, :, P * k : P * k + P])
-
         def Mh(c, G, i):
             if G == 0:
                 res_bf[c, i] = tile([P, 2, P, 4], BF16, "res_half_%d" % i)
-            times_v(res_bf[c, i][:, G, :, :], probs(c, G)[:, :, P * i : P * i + P], G, P)
+            times_v(res_bf[c, i][:, G, :, :], diff[c, G][:, :, P * i : P * i + P, :], G, P)
 
         def Rh(c, i):
             codes, scales = quantize_res("half_%d" % i, res_bf[c, i], P)
@@ -323,13 +313,13 @@ def tile_innerproductsigmoidresidualprojection_kernel(tc, z, y, adj, g, bj, v, r
             nc.scalar.copy(out=r_f32[:], in_=vecs["r"][:])
             Y(0,0,0); YRh(0,0,0); YRh(0,1,0); Y(0,1,0); YRh(0,2,0); YRh(0,3,0); Ye(0,0,0); YRi(0,0,512); Y(0,0,1); Y(0,1,1); Ye(0,1,0); YRh(0,0,1); YRh(0,1,1); Ye(0,0,1); YRh(0,2,1); YRh(0,3,1); Ye(0,1,1)
             Z(0,0); Zc(0,0); Z(0,1); Zc(0,1); YRq(0,0); Yq(0); Z(1,0); Zc(1,0); Z(1,1); Zc(1,1); YRi(0,512,512); Zq(0,0); Zq(0,1)
-            Y(1,0,0); YRs(1,0,"G"); YRs(1,1,"G"); Ye(1,0,0); Y(1,0,1); Ye(1,0,1)
+            Y(1,0,0); YRs(1,0,"G"); Ye(1,0,0); Y(1,0,1); Ye(1,0,1)
             Y(1,1,0); Y(1,1,1); Ye(1,1,0); Ye(1,1,1)
-            S1(0,0,0); S1(0,0,1); S1(0,0,2); S1(0,0,3); YRq(0,1); Yq(1); YRs(1,2); YRs(1,3); YRi(1,0,320,"G")
-            A(0,0); A(1,0); S1(0,1,0); Z(2,0); Zc(2,0); Z(2,1); Zc(2,1); S1(0,1,1); Z(3,0); Zc(3,0); Z(3,1); Zc(3,1); S1(0,1,2); S1(0,1,3); A(0,1); R(0,0); A(1,1); R(1,0); Mu(0,0); Mu(1,0); Zq(1); YRi(1,512,320,"G"); YRi(1,320,192); YRi(1,832,192)
+            S1(0,0,0); S1(0,0,1); S1(0,0,2); S1(0,0,3); YRq(0,1); Yq(1); YRs(1,1); YRs(1,2); YRs(1,3); YRi(1,0,256,"G")
+            A(0,0); A(1,0); S1(0,1,0); Z(2,0); Zc(2,0); Z(2,1); Zc(2,1); S1(0,1,1); Z(3,0); Zc(3,0); Z(3,1); Zc(3,1); S1(0,1,2); S1(0,1,3); A(0,1); R(0,0); A(1,1); R(1,0); Mu(0,0); Mu(1,0); Zq(1); YRi(1,512,256,"G"); YRi(1,256,256); YRi(1,768,256)
             R(0,1); R(1,1); Mu(0,1); YRq(1,0); Rq(0); S1(1,0,0); S1(1,0,1); S1(1,0,2); S1(1,0,3); A(2,0); Mu(1,1); YRq(1,1); S1(1,1,0); S1(1,1,1); S1(1,1,2); S1(1,1,3); A(2,1); R(2,0); Rq(1); R(2,1); Mu(2,0)
-            O(0,0,0); C(0,0,0,"PS"); Oe(0,0,0); O(0,0,1); C(0,0,1,"PS"); Oe(0,0,1); O(0,1,0); C(0,1,0,"PS"); Oe(0,1,0); O(0,1,1); C(0,1,1,"PS"); Oe(0,1,1); A(3,0); Mu(2,1); R(3,0); Rq(2); O(1,0,0); Oe(1,0,0,"S"); O(1,0,1); Oe(1,0,1,"S"); A(3,1); O(1,1,0); Oe(1,1,0,"S"); O(1,1,1); Oe(1,1,1,"S"); Pt(0,0); Pt(0,1); R(3,1)
-            Pc(0,0); Pc(0,1); Cw(1,0); Cw(1,1); Mh(3,0,0); Mh(3,1,0); Mh(3,0,1); O(2,0,0); Oe(2,0,0,"S"); O(2,0,1); Oe(2,0,1,"S"); O(2,1,0); Oe(2,1,0,"S"); O(2,1,1); Oe(2,1,1,"S"); Pt(1,0); Pt(1,1); Rh(3,0); Mh(3,1,1); Pq(0,0); Rh(3,1); Pq(0,1); Pc(1,0); Pc(1,1)
+            O(0,0,0); C(0,0,0,"PS"); Oe(0,0,0); O(0,0,1); C(0,0,1,"PS"); Oe(0,0,1); O(0,1,0); C(0,1,0,"PS"); Oe(0,1,0); O(0,1,1); C(0,1,1,"PS"); Oe(0,1,1); A(3,0); Mu(2,1); R(3,0); Rq(2); O(1,0,0); Oe(1,0,0,"S"); O(1,0,1); Oe(1,0,1,"S"); A(3,1); O(1,1,0); Oe(1,1,0,"S"); O(1,1,1); Oe(1,1,1,"S"); R(3,1)
+            O(2,0,0); Oe(2,0,0,"S"); O(2,0,1); Oe(2,0,1,"S"); Pt(0,0); Pt(0,1); Pc(0,0); Pc(0,1); Cw(1,0); Cw(1,1); Mh(3,0,0); Mh(3,1,0); Mh(3,0,1); O(2,1,0); Oe(2,1,0,"S"); O(2,1,1); Oe(2,1,1,"S"); Pt(1,0); Pt(1,1); Rh(3,0); Mh(3,1,1); Pq(0,0); Rh(3,1); Pq(0,1); Pc(1,0); Pc(1,1)
             O(3,0,0); Oe(3,0,0,"S"); O(3,0,1); Oe(3,0,1,"S"); Cw(2,0); Cw(2,1); O(3,1,0); O(3,1,1); Pt(2,0); Pt(2,1); C(3,1,0,"PS"); C(3,1,1,"PS"); Pq(1,0); Pq(1,1); Cw(3,0); Pt(3,0)
             Pc(2,0); Pt(3,1); Oe(3,1,0,"V"); Pc(2,1); Pc(3,0); Pc(3,1); Oe(3,1,1,"V"); Pq(2,0); Pq(2,1); Pq(3,0); Pq(3,1)
             store_scales()

@@ -16,76 +16,83 @@ ACT = mybir.ActivationFunctionType
 ALU = mybir.AluOpType
 
 P = 128
+HALF = 512
 CH = 256
-NCH = N // CH
-RING = 5
-ADJ_BANKS = 3
-SCALED_TAG = "turned_0"
-LAST_TAG = "turned_1"
+LAST = N // CH - 1
+INV_SQRT = 1.0 / 32.0
+RING_BANKS = 5
+SIDE_BANKS = 2
+GPSIMD_COLS = 384
 
 
 def tile_innerproductsigmoidresidualprojection_kernel(tc, z, y, adj, g, bj, v, r, out_0, out_1, out_2):
     nc = tc.nc
     with ExitStack() as ctx:
-        sb = ctx.enter_context(tc.tile_pool(name="sb", bufs=1))
+        sbuf = ctx.enter_context(tc.tile_pool(name="sbuf", bufs=1))
         psum = ctx.enter_context(tc.psum_pool(name="psum", bufs=1))
 
         def tile(shape, dtype, tag):
-            return sb.tile(shape, dtype, name=tag, tag=tag, align_bytes=64)
+            return sbuf.tile(shape, dtype, name=tag, tag=tag, align_bytes=64)
 
-        taken = []
+        ring_taken, side_taken = [], []
+
+        def next_bank(taken, name, count):
+            tag = "%s_%d" % (name, len(taken) % count)
+            taken.append(tag)
+            return psum.tile([P, HALF], F32, name=tag, tag=tag)
 
         def ring_bank():
-            tag = "ring_%d" % (len(taken) % RING)
-            taken.append(tag)
-            return psum.tile([P, 512], F32, name=tag, tag=tag)
-
-        side = []
+            return next_bank(ring_taken, "ring", RING_BANKS)
 
         def side_bank():
-            tag = "side_%d" % (len(side) % ADJ_BANKS)
-            side.append(tag)
-            return psum.tile([P, 512], F32, name=tag, tag=tag)
+            return next_bank(side_taken, "side", SIDE_BANKS)
+
+        def half(h):
+            return slice(HALF * h, HALF * h + HALF)
+
+        def chunk(c):
+            return slice(CH * c, CH * c + CH)
 
         vecs = {name: tile([P, 2, 4], BF16, "vec_" + name) for name in ("r", "g", "bj", "v")}
-        y_scaled_halves = [tile([P, 4, 512], BF16, "y_scaled_0%d" % f) for f in range(2)]
-        y_scaled_late, yr_bf = {}, {}
+        y_scaled_first = [tile([P, 4, HALF], BF16, "y_scaled_%d" % f) for f in range(2)]
         yr_codes = [tile([P, D], U32, "yr_codes_%d" % G) for G in range(2)]
         yr_scales = [tile([P, D], U8, "yr_scales_%d" % G) for G in range(2)]
-        yg_bf = [tile([P, 2, 512, 4], BF16, "yg_bf_%d" % G) for G in range(2)]
-        yg_codes = [tile([P, 2, 512], U32, "yg_codes_%d" % G) for G in range(2)]
-        yg_scales = [tile([P, 2, 512], U8, "yg_scales_%d" % G) for G in range(2)]
+        yg_bf = [tile([P, 2, HALF, 4], BF16, "yg_bf_%d" % G) for G in range(2)]
+        yg_codes = [tile([P, 2, HALF], U32, "yg_codes_%d" % G) for G in range(2)]
+        yg_scales = [tile([P, 2, HALF], U8, "yg_scales_%d" % G) for G in range(2)]
         out_scales = tile([P, 2, N], U8, "out_scales")
         ident = tile([P, P], F32, "ident")
         r_f32 = tile([P, 2, 4], F32, "r_f32")
-        warm = tile([P, 1], F32, "warm")
+        v_cols = tile([P, P], F32, "v_cols")
+        v_rows = tile([P, P], F32, "v_rows")
+        v_bank = psum.tile([P, HALF], F32, name="v_bank", tag="v_bank")
+        table_probe = tile([P, 1], F32, "table_probe")
 
-        y_raw, y_whole, z_raw, a_raw = {}, {}, {}, {}
-        t_y, t_z, t_a, t_o, t_p = {}, {}, {}, {}, {}
-        z_bf, z_codes, z_scales, pr, diff = {}, {}, {}, {}, {}
-        res_bf, res_mx, of, cast, p_bf, p_codes = {}, {}, {}, {}, {}, {}
-
-        def y_pair(G, jp):
-            return y[512 * G : 512 * G + 512, :].rearrange("(p j) d -> p j d", j=4)[:, 2 * jp : 2 * jp + 2, :]
-
-        def load_y(G, jp):
-            whole = tile([P, 2, D], BF16, "raw_y%d" % (2 * G + jp))
-            nc.sync.dma_start(out=whole[:], in_=y_pair(G, jp))
-            for f in range(2):
-                y_raw[G, jp, f] = whole[:, :, 512 * f : 512 * f + 512]
-            y_whole[G, jp] = whole
-
-        def load_y_half(G, jp, f):
-            half = tile([P, 2, 512], BF16, "raw_half%d" % (2 * jp + f))
-            nc.sync.dma_start(out=half[:], in_=y_pair(G, jp)[:, :, 512 * f : 512 * f + 512])
-            y_raw[G, jp, f] = half[:]
+        y_raw, y_second, z_raw, adj_raw = {}, {}, {}, {}
+        y_bank, z_bank, adj_bank, out_bank, plane_bank = {}, {}, {}, {}, {}
+        yr_bf, z_bf, z_codes, z_scales, prob, diff = {}, {}, {}, {}, {}, {}
+        res_bf, res_mx, out_f32, out_bf, plane_bf, plane_codes = {}, {}, {}, {}, {}, {}
 
         def load_vec(name, src, queue):
             queue.dma_start(out=vecs[name][:], in_=src.rearrange("(G p t) -> p G t", p=P, t=4))
 
-        def load_rows(dst, src, c, name):
-            dst[c] = tile([P, 2, D], BF16, "raw_%s%d" % (name, c))
-            nc.sync.dma_start(out=dst[c][:], in_=src[CH * c : CH * c + CH, :].rearrange("(p i) k -> p i k", i=2))
+        def y_slots(G, jp):
+            return y[half(G), :].rearrange("(p j) d -> p j d", j=4)[:, 2 * jp : 2 * jp + 2, :]
+
+        def load_y_first(jp, f):
+            raw = tile([P, 2, HALF], BF16, "raw_y_first_%d" % (2 * jp + f))
+            nc.sync.dma_start(out=raw[:], in_=y_slots(0, jp)[:, :, half(f)])
+            y_raw[0, jp, f] = raw[:]
+
+        def load_y_second(jp):
+            y_second[jp] = tile([P, 2, D], BF16, "raw_y_second_%d" % jp)
+            nc.sync.dma_start(out=y_second[jp][:], in_=y_slots(1, jp))
+            for f in range(2):
+                y_raw[1, jp, f] = y_second[jp][:, :, half(f)]
+
+        def load_rows(dst, src, name, c):
+            dst[c] = tile([P, 2, D], BF16, "raw_%s_%d" % (name, c))
+            nc.sync.dma_start(out=dst[c][:], in_=src[chunk(c), :].rearrange("(p i) k -> p i k", i=2))
 
         def turn(bank, rows):
             for i in range(2):
@@ -93,233 +100,348 @@ def tile_innerproductsigmoidresidualprojection_kernel(tc, z, y, adj, g, bj, v, r
                 for u in range(2):
                     nc.tensor.transpose(bank[:, CH * u + P * i : CH * u + P * i + P], words[:, u:256:2], ident[:])
 
-        def Y(G, jp, f):
-            t_y[G, jp, f] = side_bank() if G == 1 and (jp, f) != (1, 1) else ring_bank()
-            turn(t_y[G, jp, f], y_raw[G, jp, f])
-
-        def Ye(G, jp, f):
-            src = t_y[G, jp, f][:].bitcast(BF16).rearrange("p (u m e) -> p m u e", u=2, e=2)
-            dst = yg_bf[G][:, f, CH * jp : CH * jp + CH, :].rearrange("p m (u e) -> p m u e", u=2)
-            fac = vecs["g"][:, f, :].unsqueeze(1).to_broadcast([P, CH, 4]).rearrange("p m (u e) -> p m u e", u=2)
-            nc.vector.tensor_tensor(out=dst, in0=src, in1=fac, op=ALU.mult)
-
         def quantize(codes, scales, src):
             nc.vector.quantize_mx(out=codes.bitcast(FP8X4), scales=scales, in_=src)
 
         def quantize_pair(codes, scales, src):
             quantize(codes[:].rearrange("p a n -> p (a n)"), scales[:].rearrange("p a n -> p (a n)"), src[:].rearrange("p a n t -> p (a n t)"))
 
-        def Yq(G):
-            quantize_pair(yg_codes[G], yg_scales[G], yg_bf[G])
+        def gpsimd_scale(dst, src, factor):
+            nc.gpsimd.tensor_scalar(out=dst, in0=src, scalar1=factor, scalar2=0.0, op0=ALU.mult, op1=ALU.add)
 
-        def Z(c, f):
-            t_z[c, f] = ring_bank()
-            turn(t_z[c, f], z_raw[c][:, :, 512 * f : 512 * f + 512])
+        def mx_product(bank, lhs_codes, lhs_scales, rhs_codes, rhs_scales):
+            for k in range(2):
+                nc.tensor.matmul_mx(
+                    out=bank[:],
+                    lhsT=lhs_codes[k].bitcast(FP8X4),
+                    lhsT_scale=lhs_scales[k],
+                    rhs=rhs_codes[k].bitcast(FP8X4),
+                    rhs_scale=rhs_scales[k],
+                    start=(k == 0),
+                    stop=(k == 1),
+                )
 
-        def A(c, G):
-            t_a[c, G] = side_bank()
-            turn(t_a[c, G], a_raw[c][:, :, 512 * G : 512 * G + 512])
+        def turn_y(G, jp, f, bank):
+            y_bank[G, jp, f] = bank
+            turn(bank, y_raw[G, jp, f])
 
-        def Zc(c, f):
+        def times_g(G, jp, f):
+            src = y_bank[G, jp, f][:].bitcast(BF16).rearrange("p (u m e) -> p m u e", u=2, e=2)
+            dst = yg_bf[G][:, f, chunk(jp), :].rearrange("p m (u e) -> p m u e", u=2)
+            factor = vecs["g"][:, f, :].unsqueeze(1).to_broadcast([P, CH, 4]).rearrange("p m (u e) -> p m u e", u=2)
+            nc.vector.tensor_tensor(out=dst, in0=src, in1=factor, op=ALU.mult)
+
+        def turn_z(c):
             H, k = divmod(c, 2)
-            if H not in z_bf:
-                z_bf[H] = tile([P, 2, 512, 4], BF16, "turned_%d" % H)
-            dst = z_bf[H][:, f, CH * k : CH * k + CH, :].rearrange("p n t -> p (n t)").bitcast(F32).rearrange("p (n u) -> p n u", u=2)
-            nc.scalar.copy(out=dst, in_=t_z[c, f][:].rearrange("p (u n) -> p n u", u=2))
-
-        def Zq(H, f=None):
-            if H not in z_codes:
-                z_codes[H] = tile([P, 2, 512], U32, "z_codes_%d" % H)
-                z_scales[H] = tile([P, 2, 512], U8, "z_scales_%d" % H)
-            if f is None:
-                quantize_pair(z_codes[H], z_scales[H], z_bf[H])
-            else:
-                quantize(z_codes[H][:, f, :], z_scales[H][:, f, :], z_bf[H][:, f, :, :].rearrange("p n t -> p (n t)"))
-
-        def YRs(G, j, engine="V"):
-            if G not in y_scaled_late:
-                y_scaled_late[G] = tile([P, 4, D], BF16, SCALED_TAG)
-            dst, src = y_scaled_late[G][:, j, :], y_whole[G, j // 2][:, j % 2, :]
-            if engine == "V":
-                nc.vector.tensor_scalar_mul(dst, src, vecs["r"][:, G, j : j + 1])
-            else:
-                nc.gpsimd.tensor_scalar(out=dst, in0=src, scalar1=r_f32[:, G, j : j + 1], scalar2=0.0, op0=ALU.mult, op1=ALU.add)
-
-        def YRh(G, j, f):
-            nc.vector.tensor_scalar_mul(y_scaled_halves[f][:, j, :], y_raw[G, j // 2, f][:, j % 2, :], vecs["r"][:, G, j : j + 1])
-
-        def YRi(G, d0, width, engine="S"):
-            src = y_scaled_halves[d0 // 512][:, :, d0 % 512 : d0 % 512 + width] if G == 0 else y_scaled_late[G][:, :, d0 : d0 + width]
-            h, k0 = divmod(d0, 512)
-            if (G, h) not in yr_bf:
-                yr_bf[G, h] = tile([P, 512, 4], BF16, LAST_TAG if (G, h) == (1, 1) else "yr_bf_%d%d" % (G, h))
-            dst = yr_bf[G, h][:, k0 : k0 + width, :]
-            if engine == "S":
-                nc.scalar.copy(out=dst.rearrange("p (c i) t -> p c t i", i=4), in_=src.rearrange("p t (c i) -> p c t i", i=4))
-            else:
-                nc.gpsimd.tensor_scalar(out=dst, in0=src.rearrange("p t d -> p d t"), scalar1=1.0, scalar2=0.0, op0=ALU.mult, op1=ALU.add)
-
-        def YRq(G, h):
-            cols = slice(512 * h, 512 * h + 512)
-            quantize(yr_codes[G][:, cols], yr_scales[G][:, cols], yr_bf[G, h][:].rearrange("p d t -> p (d t)"))
-
-        def S1(H, G, t):
-            if t == 0:
-                pr[H, G] = tile([P, 4, 512], F32, "pr_%d" % (2 * H + G))
-            bank = ring_bank()
-            m0 = P * t
+            if k == 0:
+                z_bf[H] = tile([P, 2, HALF, 4], BF16, "z_bf_%d" % H)
             for f in range(2):
-                nc.tensor.matmul_mx(out=bank[:], lhsT=yg_codes[G][:, f, m0 : m0 + P].bitcast(FP8X4), lhsT_scale=yg_scales[G][:, f, m0 : m0 + P], rhs=z_codes[H][:, f, :].bitcast(FP8X4), rhs_scale=z_scales[H][:, f, :], start=(f == 0), stop=(f == 1))
-            nc.scalar.activation(out=pr[H, G][:, t, :], in_=bank[:], func=ACT.Sigmoid, bias=vecs["bj"][:, G, t : t + 1], scale=1.0 / 32.0)
+                z_bank[c, f] = ring_bank()
+                turn(z_bank[c, f], z_raw[c][:, :, half(f)])
+                dst = z_bf[H][:, f, chunk(k), :].rearrange("p n t -> p (n t)").bitcast(F32).rearrange("p (n u) -> p n u", u=2)
+                nc.scalar.copy(out=dst, in_=z_bank[c, f][:].rearrange("p (u n) -> p n u", u=2))
 
-        def probs(c, G):
-            return pr[c // 2, G][:, :, CH * (c % 2) : CH * (c % 2) + CH]
+        def new_z_planes(H):
+            z_codes[H] = tile([P, 2, HALF], U32, "z_codes_%d" % H)
+            z_scales[H] = tile([P, 2, HALF], U8, "z_scales_%d" % H)
 
-        def R(c, G):
+        def times_r_first(jp, f):
+            for j in range(2 * jp, 2 * jp + 2):
+                nc.vector.tensor_scalar_mul(y_scaled_first[f][:, j, :], y_raw[0, jp, f][:, j % 2, :], vecs["r"][:, 0, j : j + 1])
+
+        def interleave_scalar(dst, src):
+            nc.scalar.copy(out=dst.rearrange("p (c i) t -> p c t i", i=4), in_=src.rearrange("p t (c i) -> p c t i", i=4))
+
+        def interleave_gpsimd(dst, src):
+            gpsimd_scale(dst, src.rearrange("p t d -> p d t"), 1.0)
+
+        def quantize_yr(G, h):
+            quantize(yr_codes[G][:, half(h)], yr_scales[G][:, half(h)], yr_bf[G, h][:].rearrange("p d t -> p (d t)"))
+
+        def scores(H, G, t):
+            if t == 0:
+                prob[H, G] = tile([P, 4, HALF], F32, "prob_%d" % (2 * H + G))
+            bank = ring_bank()
+            cols = slice(P * t, P * t + P)
+            mx_product(
+                bank,
+                [yg_codes[G][:, f, cols] for f in range(2)],
+                [yg_scales[G][:, f, cols] for f in range(2)],
+                [z_codes[H][:, f, :] for f in range(2)],
+                [z_scales[H][:, f, :] for f in range(2)],
+            )
+            nc.scalar.activation(out=prob[H, G][:, t, :], in_=bank[:], func=ACT.Sigmoid, bias=vecs["bj"][:, G, t : t + 1], scale=INV_SQRT)
+
+        def turn_adj(c, G):
+            adj_bank[c, G] = side_bank()
+            turn(adj_bank[c, G], adj_raw[c][:, :, half(G)])
+
+        def minus_adj(c, G):
             diff[c, G] = tile([P, 2, CH, 2], F32, "diff_%d" % (len(diff) % 2))
-            nc.vector.tensor_tensor(out=diff[c, G][:], in0=probs(c, G).rearrange("p (u e) n -> p u n e", u=2), in1=t_a[c, G][:].bitcast(BF16).rearrange("p (u n e) -> p u n e", u=2, e=2), op=ALU.subtract)
+            nc.vector.tensor_tensor(
+                out=diff[c, G][:],
+                in0=prob[c // 2, G][:, :, chunk(c % 2)].rearrange("p (u e) n -> p u n e", u=2),
+                in1=adj_bank[c, G][:].bitcast(BF16).rearrange("p (u n e) -> p u n e", u=2, e=2),
+                op=ALU.subtract,
+            )
 
-        def times_v(dst, src, G, width):
+        def multiply_v(dst, src, G, width):
             nc.vector.tensor_tensor(
                 out=dst.rearrange("p n (u e) -> p n u e", u=2),
                 in0=src.rearrange("p u n e -> p n u e"),
-                in1=vecs["v"][:, G, :].unsqueeze(1).to_broadcast([P, width, 4]).rearrange("p n (u e) -> p n u e", u=2),
+                in1=v_bank[:, 4 * G : 4 * G + 4].unsqueeze(1).to_broadcast([P, width, 4]).rearrange("p n (u e) -> p n u e", u=2),
                 op=ALU.mult,
             )
 
-        def quantize_res(key, src, width):
-            codes = tile([P, 2, width], U32, "res_codes_%s" % key)
-            scales = tile([P, 2, width], U8, "res_scales_%s" % key)
-            quantize_pair(codes, scales, src)
-            return codes, scales
-
-        def Mu(c, G):
+        def times_v(c, G):
             if G == 0:
                 res_bf[c] = tile([P, 2, CH, 4], BF16, "res_bf_%d" % (c % 2))
-            times_v(res_bf[c][:, G, :, :], diff[c, G][:], G, CH)
+            multiply_v(res_bf[c][:, G, :, :], diff[c, G][:], G, CH)
 
-        def Rq(c):
-            codes, scales = quantize_res(str(c), res_bf[c], CH)
+        def quantize_res(c):
+            codes = tile([P, 2, CH], U32, "res_codes_%d" % c)
+            scales = tile([P, 2, CH], U8, "res_scales_%d" % c)
+            quantize_pair(codes, scales, res_bf[c])
             for i in range(2):
                 res_mx[c, i] = (codes[:, :, P * i : P * i + P], scales[:, :, P * i : P * i + P])
 
-        def Mh(c, G, i):
+        def times_v_last(G, i):
             if G == 0:
-                res_bf[c, i] = tile([P, 2, P, 4], BF16, "res_half_%d" % i)
-            times_v(res_bf[c, i][:, G, :, :], diff[c, G][:, :, P * i : P * i + P, :], G, P)
+                res_bf[LAST, i] = tile([P, 2, P, 4], BF16, "res_last_%d" % i)
+            multiply_v(res_bf[LAST, i][:, G, :, :], diff[LAST, G][:, :, P * i : P * i + P, :], G, P)
 
-        def Rh(c, i):
-            codes, scales = quantize_res("half_%d" % i, res_bf[c, i], P)
-            res_mx[c, i] = (codes[:], scales[:])
+        def quantize_res_last(i):
+            codes = tile([P, 2, P], U32, "res_codes_last_%d" % i)
+            scales = tile([P, 2, P], U8, "res_scales_last_%d" % i)
+            quantize_pair(codes, scales, res_bf[LAST, i])
+            res_mx[LAST, i] = (codes[:], scales[:])
 
-        def O(c, i, h):
-            bank = ring_bank()
-            t_o[c, i, h] = bank
+        def product(c, i, h):
+            out_bank[c, i, h] = ring_bank()
             codes, scales = res_mx[c, i]
-            for G in range(2):
-                nc.tensor.matmul_mx(out=bank[:], lhsT=codes[:, G, :].bitcast(FP8X4), lhsT_scale=scales[:, G, :], rhs=yr_codes[G][:, 512 * h : 512 * h + 512].bitcast(FP8X4), rhs_scale=yr_scales[G][:, 512 * h : 512 * h + 512], start=(G == 0), stop=(G == 1))
+            mx_product(
+                out_bank[c, i, h],
+                [codes[:, G, :] for G in range(2)],
+                [scales[:, G, :] for G in range(2)],
+                [yr_codes[G][:, half(h)] for G in range(2)],
+                [yr_scales[G][:, half(h)] for G in range(2)],
+            )
 
-        def Oe(c, i, h, engine="S"):
+        def copy_out(c, i, h):
             if h == 0:
-                of[c, i] = tile([P, D], F32, ("raw_z%d" % c) if i == 0 else ("raw_a%d" % c))
-            dst = of[c, i][:, 512 * h : 512 * h + 512]
-            if engine == "S":
-                nc.scalar.mul(dst, t_o[c, i, h][:], 1.0 / 32.0)
-            else:
-                nc.vector.tensor_scalar_mul(dst, t_o[c, i, h][:], 1.0 / 32.0)
-            rows = out_0[CH * c : CH * c + CH, :].rearrange("(p i) d -> p i d", i=2)[:, i, :]
-            if (c, i) == (NCH - 1, 1):
-                nc.sync.dma_start(out=rows[:, 512 * h : 512 * h + 512], in_=dst)
+                out_f32[c, i] = tile([P, D], F32, "raw_%s_%d" % (("z", "adj")[i], c))
+            dst = out_f32[c, i][:, half(h)]
+            nc.scalar.mul(dst, out_bank[c, i, h][:], INV_SQRT)
+            rows = out_0[chunk(c), :].rearrange("(p i) d -> p i d", i=2)[:, i, :]
+            if (c, i) == (LAST, 1):
+                nc.sync.dma_start(out=rows[:, half(h)], in_=dst)
             elif h == 1:
-                nc.sync.dma_start(out=rows, in_=of[c, i][:])
+                nc.sync.dma_start(out=rows, in_=out_f32[c, i][:])
 
-        def cast_tile(c, i):
-            if (c, i) not in cast:
-                cast[c, i] = tile([P, D], BF16, "cast_%d" % (2 * c + i))
-            return cast[c, i]
+        def row_block(c, i):
+            for h in range(2):
+                product(c, i, h)
+                copy_out(c, i, h)
 
-        def C(c, i, h, engine="V"):
-            dst = cast_tile(c, i)[:, 512 * h : 512 * h + 512].rearrange("p (u q e) -> p u q e", u=2, e=2)
-            if engine in ("PS", "PV"):
-                src = t_o[c, i, h][:].rearrange("p (q u e) -> p u q e", u=2, e=2)
-                if engine == "PS":
-                    nc.scalar.mul(dst, src, 1.0 / 32.0)
-                else:
-                    nc.vector.tensor_scalar_mul(dst, src, 1.0 / 32.0)
-                return
-            src = of[c, i][:, 512 * h : 512 * h + 512].rearrange("p (q u e) -> p u q e", u=2, e=2)
-            if engine == "V":
-                nc.vector.tensor_copy(out=dst, in_=src)
-            else:
-                nc.gpsimd.tensor_scalar(out=dst, in0=src, scalar1=1.0, scalar2=0.0, op0=ALU.mult, op1=ALU.add)
+        def new_out_bf(c, i, tag=None):
+            out_bf[c, i] = tile([P, D], BF16, tag or "out_bf_%d" % (2 * c + i))
+            return out_bf[c, i][:].rearrange("p (u q e) -> p u q e", u=2, e=2)
 
-        def Cw(c, i):
-            dst = cast_tile(c, i)[:].rearrange("p (h u q e) -> p h u q e", h=2, u=2, e=2)
-            nc.vector.tensor_copy(out=dst, in_=of[c, i][:].rearrange("p (h q u e) -> p h u q e", h=2, u=2, e=2))
+        def by_words(src):
+            return src.rearrange("p (q u e) -> p u q e", u=2, e=2)
 
-        def Pt(c, f):
-            bank = side_bank()
-            t_p[c, f] = bank
-            for i in range(2):
-                words = cast[c, i][:].bitcast(F32)
-                for u in range(2):
-                    w0 = CH * f + P * u
-                    nc.tensor.transpose(bank[:, CH * u + P * i : CH * u + P * i + P], words[:, w0 : w0 + P], ident[:])
+        def round_vector(c, i):
+            nc.vector.tensor_copy(out=new_out_bf(c, i), in_=by_words(out_f32[c, i][:]))
 
-        def Pc(c, f, engine="S"):
-            p_bf[c, f] = tile([P, CH, 4], BF16, "p_bf_%d" % (2 * (c % 2) + f))
-            dst = p_bf[c, f][:].rearrange("p n t -> p (n t)").bitcast(F32).rearrange("p (q i u) -> p q i u", i=2, u=2)
-            src = t_p[c, f][:].rearrange("p (u i q) -> p q i u", u=2, i=2)
-            if engine == "S":
-                nc.scalar.copy(out=dst, in_=src)
-            else:
-                nc.vector.tensor_copy(out=dst, in_=src)
+        def round_gpsimd(c, i, tag=None):
+            gpsimd_scale(new_out_bf(c, i, tag), by_words(out_f32[c, i][:]), 1.0)
 
-        def store_codes(codes, n0, width):
-            nc.sync.dma_start(out=out_1[:, :, n0 : n0 + width, :].rearrange("f p n t -> p f (n t)").bitcast(I32), in_=codes[:].bitcast(I32))
+        def round_from_psum(c, i, h):
+            if h == 0:
+                new_out_bf(c, i)
+            dst = out_bf[c, i][:].rearrange("p (u q e) -> p u q e", u=2, e=2)[:, :, P * h : P * h + P, :]
+            nc.scalar.mul(dst, by_words(out_bank[c, i, h][:]), INV_SQRT)
 
-        def Pq(c, f):
+        def turn_out(c, new_bank):
+            for f in range(2):
+                bank = new_bank()
+                plane_bank[c, f] = bank
+                for i in range(2):
+                    words = out_bf[c, i][:].bitcast(F32)
+                    for u in range(2):
+                        first = CH * u + P * f
+                        nc.tensor.transpose(bank[:, CH * u + P * i : CH * u + P * i + P], words[:, first : first + P], ident[:])
+
+        def copy_planes(c, copy):
+            for f in range(2):
+                plane_bf[c, f] = tile([P, CH, 4], BF16, "plane_bf_%d" % (2 * (c % 2) + f))
+                dst = plane_bf[c, f][:].rearrange("p n t -> p (n t)").bitcast(F32).rearrange("p (q i u) -> p q i u", i=2, u=2)
+                copy(out=dst, in_=plane_bank[c, f][:].rearrange("p (u i q) -> p q i u", u=2, i=2))
+
+        def quantize_plane(c, f):
             if f == 0:
-                p_codes[c] = tile([P, 2, CH], U32, "p_codes_%d" % c)
-            quantize(p_codes[c][:, f, :], out_scales[:, f, CH * c : CH * c + CH], p_bf[c, f][:].rearrange("p n t -> p (n t)"))
+                plane_codes[c] = tile([P, 2, CH], U32, "plane_codes_%d" % c)
+            quantize(plane_codes[c][:, f, :], out_scales[:, f, chunk(c)], plane_bf[c, f][:].rearrange("p n t -> p (n t)"))
             if f == 1:
-                store_codes(p_codes[c], CH * c, CH)
-
-        def store_scales():
-            for Q in range(4):
-                queue = nc.scalar if Q % 2 == 0 else nc.sync
-                queue.dma_start(out=out_2[:, 4 * Q : 4 * Q + 4, :].rearrange("f q n -> q f n").bitcast(I32), in_=out_scales[32 * Q : 32 * Q + 4, :, :].bitcast(I32))
+                nc.sync.dma_start(out=out_1[:, :, chunk(c), :].rearrange("f p n t -> p f (n t)").bitcast(I32), in_=plane_codes[c][:].bitcast(I32))
 
         with tc.manual_schedule():
             load_vec("r", r, nc.scalar)
             load_vec("g", g, nc.scalar)
             make_identity(nc, ident[:])
-            nc.scalar.activation(out=warm[:], in_=ident[:, 0:1], func=ACT.Sigmoid)
+            nc.gpsimd.memset(v_cols[:], 0.0)
+            nc.scalar.activation(out=table_probe[:], in_=ident[:, 0:1], func=ACT.Sigmoid)
+
             for f in range(2):
                 for jp in range(2):
-                    load_y_half(0, jp, f)
-            load_rows(z_raw, z, 0, "z")
-            load_rows(z_raw, z, 1, "z")
-            load_y(1, 0)
-            load_y(1, 1)
-            load_vec("bj", bj, nc.sync)
+                    load_y_first(jp, f)
             load_vec("v", v, nc.sync)
-            load_rows(a_raw, adj, 0, "a")
-            load_rows(a_raw, adj, 1, "a")
-            load_rows(z_raw, z, 2, "z")
-            load_rows(z_raw, z, 3, "z")
-            for c in range(2, NCH):
-                load_rows(a_raw, adj, c, "a")
+            for c in range(2):
+                load_rows(z_raw, z, "z", c)
+            for jp in range(2):
+                load_y_second(jp)
+            load_vec("bj", bj, nc.sync)
+            for c in range(2):
+                load_rows(adj_raw, adj, "adj", c)
+            for c in range(2, 4):
+                load_rows(z_raw, z, "z", c)
+            for c in range(2, 4):
+                load_rows(adj_raw, adj, "adj", c)
             nc.scalar.copy(out=r_f32[:], in_=vecs["r"][:])
-            Y(0,0,0); YRh(0,0,0); YRh(0,1,0); Y(0,1,0); YRh(0,2,0); YRh(0,3,0); Ye(0,0,0); YRi(0,0,512); Y(0,0,1); Y(0,1,1); Ye(0,1,0); YRh(0,0,1); YRh(0,1,1); Ye(0,0,1); YRh(0,2,1); YRh(0,3,1); Ye(0,1,1)
-            Z(0,0); Zc(0,0); Z(0,1); Zc(0,1); YRq(0,0); Yq(0); Z(1,0); Zc(1,0); Z(1,1); Zc(1,1); YRi(0,512,512); Zq(0,0); Zq(0,1)
-            Y(1,0,0); YRs(1,0,"G"); Ye(1,0,0); Y(1,0,1); Ye(1,0,1)
-            Y(1,1,0); Y(1,1,1); Ye(1,1,0); Ye(1,1,1)
-            S1(0,0,0); S1(0,0,1); S1(0,0,2); S1(0,0,3); YRq(0,1); Yq(1); YRs(1,1); YRs(1,2); YRs(1,3); YRi(1,0,256,"G")
-            A(0,0); A(1,0); S1(0,1,0); Z(2,0); Zc(2,0); Z(2,1); Zc(2,1); S1(0,1,1); Z(3,0); Zc(3,0); Z(3,1); Zc(3,1); S1(0,1,2); S1(0,1,3); A(0,1); R(0,0); A(1,1); R(1,0); Mu(0,0); Mu(1,0); Zq(1); YRi(1,512,256,"G"); YRi(1,256,256); YRi(1,768,256)
-            R(0,1); R(1,1); Mu(0,1); YRq(1,0); Rq(0); S1(1,0,0); S1(1,0,1); S1(1,0,2); S1(1,0,3); A(2,0); Mu(1,1); YRq(1,1); S1(1,1,0); S1(1,1,1); S1(1,1,2); S1(1,1,3); A(2,1); R(2,0); Rq(1); R(2,1); Mu(2,0)
-            O(0,0,0); C(0,0,0,"PS"); Oe(0,0,0); O(0,0,1); C(0,0,1,"PS"); Oe(0,0,1); O(0,1,0); C(0,1,0,"PS"); Oe(0,1,0); O(0,1,1); C(0,1,1,"PS"); Oe(0,1,1); A(3,0); Mu(2,1); R(3,0); Rq(2); O(1,0,0); Oe(1,0,0,"S"); O(1,0,1); Oe(1,0,1,"S"); A(3,1); O(1,1,0); Oe(1,1,0,"S"); O(1,1,1); Oe(1,1,1,"S"); R(3,1)
-            O(2,0,0); Oe(2,0,0,"S"); O(2,0,1); Oe(2,0,1,"S"); Pt(0,0); Pt(0,1); Pc(0,0); Pc(0,1); Cw(1,0); Cw(1,1); Mh(3,0,0); Mh(3,1,0); Mh(3,0,1); O(2,1,0); Oe(2,1,0,"S"); O(2,1,1); Oe(2,1,1,"S"); Pt(1,0); Pt(1,1); Rh(3,0); Mh(3,1,1); Pq(0,0); Rh(3,1); Pq(0,1); Pc(1,0); Pc(1,1)
-            O(3,0,0); Oe(3,0,0,"S"); O(3,0,1); Oe(3,0,1,"S"); Cw(2,0); Cw(2,1); O(3,1,0); O(3,1,1); Pt(2,0); Pt(2,1); C(3,1,0,"PS"); C(3,1,1,"PS"); Pq(1,0); Pq(1,1); Cw(3,0); Pt(3,0)
-            Pc(2,0); Pt(3,1); Oe(3,1,0,"V"); Pc(2,1); Pc(3,0); Pc(3,1); Oe(3,1,1,"V"); Pq(2,0); Pq(2,1); Pq(3,0); Pq(3,1)
-            store_scales()
+
+            for jp in range(2):
+                turn_y(0, jp, 0, ring_bank())
+                times_r_first(jp, 0)
+            times_g(0, 0, 0)
+            yr_bf[0, 0] = tile([P, HALF, 4], BF16, "yr_bf_0")
+            interleave_scalar(yr_bf[0, 0][:], y_scaled_first[0][:])
+            for jp in range(2):
+                turn_y(0, jp, 1, ring_bank())
+            times_g(0, 1, 0)
+            for jp in range(2):
+                times_r_first(jp, 1)
+                times_g(0, jp, 1)
+
+            turn_z(0)
+            quantize_yr(0, 0)
+            nc.vector.tensor_copy(out=v_cols[:, 0:8], in_=vecs["v"][:].rearrange("p G t -> p (G t)"))
+            quantize_pair(yg_codes[0], yg_scales[0], yg_bf[0])
+            turn_z(1)
+            bank = ring_bank()
+            nc.tensor.transpose(bank[:, 0:P], v_cols[:], ident[:])
+            nc.scalar.copy(out=v_rows[:], in_=bank[:, 0:P])
+            yr_bf[0, 1] = tile([P, HALF, 4], BF16, "yr_bf_1")
+            interleave_scalar(yr_bf[0, 1][:], y_scaled_first[1][:])
+            new_z_planes(0)
+            for f in range(2):
+                quantize(z_codes[0][:, f, :], z_scales[0][:, f, :], z_bf[0][:, f, :, :].rearrange("p n t -> p (n t)"))
+
+            y_scaled = tile([P, 4, D], BF16, "z_bf_0")
+            gpsimd_scale(y_scaled[:, 0, :], y_second[0][:, 0, :], r_f32[:, 1, 0:1])
+            for f in range(2):
+                turn_y(1, 0, f, side_bank())
+                times_g(1, 0, f)
+            for f in range(2):
+                turn_y(1, 1, f, ring_bank())
+            for f in range(2):
+                times_g(1, 1, f)
+            for t in range(4):
+                scores(0, 0, t)
+            quantize_yr(0, 1)
+            quantize_pair(yg_codes[1], yg_scales[1], yg_bf[1])
+            nc.scalar.activation(out=y_scaled[:, 1, :], in_=y_second[0][:, 1, :], func=ACT.Copy, scale=r_f32[:, 1, 1:2])
+            for j in range(2, 4):
+                nc.vector.tensor_scalar_mul(y_scaled[:, j, :], y_second[1][:, j % 2, :], vecs["r"][:, 1, j : j + 1])
+            yr_bf[1, 0] = tile([P, HALF, 4], BF16, "yr_bf_2")
+            interleave_gpsimd(yr_bf[1, 0][:], y_scaled[:, :, half(0)])
+
+            nc.tensor.transpose(v_bank[:, 0:P], v_rows[:], ident[:])
+            for c in range(2):
+                turn_adj(c, 0)
+            for k in range(2):
+                scores(0, 1, k)
+                turn_z(2 + k)
+            for t in range(2, 4):
+                scores(0, 1, t)
+            for c in range(2):
+                minus_adj(c, 0)
+                turn_adj(c, 1)
+            for c in range(2):
+                times_v(c, 0)
+            new_z_planes(1)
+            quantize_pair(z_codes[1], z_scales[1], z_bf[1])
+
+            yr_bf[1, 1] = tile([P, HALF, 4], BF16, "z_bf_1")
+            interleave_gpsimd(yr_bf[1, 1][:, 0:GPSIMD_COLS, :], y_scaled[:, :, HALF : HALF + GPSIMD_COLS])
+            interleave_scalar(yr_bf[1, 1][:, GPSIMD_COLS:HALF, :], y_scaled[:, :, HALF + GPSIMD_COLS : D])
+            for c in range(2):
+                minus_adj(c, 1)
+            times_v(0, 1)
+            quantize_yr(1, 0)
+            quantize_res(0)
+            times_v(1, 1)
+            quantize_yr(1, 1)
+            for G in range(2):
+                for t in range(4):
+                    scores(1, G, t)
+                turn_adj(2, G)
+
+            minus_adj(2, 0)
+            quantize_res(1)
+            minus_adj(2, 1)
+            for i in range(2):
+                row_block(0, i)
+                round_gpsimd(0, i)
+            turn_adj(LAST, 0)
+            for G in range(2):
+                times_v(2, G)
+            minus_adj(LAST, 0)
+            quantize_res(2)
+
+            row_block(1, 0)
+            for h in range(2):
+                product(1, 1, h)
+                round_from_psum(1, 1, h)
+                copy_out(1, 1, h)
+                if h == 0:
+                    turn_adj(LAST, 1)
+            round_gpsimd(1, 0, "res_bf_0")
+            minus_adj(LAST, 1)
+            turn_out(0, ring_bank)
+            copy_planes(0, nc.scalar.copy)
+            for i in range(2):
+                row_block(2, i)
+            turn_out(1, side_bank)
+            copy_planes(1, nc.scalar.copy)
+            for G in range(2):
+                times_v_last(G, 0)
+            times_v_last(0, 1)
+            quantize_res_last(0)
+            times_v_last(1, 1)
+            quantize_plane(0, 0)
+            quantize_res_last(1)
+            quantize_plane(0, 1)
+
+            for i in range(2):
+                round_vector(2, i)
+            row_block(LAST, 0)
+            for h in range(2):
+                product(LAST, 1, h)
+            turn_out(2, side_bank)
+            for h in range(2):
+                round_from_psum(LAST, 1, h)
+            for f in range(2):
+                quantize_plane(1, f)
+            round_vector(LAST, 0)
+            copy_planes(2, nc.vector.tensor_copy)
+            turn_out(LAST, ring_bank)
+            for h in range(2):
+                copy_out(LAST, 1, h)
+            copy_planes(LAST, nc.scalar.copy)
+            for c in range(2, 4):
+                for f in range(2):
+                    quantize_plane(c, f)
+
+            for Q in range(4):
+                queue = nc.scalar if Q % 2 == 0 else nc.sync
+                queue.dma_start(out=out_2[:, 4 * Q : 4 * Q + 4, :].rearrange("f q n -> q f n").bitcast(I32), in_=out_scales[32 * Q : 32 * Q + 4, :, :].bitcast(I32))

@@ -53,7 +53,7 @@ def tile_innerproductsigmoidresidualprojection_kernel(tc, z, y, adj, g, bj, v, r
         def chunk(c):
             return slice(CH * c, CH * c + CH)
 
-        vecs = {name: tile([P, 2, 4], BF16, "vec_" + name) for name in ("r", "g", "bj", "v")}
+        vecs = {name: tile([P, 2, 4], BF16, "vec_" + name) for name in ("r", "g", "bj")}
         y_scaled_first = [tile([P, 4, HALF], BF16, "y_scaled_%d" % f) for f in range(2)]
         yr_codes = [tile([P, D], U32, "yr_codes_%d" % G) for G in range(2)]
         yr_scales = [tile([P, D], U8, "yr_scales_%d" % G) for G in range(2)]
@@ -63,8 +63,7 @@ def tile_innerproductsigmoidresidualprojection_kernel(tc, z, y, adj, g, bj, v, r
         out_scales = tile([P, 2, N], U8, "out_scales")
         ident = tile([P, P], F32, "ident")
         r_f32 = tile([P, 2, 4], F32, "r_f32")
-        v_cols = tile([P, P], F32, "v_cols")
-        v_rows = tile([P, P], F32, "v_rows")
+        vec_rows = tile([P, HALF], BF16, "vec_rows")
         v_bank = psum.tile([P, HALF], F32, name="v_bank", tag="v_bank")
         table_probe = tile([P, 1], F32, "table_probe")
 
@@ -73,8 +72,14 @@ def tile_innerproductsigmoidresidualprojection_kernel(tc, z, y, adj, g, bj, v, r
         yr_bf, z_bf, z_codes, z_scales, prob, diff = {}, {}, {}, {}, {}, {}
         res_bf, res_mx, out_f32, out_bf, plane_bf, plane_codes = {}, {}, {}, {}, {}, {}
 
-        def load_vec(name, src, queue):
-            queue.dma_start(out=vecs[name][:], in_=src.rearrange("(G p t) -> p G t", p=P, t=4))
+        def load_vec(name, src):
+            nc.scalar.dma_start(out=vecs[name][:], in_=src.rearrange("(G p t) -> p G t", p=P, t=4))
+
+        def load_vec_rows(first, src):
+            nc.sync.dma_start(out=vec_rows[first : first + 2, :], in_=src.rearrange("(G k) -> G k", G=2))
+
+        def turned_vec(row):
+            return v_bank[:, 0 : 2 * P].bitcast(BF16).rearrange("p (u c e) -> p c u e", u=2, e=2)[:, row, :, :]
 
         def y_slots(G, jp):
             return y[half(G), :].rearrange("(p j) d -> p j d", j=4)[:, 2 * jp : 2 * jp + 2, :]
@@ -189,7 +194,7 @@ def tile_innerproductsigmoidresidualprojection_kernel(tc, z, y, adj, g, bj, v, r
             nc.vector.tensor_tensor(
                 out=dst.rearrange("p n (u e) -> p n u e", u=2),
                 in0=src.rearrange("p u n e -> p n u e"),
-                in1=v_bank[:, 4 * G : 4 * G + 4].unsqueeze(1).to_broadcast([P, width, 4]).rearrange("p n (u e) -> p n u e", u=2),
+                in1=turned_vec(G).unsqueeze(1).to_broadcast([P, width, 2, 2]),
                 op=ALU.mult,
             )
 
@@ -286,21 +291,21 @@ def tile_innerproductsigmoidresidualprojection_kernel(tc, z, y, adj, g, bj, v, r
                 nc.sync.dma_start(out=out_1[:, :, chunk(c), :].rearrange("f p n t -> p f (n t)").bitcast(I32), in_=plane_codes[c][:].bitcast(I32))
 
         with tc.manual_schedule():
-            load_vec("r", r, nc.scalar)
-            load_vec("g", g, nc.scalar)
+            load_vec("r", r)
+            load_vec("g", g)
+            nc.vector.memset(vec_rows[:], 0.0)
             make_identity(nc, ident[:])
-            nc.gpsimd.memset(v_cols[:], 0.0)
             nc.scalar.activation(out=table_probe[:], in_=ident[:, 0:1], func=ACT.Sigmoid)
 
             for f in range(2):
                 for jp in range(2):
                     load_y_first(jp, f)
-            load_vec("v", v, nc.sync)
+            load_vec_rows(0, v)
+            load_vec_rows(2, bj)
             for c in range(2):
                 load_rows(z_raw, z, "z", c)
             for jp in range(2):
                 load_y_second(jp)
-            load_vec("bj", bj, nc.sync)
             for c in range(2):
                 load_rows(adj_raw, adj, "adj", c)
             for c in range(2, 4):
@@ -322,14 +327,15 @@ def tile_innerproductsigmoidresidualprojection_kernel(tc, z, y, adj, g, bj, v, r
                 times_r_first(jp, 1)
                 times_g(0, jp, 1)
 
+            vec_words = vec_rows[:].bitcast(F32)
+            for u in range(2):
+                nc.tensor.transpose(v_bank[:, P * u : P * u + P], vec_words[:, u:256:2], ident[:])
+            nc.scalar.copy(out=vecs["bj"][:].rearrange("p G (u e) -> p G u e", u=2), in_=turned_vec(slice(2, 4)))
+
             turn_z(0)
             quantize_yr(0, 0)
-            nc.vector.tensor_copy(out=v_cols[:, 0:8], in_=vecs["v"][:].rearrange("p G t -> p (G t)"))
             quantize_pair(yg_codes[0], yg_scales[0], yg_bf[0])
             turn_z(1)
-            bank = ring_bank()
-            nc.tensor.transpose(bank[:, 0:P], v_cols[:], ident[:])
-            nc.scalar.copy(out=v_rows[:], in_=bank[:, 0:P])
             yr_bf[0, 1] = tile([P, HALF, 4], BF16, "yr_bf_1")
             interleave_scalar(yr_bf[0, 1][:], y_scaled_first[1][:])
             new_z_planes(0)
@@ -355,7 +361,6 @@ def tile_innerproductsigmoidresidualprojection_kernel(tc, z, y, adj, g, bj, v, r
             yr_bf[1, 0] = tile([P, HALF, 4], BF16, "yr_bf_2")
             interleave_gpsimd(yr_bf[1, 0][:], y_scaled[:, :, half(0)])
 
-            nc.tensor.transpose(v_bank[:, 0:P], v_rows[:], ident[:])
             for c in range(2):
                 turn_adj(c, 0)
             for k in range(2):
@@ -381,10 +386,12 @@ def tile_innerproductsigmoidresidualprojection_kernel(tc, z, y, adj, g, bj, v, r
             quantize_res(0)
             times_v(1, 1)
             quantize_yr(1, 1)
+            for t in range(4):
+                scores(1, 0, t)
             for G in range(2):
-                for t in range(4):
-                    scores(1, G, t)
                 turn_adj(2, G)
+            for t in range(4):
+                scores(1, 1, t)
 
             minus_adj(2, 0)
             quantize_res(1)

@@ -22,7 +22,9 @@ LAST = N // CH - 1
 INV_SQRT = 1.0 / 32.0
 RING_BANKS = 5
 SIDE_BANKS = 2
-GPSIMD_COLS = 384
+G1 = 320
+G2 = 352
+S1 = 256
 
 
 def tile_innerproductsigmoidresidualprojection_kernel(tc, z, y, adj, g, bj, v, r, out_0, out_1, out_2):
@@ -54,20 +56,18 @@ def tile_innerproductsigmoidresidualprojection_kernel(tc, z, y, adj, g, bj, v, r
             return slice(CH * c, CH * c + CH)
 
         vecs = {name: tile([P, 2, 4], BF16, "vec_" + name) for name in ("r", "g", "bj")}
-        y_scaled_first = [tile([P, 4, HALF], BF16, "y_scaled_%d" % f) for f in range(2)]
+        y_scaled = [tile([P, 4, D], BF16, "y_scaled_%d" % G) for G in range(2)]
         yr_codes = [tile([P, D], U32, "yr_codes_%d" % G) for G in range(2)]
         yr_scales = [tile([P, D], U8, "yr_scales_%d" % G) for G in range(2)]
-        yg_bf = [tile([P, 2, HALF, 4], BF16, "yg_bf_%d" % G) for G in range(2)]
         yg_codes = [tile([P, 2, HALF], U32, "yg_codes_%d" % G) for G in range(2)]
         yg_scales = [tile([P, 2, HALF], U8, "yg_scales_%d" % G) for G in range(2)]
         out_scales = tile([P, 2, N], U8, "out_scales")
         ident = tile([P, P], F32, "ident")
-        r_f32 = tile([P, 2, 4], F32, "r_f32")
         vec_rows = tile([P, HALF], BF16, "vec_rows")
         v_bank = psum.tile([P, HALF], F32, name="v_bank", tag="v_bank")
         table_probe = tile([P, 1], F32, "table_probe")
 
-        y_raw, y_second, z_raw, adj_raw = {}, {}, {}, {}
+        y_raw, adj_sorted, z_raw, adj_raw, yg_bf = {}, {}, {}, {}, {}
         y_bank, z_bank, adj_bank, out_bank, plane_bank = {}, {}, {}, {}, {}
         yr_bf, z_bf, z_codes, z_scales, prob, diff = {}, {}, {}, {}, {}, {}
         res_bf, res_mx, out_f32, out_bf, plane_bf, plane_codes = {}, {}, {}, {}, {}, {}
@@ -84,20 +84,16 @@ def tile_innerproductsigmoidresidualprojection_kernel(tc, z, y, adj, g, bj, v, r
         def y_slots(G, jp):
             return y[half(G), :].rearrange("(p j) d -> p j d", j=4)[:, 2 * jp : 2 * jp + 2, :]
 
-        def load_y_first(jp, f):
-            raw = tile([P, 2, HALF], BF16, "raw_y_first_%d" % (2 * jp + f))
-            nc.sync.dma_start(out=raw[:], in_=y_slots(0, jp)[:, :, half(f)])
-            y_raw[0, jp, f] = raw[:]
+        def load_y(G, jp):
+            y_raw[G, jp] = tile([P, 2, D], BF16, "raw_y_%d" % (2 * G + jp))
+            nc.sync.dma_start(out=y_raw[G, jp][:], in_=y_slots(G, jp))
 
-        def load_y_second(jp):
-            y_second[jp] = tile([P, 2, D], BF16, "raw_y_second_%d" % jp)
-            nc.sync.dma_start(out=y_second[jp][:], in_=y_slots(1, jp))
-            for f in range(2):
-                y_raw[1, jp, f] = y_second[jp][:, :, half(f)]
+        def slots(rows, c):
+            return rows[chunk(c), :].rearrange("(i p) k -> p i k" if c == LAST else "(p i) k -> p i k", i=2)
 
         def load_rows(dst, src, name, c):
             dst[c] = tile([P, 2, D], BF16, "raw_%s_%d" % (name, c))
-            nc.sync.dma_start(out=dst[c][:], in_=src[chunk(c), :].rearrange("(p i) k -> p i k", i=2))
+            nc.sync.dma_start(out=dst[c][:], in_=slots(src, c))
 
         def turn(bank, rows):
             for i in range(2):
@@ -117,7 +113,7 @@ def tile_innerproductsigmoidresidualprojection_kernel(tc, z, y, adj, g, bj, v, r
         def mx_product(bank, lhs_codes, lhs_scales, rhs_codes, rhs_scales):
             for k in range(2):
                 nc.tensor.matmul_mx(
-                    out=bank[:],
+                    out=bank,
                     lhsT=lhs_codes[k].bitcast(FP8X4),
                     lhsT_scale=lhs_scales[k],
                     rhs=rhs_codes[k].bitcast(FP8X4),
@@ -126,36 +122,53 @@ def tile_innerproductsigmoidresidualprojection_kernel(tc, z, y, adj, g, bj, v, r
                     stop=(k == 1),
                 )
 
-        def turn_y(G, jp, f, bank):
-            y_bank[G, jp, f] = bank
-            turn(bank, y_raw[G, jp, f])
+        def turn_y(G, jp, f):
+            y_bank[G, jp, f] = ring_bank()
+            turn(y_bank[G, jp, f], y_raw[G, jp][:, :, half(f)])
 
         def times_g(G, jp, f):
+            if (jp, f) == (0, 0):
+                yg_bf[G] = tile([P, 2, HALF, 4], BF16, "yg_bf")
             src = y_bank[G, jp, f][:].bitcast(BF16).rearrange("p (u m e) -> p m u e", u=2, e=2)
             dst = yg_bf[G][:, f, chunk(jp), :].rearrange("p m (u e) -> p m u e", u=2)
             factor = vecs["g"][:, f, :].unsqueeze(1).to_broadcast([P, CH, 4]).rearrange("p m (u e) -> p m u e", u=2)
             nc.vector.tensor_tensor(out=dst, in0=src, in1=factor, op=ALU.mult)
 
+        def quantize_yg(G):
+            quantize_pair(yg_codes[G], yg_scales[G], yg_bf[G])
+
+        def turn_z_half(c, f):
+            if f == 0:
+                z_bf[c] = tile([P, 2, CH, 4], BF16, "z_bf_%d" % c)
+            z_bank[c, f] = ring_bank()
+            turn(z_bank[c, f], z_raw[c][:, :, half(f)])
+
+        def copy_z(c, f):
+            dst = z_bf[c][:, f, :, :].rearrange("p n t -> p (n t)").bitcast(F32).rearrange("p (n u) -> p n u", u=2)
+            nc.scalar.copy(out=dst, in_=z_bank[c, f][:].rearrange("p (u n) -> p n u", u=2))
+
         def turn_z(c):
-            H, k = divmod(c, 2)
-            if k == 0:
-                z_bf[H] = tile([P, 2, HALF, 4], BF16, "z_bf_%d" % H)
             for f in range(2):
-                z_bank[c, f] = ring_bank()
-                turn(z_bank[c, f], z_raw[c][:, :, half(f)])
-                dst = z_bf[H][:, f, chunk(k), :].rearrange("p n t -> p (n t)").bitcast(F32).rearrange("p (n u) -> p n u", u=2)
-                nc.scalar.copy(out=dst, in_=z_bank[c, f][:].rearrange("p (u n) -> p n u", u=2))
+                turn_z_half(c, f)
+                copy_z(c, f)
 
-        def new_z_planes(H):
-            z_codes[H] = tile([P, 2, HALF], U32, "z_codes_%d" % H)
-            z_scales[H] = tile([P, 2, HALF], U8, "z_scales_%d" % H)
+        def quantize_z(c):
+            z_codes[c] = tile([P, 2, CH], U32, "z_codes_%d" % c)
+            z_scales[c] = tile([P, 2, CH], U8, "z_scales_%d" % c)
+            quantize_pair(z_codes[c], z_scales[c], z_bf[c])
 
-        def times_r_first(jp, f):
-            for j in range(2 * jp, 2 * jp + 2):
-                nc.vector.tensor_scalar_mul(y_scaled_first[f][:, j, :], y_raw[0, jp, f][:, j % 2, :], vecs["r"][:, 0, j : j + 1])
+        def times_r(G, j):
+            nc.vector.tensor_scalar_mul(y_scaled[G][:, j, :], y_raw[G, j // 2][:, j % 2, :], vecs["r"][:, G, j : j + 1])
 
         def interleave_scalar(dst, src):
             nc.scalar.copy(out=dst.rearrange("p (c i) t -> p c t i", i=4), in_=src.rearrange("p t (c i) -> p c t i", i=4))
+
+        def interleave_vector(dst, src):
+            nc.vector.tensor_copy(out=dst.rearrange("p (c i) t -> p c t i", i=4), in_=src.rearrange("p t (c i) -> p c t i", i=4))
+
+        def interleave(engine, G, first, last):
+            h, col = divmod(first, HALF)
+            engine(yr_bf[G, h][:, col : col + last - first, :], y_scaled[G][:, :, first:last])
 
         def interleave_gpsimd(dst, src):
             gpsimd_scale(dst, src.rearrange("p t d -> p d t"), 1.0)
@@ -163,30 +176,52 @@ def tile_innerproductsigmoidresidualprojection_kernel(tc, z, y, adj, g, bj, v, r
         def quantize_yr(G, h):
             quantize(yr_codes[G][:, half(h)], yr_scales[G][:, half(h)], yr_bf[G, h][:].rearrange("p d t -> p (d t)"))
 
-        def scores(H, G, t):
-            if t == 0:
-                prob[H, G] = tile([P, 4, HALF], F32, "prob_%d" % (2 * H + G))
-            bank = ring_bank()
-            cols = slice(P * t, P * t + P)
+        def sigmoid(dst, src, G, t):
+            nc.scalar.activation(out=dst, in_=src, func=ACT.Sigmoid, bias=vecs["bj"][:, G, t : t + 1], scale=INV_SQRT)
+
+        def score_product(out, G, t, codes, scales):
             mx_product(
-                bank,
-                [yg_codes[G][:, f, cols] for f in range(2)],
-                [yg_scales[G][:, f, cols] for f in range(2)],
-                [z_codes[H][:, f, :] for f in range(2)],
-                [z_scales[H][:, f, :] for f in range(2)],
+                out,
+                [yg_codes[G][:, f, P * t : P * t + P] for f in range(2)],
+                [yg_scales[G][:, f, P * t : P * t + P] for f in range(2)],
+                [codes[:, f, :] for f in range(2)],
+                [scales[:, f, :] for f in range(2)],
             )
-            nc.scalar.activation(out=prob[H, G][:, t, :], in_=bank[:], func=ACT.Sigmoid, bias=vecs["bj"][:, G, t : t + 1], scale=INV_SQRT)
+
+        def scores(c, G, tp):
+            if tp == 0:
+                prob[c, G] = tile([P, 4, CH], F32, "prob_%d_%d" % (c, G))[:]
+            bank = ring_bank()
+            for e in range(2):
+                score_product(bank[:, chunk(e)], G, 2 * tp + e, z_codes[c], z_scales[c])
+            for e in range(2):
+                sigmoid(prob[c, G][:, 2 * tp + e, :], bank[:, chunk(e)], G, 2 * tp + e)
 
         def turn_adj(c, G):
             adj_bank[c, G] = side_bank()
             turn(adj_bank[c, G], adj_raw[c][:, :, half(G)])
 
-        def minus_adj(c, G):
-            diff[c, G] = tile([P, 2, CH, 2], F32, "diff_%d" % (len(diff) % 2))
+        def sort_adj(c, tag):
+            adj_sorted[c] = tile([P, 2, 4 * P, 2], BF16, tag)
+            gpsimd_scale(adj_sorted[c][:], adj_raw[c][:].rearrange("p i (w u e) -> p u (i w) e", u=2, e=2), 1.0)
+
+        def turn_sorted_adj(c, G):
+            adj_bank[c, G] = side_bank()
+            for i in range(2):
+                for u in range(2):
+                    words = adj_sorted[c][:, u, block(2 * i + G), :].rearrange("p q e -> p (q e)").bitcast(F32)
+                    nc.tensor.transpose(adj_bank[c, G][:, CH * u + P * i : CH * u + P * i + P], words, ident[:])
+
+        def block(i):
+            return slice(P * i, P * i + P)
+
+        def minus_adj(c, G, cols=slice(0, CH)):
+            if cols.start == 0:
+                diff[c, G] = tile([P, 2, CH, 2], F32, "diff_%d" % G)
             nc.vector.tensor_tensor(
-                out=diff[c, G][:],
-                in0=prob[c // 2, G][:, :, chunk(c % 2)].rearrange("p (u e) n -> p u n e", u=2),
-                in1=adj_bank[c, G][:].bitcast(BF16).rearrange("p (u n e) -> p u n e", u=2, e=2),
+                out=diff[c, G][:, :, cols, :],
+                in0=prob[c, G].rearrange("p (u e) n -> p u n e", u=2)[:, :, cols, :],
+                in1=adj_bank[c, G][:].bitcast(BF16).rearrange("p (u n e) -> p u n e", u=2, e=2)[:, :, cols, :],
                 op=ALU.subtract,
             )
 
@@ -198,17 +233,18 @@ def tile_innerproductsigmoidresidualprojection_kernel(tc, z, y, adj, g, bj, v, r
                 op=ALU.mult,
             )
 
-        def times_v(c, G):
-            if G == 0:
+        def times_v(c, G, cols=slice(0, CH)):
+            if G == 0 and cols.start == 0:
                 res_bf[c] = tile([P, 2, CH, 4], BF16, "res_bf_%d" % (c % 2))
-            multiply_v(res_bf[c][:, G, :, :], diff[c, G][:], G, CH)
+            multiply_v(res_bf[c][:, G, cols, :], diff[c, G][:, :, cols, :], G, cols.stop - cols.start)
 
         def quantize_res(c):
             codes = tile([P, 2, CH], U32, "res_codes_%d" % c)
             scales = tile([P, 2, CH], U8, "res_scales_%d" % c)
-            quantize_pair(codes, scales, res_bf[c])
+            for G in range(2):
+                quantize(codes[:, G, :], scales[:, G, :], res_bf[c][:, G, :, :].rearrange("p n t -> p (n t)"))
             for i in range(2):
-                res_mx[c, i] = (codes[:, :, P * i : P * i + P], scales[:, :, P * i : P * i + P])
+                res_mx[c, i] = (codes[:, :, block(i)], scales[:, :, block(i)])
 
         def times_v_last(G, i):
             if G == 0:
@@ -225,19 +261,19 @@ def tile_innerproductsigmoidresidualprojection_kernel(tc, z, y, adj, g, bj, v, r
             out_bank[c, i, h] = ring_bank()
             codes, scales = res_mx[c, i]
             mx_product(
-                out_bank[c, i, h],
+                out_bank[c, i, h][:],
                 [codes[:, G, :] for G in range(2)],
                 [scales[:, G, :] for G in range(2)],
                 [yr_codes[G][:, half(h)] for G in range(2)],
                 [yr_scales[G][:, half(h)] for G in range(2)],
             )
 
-        def copy_out(c, i, h):
+        def copy_out(c, i, h, scale=nc.scalar.mul):
             if h == 0:
                 out_f32[c, i] = tile([P, D], F32, "raw_%s_%d" % (("z", "adj")[i], c))
             dst = out_f32[c, i][:, half(h)]
-            nc.scalar.mul(dst, out_bank[c, i, h][:], INV_SQRT)
-            rows = out_0[chunk(c), :].rearrange("(p i) d -> p i d", i=2)[:, i, :]
+            scale(dst, out_bank[c, i, h][:], INV_SQRT)
+            rows = slots(out_0, c)[:, i, :]
             if (c, i) == (LAST, 1):
                 nc.sync.dma_start(out=rows[:, half(h)], in_=dst)
             elif h == 1:
@@ -261,27 +297,52 @@ def tile_innerproductsigmoidresidualprojection_kernel(tc, z, y, adj, g, bj, v, r
         def round_gpsimd(c, i, tag=None):
             gpsimd_scale(new_out_bf(c, i, tag), by_words(out_f32[c, i][:]), 1.0)
 
-        def round_from_psum(c, i, h):
+        def round_from_psum(c, i, h, engine="scalar"):
             if h == 0:
                 new_out_bf(c, i)
             dst = out_bf[c, i][:].rearrange("p (u q e) -> p u q e", u=2, e=2)[:, :, P * h : P * h + P, :]
-            nc.scalar.mul(dst, by_words(out_bank[c, i, h][:]), INV_SQRT)
+            if engine == "scalar":
+                nc.scalar.mul(dst, by_words(out_bank[c, i, h][:]), INV_SQRT)
+            else:
+                nc.vector.tensor_scalar_mul(dst, by_words(out_bank[c, i, h][:]), INV_SQRT)
+
+        def turn_out_block(c, i, new_bank):
+            words = out_bf[c, i][:].bitcast(F32)
+            for f in range(2):
+                if i == 0:
+                    plane_bank[c, f] = new_bank()
+                for u in range(2):
+                    first = CH * u + P * f
+                    nc.tensor.transpose(plane_bank[c, f][:, CH * u + P * i : CH * u + P * i + P], words[:, first : first + P], ident[:])
 
         def turn_out(c, new_bank):
-            for f in range(2):
-                bank = new_bank()
-                plane_bank[c, f] = bank
-                for i in range(2):
-                    words = out_bf[c, i][:].bitcast(F32)
-                    for u in range(2):
-                        first = CH * u + P * f
-                        nc.tensor.transpose(bank[:, CH * u + P * i : CH * u + P * i + P], words[:, first : first + P], ident[:])
+            for i in range(2):
+                turn_out_block(c, i, new_bank)
 
-        def copy_planes(c, copy):
-            for f in range(2):
-                plane_bf[c, f] = tile([P, CH, 4], BF16, "plane_bf_%d" % (2 * (c % 2) + f))
-                dst = plane_bf[c, f][:].rearrange("p n t -> p (n t)").bitcast(F32).rearrange("p (q i u) -> p q i u", i=2, u=2)
-                copy(out=dst, in_=plane_bank[c, f][:].rearrange("p (u i q) -> p q i u", u=2, i=2))
+        def copy_plane(c, f, copy):
+            plane_bf[c, f] = tile([P, CH, 4], BF16, "plane_bf_%d" % (2 * (c % 2) + f))
+            dst = plane_bf[c, f][:].rearrange("p n t -> p (n t)").bitcast(F32).rearrange("p (q i u) -> p q i u", i=2, u=2)
+            copy(out=dst, in_=plane_bank[c, f][:].rearrange("p (u i q) -> p q i u", u=2, i=2))
+
+        def turn_out_last(i, f, bank):
+            plane_bank[LAST, i, f] = bank
+            words = out_bf[LAST, i][:].bitcast(F32)
+            for u in range(2):
+                first = CH * u + P * f
+                nc.tensor.transpose(bank[:, P * u : P * u + P], words[:, first : first + P], ident[:])
+
+        def copy_plane_last(i, f, copy):
+            plane_bf[LAST, i, f] = tile([P, P, 4], BF16, "plane_last_%d" % (2 * i + f))
+            dst = plane_bf[LAST, i, f][:].rearrange("p n t -> p (n t)").bitcast(F32).rearrange("p (n u) -> p n u", u=2)
+            copy(out=dst, in_=plane_bank[LAST, i, f][:, 0:CH].rearrange("p (u n) -> p n u", u=2))
+
+        def quantize_plane_last(i, f):
+            if f == 0:
+                plane_codes[LAST, i] = tile([P, 2, P], U32, "plane_codes_last_%d" % i)
+            rows = slice(CH * LAST + P * i, CH * LAST + P * i + P)
+            quantize(plane_codes[LAST, i][:, f, :], out_scales[:, f, rows], plane_bf[LAST, i, f][:].rearrange("p n t -> p (n t)"))
+            if f == 1:
+                nc.sync.dma_start(out=out_1[:, :, rows, :].rearrange("f p n t -> p f (n t)").bitcast(I32), in_=plane_codes[LAST, i][:].bitcast(I32))
 
         def quantize_plane(c, f):
             if f == 0:
@@ -297,157 +358,171 @@ def tile_innerproductsigmoidresidualprojection_kernel(tc, z, y, adj, g, bj, v, r
             make_identity(nc, ident[:])
             nc.scalar.activation(out=table_probe[:], in_=ident[:, 0:1], func=ACT.Sigmoid)
 
-            for f in range(2):
-                for jp in range(2):
-                    load_y_first(jp, f)
+            for jp in range(2):
+                load_y(0, jp)
+            load_rows(z_raw, z, "z", 0)
             load_vec_rows(0, v)
             load_vec_rows(2, bj)
-            for c in range(2):
-                load_rows(z_raw, z, "z", c)
             for jp in range(2):
-                load_y_second(jp)
-            for c in range(2):
-                load_rows(adj_raw, adj, "adj", c)
-            for c in range(2, 4):
+                load_y(1, jp)
+            load_rows(adj_raw, adj, "adj", 0)
+            for c in range(1, 4):
                 load_rows(z_raw, z, "z", c)
-            for c in range(2, 4):
-                load_rows(adj_raw, adj, "adj", c)
-            nc.scalar.copy(out=r_f32[:], in_=vecs["r"][:])
+                if c > 1:
+                    load_rows(adj_raw, adj, "adj", c - 1)
+            load_rows(adj_raw, adj, "adj", LAST)
 
+            for h in range(2):
+                yr_bf[0, h] = tile([P, HALF, 4], BF16, "yr_bf_%d" % h)
             for jp in range(2):
-                turn_y(0, jp, 0, ring_bank())
-                times_r_first(jp, 0)
+                for f in range(2):
+                    turn_y(0, jp, f)
+            for j in range(2):
+                times_r(0, j)
             times_g(0, 0, 0)
-            yr_bf[0, 0] = tile([P, HALF, 4], BF16, "yr_bf_0")
-            interleave_scalar(yr_bf[0, 0][:], y_scaled_first[0][:])
-            for jp in range(2):
-                turn_y(0, jp, 1, ring_bank())
-            times_g(0, 1, 0)
-            for jp in range(2):
-                times_r_first(jp, 1)
-                times_g(0, jp, 1)
-
+            for j in range(2, 4):
+                times_r(0, j)
+            interleave(interleave_scalar, 0, 0, S1)
+            times_g(0, 0, 1)
+            for f in range(2):
+                times_g(0, 1, f)
+            turn_z(0)
             vec_words = vec_rows[:].bitcast(F32)
             for u in range(2):
                 nc.tensor.transpose(v_bank[:, P * u : P * u + P], vec_words[:, u:256:2], ident[:])
             nc.scalar.copy(out=vecs["bj"][:].rearrange("p G (u e) -> p G u e", u=2), in_=turned_vec(slice(2, 4)))
+            interleave(interleave_scalar, 0, S1, HALF)
+            interleave(interleave_scalar, 0, HALF, D)
 
-            turn_z(0)
-            quantize_yr(0, 0)
-            quantize_pair(yg_codes[0], yg_scales[0], yg_bf[0])
-            turn_z(1)
-            yr_bf[0, 1] = tile([P, HALF, 4], BF16, "yr_bf_1")
-            interleave_scalar(yr_bf[0, 1][:], y_scaled_first[1][:])
-            new_z_planes(0)
-            for f in range(2):
-                quantize(z_codes[0][:, f, :], z_scales[0][:, f, :], z_bf[0][:, f, :, :].rearrange("p n t -> p (n t)"))
-
-            y_scaled = tile([P, 4, D], BF16, "z_bf_0")
-            gpsimd_scale(y_scaled[:, 0, :], y_second[0][:, 0, :], r_f32[:, 1, 0:1])
-            for f in range(2):
-                turn_y(1, 0, f, side_bank())
-                times_g(1, 0, f)
-            for f in range(2):
-                turn_y(1, 1, f, ring_bank())
-            for f in range(2):
-                times_g(1, 1, f)
-            for t in range(4):
-                scores(0, 0, t)
-            quantize_yr(0, 1)
-            quantize_pair(yg_codes[1], yg_scales[1], yg_bf[1])
-            nc.scalar.activation(out=y_scaled[:, 1, :], in_=y_second[0][:, 1, :], func=ACT.Copy, scale=r_f32[:, 1, 1:2])
+            for jp in range(2):
+                for f in range(2):
+                    turn_y(1, jp, f)
+            times_r(1, 0)
+            quantize_yg(0)
+            times_r(1, 1)
+            quantize_z(0)
             for j in range(2, 4):
-                nc.vector.tensor_scalar_mul(y_scaled[:, j, :], y_second[1][:, j % 2, :], vecs["r"][:, 1, j : j + 1])
+                times_r(1, j)
             yr_bf[1, 0] = tile([P, HALF, 4], BF16, "yr_bf_2")
-            interleave_gpsimd(yr_bf[1, 0][:], y_scaled[:, :, half(0)])
+            interleave(interleave_gpsimd, 1, 0, G1)
+            for jp in range(2):
+                for f in range(2):
+                    times_g(1, jp, f)
+            scores(0, 0, 0)
+            for G in range(2):
+                turn_adj(0, G)
+            interleave(interleave_scalar, 1, G1, HALF)
+            scores(0, 0, 1)
+            quantize_yr(0, 0)
+            quantize_yg(1)
+            turn_z(1)
+            for tp in range(2):
+                scores(0, 1, tp)
 
-            for c in range(2):
-                turn_adj(c, 0)
-            for k in range(2):
-                scores(0, 1, k)
-                turn_z(2 + k)
-            for t in range(2, 4):
-                scores(0, 1, t)
-            for c in range(2):
-                minus_adj(c, 0)
-                turn_adj(c, 1)
-            for c in range(2):
-                times_v(c, 0)
-            new_z_planes(1)
-            quantize_pair(z_codes[1], z_scales[1], z_bf[1])
-
+            quantize_yr(0, 1)
+            minus_adj(0, 0)
+            quantize_z(1)
             yr_bf[1, 1] = tile([P, HALF, 4], BF16, "z_bf_1")
-            interleave_gpsimd(yr_bf[1, 1][:, 0:GPSIMD_COLS, :], y_scaled[:, :, HALF : HALF + GPSIMD_COLS])
-            interleave_scalar(yr_bf[1, 1][:, GPSIMD_COLS:HALF, :], y_scaled[:, :, HALF + GPSIMD_COLS : D])
-            for c in range(2):
-                minus_adj(c, 1)
+            interleave(interleave_gpsimd, 1, HALF, HALF + G2)
+            times_v(0, 0)
+            minus_adj(0, 1)
+            turn_z(2)
+            quantize_z(2)
             times_v(0, 1)
+            for G in range(2):
+                for tp in range(2):
+                    scores(1, G, tp)
+            interleave(interleave_scalar, 1, HALF + G2, D)
+            for G in range(2):
+                turn_adj(1, G)
             quantize_yr(1, 0)
             quantize_res(0)
-            times_v(1, 1)
             quantize_yr(1, 1)
-            for t in range(4):
-                scores(1, 0, t)
-            for G in range(2):
-                turn_adj(2, G)
-            for t in range(4):
-                scores(1, 1, t)
+            sort_adj(2, "z_bf_1")
+            for tp in range(2):
+                scores(2, 0, tp)
 
-            minus_adj(2, 0)
+            for G in range(2):
+                minus_adj(1, G)
+            for G in range(2):
+                times_v(1, G)
+            row_block(0, 0)
+            round_gpsimd(0, 0)
+            row_block(0, 1)
+            turn_z(LAST)
+            for tp in range(2):
+                scores(2, 1, tp)
+            for G in range(2):
+                turn_sorted_adj(2, G)
+            quantize_z(LAST)
             quantize_res(1)
-            minus_adj(2, 1)
-            for i in range(2):
-                row_block(0, i)
-                round_gpsimd(0, i)
-            turn_adj(LAST, 0)
+            sort_adj(LAST, "res_bf_1")
+            round_gpsimd(0, 1)
+            for tp in range(2):
+                scores(LAST, 0, tp)
+
+            for G in range(2):
+                minus_adj(2, G)
             for G in range(2):
                 times_v(2, G)
-            minus_adj(LAST, 0)
-            quantize_res(2)
-
-            row_block(1, 0)
-            for h in range(2):
-                product(1, 1, h)
-                round_from_psum(1, 1, h)
-                copy_out(1, 1, h)
-                if h == 0:
-                    turn_adj(LAST, 1)
-            round_gpsimd(1, 0, "res_bf_0")
-            minus_adj(LAST, 1)
-            turn_out(0, ring_bank)
-            copy_planes(0, nc.scalar.copy)
             for i in range(2):
-                row_block(2, i)
-            turn_out(1, side_bank)
-            copy_planes(1, nc.scalar.copy)
+                row_block(1, i)
+            for tp in range(2):
+                scores(LAST, 1, tp)
+            for G in range(2):
+                turn_sorted_adj(LAST, G)
+            turn_out(0, ring_bank)
+            for f in range(2):
+                copy_plane(0, f, nc.scalar.copy)
+            quantize_res(2)
+            round_gpsimd(1, 0, "res_bf_0")
+            round_gpsimd(1, 1)
+
+            for G in range(2):
+                minus_adj(LAST, G, block(0))
             for G in range(2):
                 times_v_last(G, 0)
-            times_v_last(0, 1)
+            minus_adj(LAST, 0, block(1))
             quantize_res_last(0)
-            times_v_last(1, 1)
+            row_block(2, 0)
+            round_gpsimd(2, 0, "res_last_0")
+            row_block(2, 1)
+            turn_out(1, ring_bank)
+            for f in range(2):
+                copy_plane(1, f, nc.scalar.copy)
+            minus_adj(LAST, 1, block(1))
+            for G in range(2):
+                times_v_last(G, 1)
             quantize_plane(0, 0)
             quantize_res_last(1)
             quantize_plane(0, 1)
-
-            for i in range(2):
-                round_vector(2, i)
             row_block(LAST, 0)
-            for h in range(2):
-                product(LAST, 1, h)
-            turn_out(2, side_bank)
-            for h in range(2):
-                round_from_psum(LAST, 1, h)
+            round_vector(2, 1)
             for f in range(2):
                 quantize_plane(1, f)
-            round_vector(LAST, 0)
-            copy_planes(2, nc.vector.tensor_copy)
-            turn_out(LAST, ring_bank)
+            turn_out_block(2, 0, side_bank)
             for h in range(2):
-                copy_out(LAST, 1, h)
-            copy_planes(LAST, nc.scalar.copy)
-            for c in range(2, 4):
+                product(LAST, 1, h)
+            turn_out_block(2, 1, side_bank)
+            round_vector(LAST, 0)
+            round_from_psum(LAST, 1, 0)
+            copy_out(LAST, 1, 0)
+            round_from_psum(LAST, 1, 1, "vector")
+            for i in range(2):
                 for f in range(2):
-                    quantize_plane(c, f)
+                    turn_out_last(i, f, ring_bank())
+            copy_plane(2, 0, nc.scalar.copy)
+            copy_out(LAST, 1, 1)
+            copy_plane(2, 1, nc.vector.tensor_copy)
+            for f in range(2):
+                copy_plane_last(0, f, nc.vector.tensor_copy)
+            for f in range(2):
+                copy_plane_last(1, f, nc.scalar.copy)
+            for f in range(2):
+                quantize_plane(2, f)
+            for i in range(2):
+                for f in range(2):
+                    quantize_plane_last(i, f)
 
             for Q in range(4):
                 queue = nc.scalar if Q % 2 == 0 else nc.sync

@@ -22,9 +22,13 @@ LAST = N // CH - 1
 INV_SQRT = 1.0 / 32.0
 RING_BANKS = 5
 SIDE_BANKS = 2
-G1 = 320
-G2 = 352
+G0 = 128
+G1 = 352
+G2 = 384
 S1 = 256
+X1 = 96
+X2 = 96
+PLANE_ROWS = (256, 256, 256, 256)
 
 
 def tile_innerproductsigmoidresidualprojection_kernel(tc, z, y, adj, g, bj, v, r, out_0, out_1, out_2):
@@ -55,19 +59,22 @@ def tile_innerproductsigmoidresidualprojection_kernel(tc, z, y, adj, g, bj, v, r
         def chunk(c):
             return slice(CH * c, CH * c + CH)
 
-        vecs = {name: tile([P, 2, 4], BF16, "vec_" + name) for name in ("r", "g", "bj")}
+        vecs = {name: tile([P, 2, 4], BF16, "vec_" + name) for name in ("r", "g")}
+        vec_pair = tile([P, 4, 4], BF16, "vec_pair")
+        vecs["v"], vecs["bj"] = vec_pair[:, 0:2, :], vec_pair[:, 2:4, :]
         y_scaled = [tile([P, 4, D], BF16, "y_scaled_%d" % G) for G in range(2)]
         yr_codes = [tile([P, D], U32, "yr_codes_%d" % G) for G in range(2)]
         yr_scales = [tile([P, D], U8, "yr_scales_%d" % G) for G in range(2)]
-        yg_codes = [tile([P, 2, HALF], U32, "yg_codes_%d" % G) for G in range(2)]
-        yg_scales = [tile([P, 2, HALF], U8, "yg_scales_%d" % G) for G in range(2)]
+        yg_codes = [tile([P, 4, 2, P], U32, "yg_codes_%d" % G) for G in range(2)]
+        yg_scales = [tile([P, 4, 2, P], U8, "yg_scales_%d" % G) for G in range(2)]
         out_scales = tile([P, 2, N], U8, "out_scales")
+        r_f32 = tile([P, 2, 4], F32, "r_f32")
         ident = tile([P, P], F32, "ident")
         vec_rows = tile([P, HALF], BF16, "vec_rows")
         v_bank = psum.tile([P, HALF], F32, name="v_bank", tag="v_bank")
         table_probe = tile([P, 1], F32, "table_probe")
 
-        y_raw, adj_sorted, z_raw, adj_raw, yg_bf = {}, {}, {}, {}, {}
+        y_raw, y_row, adj_sorted, z_raw, adj_raw, yg_bf = {}, {}, {}, {}, {}, {}
         y_bank, z_bank, adj_bank, out_bank, plane_bank = {}, {}, {}, {}, {}
         yr_bf, z_bf, z_codes, z_scales, prob, diff = {}, {}, {}, {}, {}, {}
         res_bf, res_mx, out_f32, out_bf, plane_bf, plane_codes = {}, {}, {}, {}, {}, {}
@@ -78,15 +85,14 @@ def tile_innerproductsigmoidresidualprojection_kernel(tc, z, y, adj, g, bj, v, r
         def load_vec_rows(first, src):
             nc.sync.dma_start(out=vec_rows[first : first + 2, :], in_=src.rearrange("(G k) -> G k", G=2))
 
-        def turned_vec(row):
-            return v_bank[:, 0 : 2 * P].bitcast(BF16).rearrange("p (u c e) -> p c u e", u=2, e=2)[:, row, :, :]
+        def turned_vec(first, count):
+            return v_bank[:, 0 : 2 * P].bitcast(BF16).rearrange("p (k t) -> p k t", t=4)[:, first : first + count, :]
 
-        def y_slots(G, jp):
-            return y[half(G), :].rearrange("(p j) d -> p j d", j=4)[:, 2 * jp : 2 * jp + 2, :]
-
-        def load_y(G, jp):
-            y_raw[G, jp] = tile([P, 2, D], BF16, "raw_y_%d" % (2 * G + jp))
-            nc.sync.dma_start(out=y_raw[G, jp][:], in_=y_slots(G, jp))
+        def load_y(G, first, count):
+            raw = tile([P, count, D], BF16, "raw_y_%d_%d" % (G, first))
+            nc.sync.dma_start(out=raw[:], in_=y[half(G), :].rearrange("(p j) d -> p j d", j=4)[:, first : first + count, :])
+            for j in range(count):
+                y_row[G, first + j] = raw[:, j, :]
 
         def slots(rows, c):
             return rows[chunk(c), :].rearrange("(i p) k -> p i k" if c == LAST else "(p i) k -> p i k", i=2)
@@ -122,43 +128,55 @@ def tile_innerproductsigmoidresidualprojection_kernel(tc, z, y, adj, g, bj, v, r
                     stop=(k == 1),
                 )
 
-        def turn_y(G, jp, f):
-            y_bank[G, jp, f] = ring_bank()
-            turn(y_bank[G, jp, f], y_raw[G, jp][:, :, half(f)])
+        def turn_y(G, j):
+            bank = ring_bank()
+            y_bank[G, j] = bank
+            words = y_row[G, j].bitcast(F32)
+            for f in range(2):
+                for u in range(2):
+                    nc.tensor.transpose(bank[:, CH * u + P * f : CH * u + P * f + P], words[:, CH * f + u : CH * f + CH : 2], ident[:])
 
-        def times_g(G, jp, f):
-            if (jp, f) == (0, 0):
-                yg_bf[G] = tile([P, 2, HALF, 4], BF16, "yg_bf")
-            src = y_bank[G, jp, f][:].bitcast(BF16).rearrange("p (u m e) -> p m u e", u=2, e=2)
-            dst = yg_bf[G][:, f, chunk(jp), :].rearrange("p m (u e) -> p m u e", u=2)
-            factor = vecs["g"][:, f, :].unsqueeze(1).to_broadcast([P, CH, 4]).rearrange("p m (u e) -> p m u e", u=2)
+        def times_g(G, j):
+            if j == 0:
+                yg_bf[G] = tile([P, 4, 2, P, 4], BF16, "yg_bf")
+            src = y_bank[G, j][:].bitcast(BF16).rearrange("p (u f m e) -> p f m u e", u=2, f=2, e=2)
+            dst = yg_bf[G][:, j, :, :, :].rearrange("p f m (u e) -> p f m u e", u=2)
+            factor = vecs["g"][:].unsqueeze(2).to_broadcast([P, 2, P, 4]).rearrange("p f m (u e) -> p f m u e", u=2)
             nc.vector.tensor_tensor(out=dst, in0=src, in1=factor, op=ALU.mult)
 
         def quantize_yg(G):
-            quantize_pair(yg_codes[G], yg_scales[G], yg_bf[G])
-
-        def turn_z_half(c, f):
-            if f == 0:
-                z_bf[c] = tile([P, 2, CH, 4], BF16, "z_bf_%d" % c)
-            z_bank[c, f] = ring_bank()
-            turn(z_bank[c, f], z_raw[c][:, :, half(f)])
-
-        def copy_z(c, f):
-            dst = z_bf[c][:, f, :, :].rearrange("p n t -> p (n t)").bitcast(F32).rearrange("p (n u) -> p n u", u=2)
-            nc.scalar.copy(out=dst, in_=z_bank[c, f][:].rearrange("p (u n) -> p n u", u=2))
+            quantize(
+                yg_codes[G][:].rearrange("p j f m -> p (j f m)"),
+                yg_scales[G][:].rearrange("p j f m -> p (j f m)"),
+                yg_bf[G][:].rearrange("p j f m t -> p (j f m t)"),
+            )
 
         def turn_z(c):
+            first = min(c, 2)
+            if c == first:
+                z_bf[first] = tile([P, 2, CH if c < 2 else HALF, 4], BF16, "z_bf_%d" % first)
             for f in range(2):
-                turn_z_half(c, f)
-                copy_z(c, f)
+                z_bank[c, f] = ring_bank()
+                turn(z_bank[c, f], z_raw[c][:, :, half(f)])
+
+        def copy_z(c):
+            first = min(c, 2)
+            for f in range(2):
+                bank = z_bank[c, f]
+                dst = z_bf[first][:, f, chunk(c - first), :].rearrange("p n t -> p (n t)").bitcast(F32).rearrange("p (n u) -> p n u", u=2)
+                nc.scalar.copy(out=dst, in_=bank[:].rearrange("p (u n) -> p n u", u=2))
 
         def quantize_z(c):
-            z_codes[c] = tile([P, 2, CH], U32, "z_codes_%d" % c)
-            z_scales[c] = tile([P, 2, CH], U8, "z_scales_%d" % c)
+            width = z_bf[c].shape[2]
+            z_codes[c] = tile([P, 2, width], U32, "z_codes_%d" % c)
+            z_scales[c] = tile([P, 2, width], U8, "z_scales_%d" % c)
             quantize_pair(z_codes[c], z_scales[c], z_bf[c])
 
         def times_r(G, j):
-            nc.vector.tensor_scalar_mul(y_scaled[G][:, j, :], y_raw[G, j // 2][:, j % 2, :], vecs["r"][:, G, j : j + 1])
+            nc.vector.tensor_scalar_mul(y_scaled[G][:, j, :], y_row[G, j], vecs["r"][:, G, j : j + 1])
+
+        def times_r_scalar(G, j):
+            nc.scalar.activation(out=y_scaled[G][:, j, :], in_=y_row[G, j], func=ACT.Copy, scale=r_f32[:, G, j : j + 1])
 
         def interleave_scalar(dst, src):
             nc.scalar.copy(out=dst.rearrange("p (c i) t -> p c t i", i=4), in_=src.rearrange("p t (c i) -> p c t i", i=4))
@@ -167,11 +185,14 @@ def tile_innerproductsigmoidresidualprojection_kernel(tc, z, y, adj, g, bj, v, r
             nc.vector.tensor_copy(out=dst.rearrange("p (c i) t -> p c t i", i=4), in_=src.rearrange("p t (c i) -> p c t i", i=4))
 
         def interleave(engine, G, first, last):
-            h, col = divmod(first, HALF)
-            engine(yr_bf[G, h][:, col : col + last - first, :], y_scaled[G][:, :, first:last])
+            dst, col = (yr_bf[0], first) if G == 0 else (yr_bf[1, first // HALF], first % HALF)
+            engine(dst[:, col : col + last - first, :], y_scaled[G][:, :, first:last])
 
         def interleave_gpsimd(dst, src):
             gpsimd_scale(dst, src.rearrange("p t d -> p d t"), 1.0)
+
+        def quantize_yr_first(h):
+            quantize(yr_codes[0][:, half(h)], yr_scales[0][:, half(h)], yr_bf[0][:, half(h), :].rearrange("p d t -> p (d t)"))
 
         def quantize_yr(G, h):
             quantize(yr_codes[G][:, half(h)], yr_scales[G][:, half(h)], yr_bf[G, h][:].rearrange("p d t -> p (d t)"))
@@ -182,8 +203,8 @@ def tile_innerproductsigmoidresidualprojection_kernel(tc, z, y, adj, g, bj, v, r
         def score_product(out, G, t, codes, scales):
             mx_product(
                 out,
-                [yg_codes[G][:, f, P * t : P * t + P] for f in range(2)],
-                [yg_scales[G][:, f, P * t : P * t + P] for f in range(2)],
+                [yg_codes[G][:, t, f, :] for f in range(2)],
+                [yg_scales[G][:, t, f, :] for f in range(2)],
                 [codes[:, f, :] for f in range(2)],
                 [scales[:, f, :] for f in range(2)],
             )
@@ -197,65 +218,96 @@ def tile_innerproductsigmoidresidualprojection_kernel(tc, z, y, adj, g, bj, v, r
             for e in range(2):
                 sigmoid(prob[c, G][:, 2 * tp + e, :], bank[:, chunk(e)], G, 2 * tp + e)
 
+        def scores_wide(G, t):
+            if t == 0:
+                prob["wide", G] = tile([P, 4, HALF], F32, "prob_wide_%d" % G)
+                for c in range(2, 4):
+                    prob[c, G] = prob["wide", G][:, :, chunk(c - 2)]
+            bank = ring_bank()
+            score_product(bank[:], G, t, z_codes[2], z_scales[2])
+            sigmoid(prob["wide", G][:, t, :], bank[:], G, t)
+
         def turn_adj(c, G):
             adj_bank[c, G] = side_bank()
             turn(adj_bank[c, G], adj_raw[c][:, :, half(G)])
 
-        def sort_adj(c, tag):
-            adj_sorted[c] = tile([P, 2, 4 * P, 2], BF16, tag)
-            gpsimd_scale(adj_sorted[c][:], adj_raw[c][:].rearrange("p i (w u e) -> p u (i w) e", u=2, e=2), 1.0)
-
-        def turn_sorted_adj(c, G):
-            adj_bank[c, G] = side_bank()
-            for i in range(2):
-                for u in range(2):
-                    words = adj_sorted[c][:, u, block(2 * i + G), :].rearrange("p q e -> p (q e)").bitcast(F32)
-                    nc.tensor.transpose(adj_bank[c, G][:, CH * u + P * i : CH * u + P * i + P], words, ident[:])
-
         def block(i):
             return slice(P * i, P * i + P)
 
-        def minus_adj(c, G, cols=slice(0, CH)):
-            if cols.start == 0:
-                diff[c, G] = tile([P, 2, CH, 2], F32, "diff_%d" % G)
+        def minus_adj(c, G):
+            parts = 2 if c == LAST else 1
+            if G == 0:
+                diff[c] = tile([P, 2, parts, 2, CH // parts, 2], F32, "diff_%d" % (c % 2))
             nc.vector.tensor_tensor(
-                out=diff[c, G][:, :, cols, :],
-                in0=prob[c, G].rearrange("p (u e) n -> p u n e", u=2)[:, :, cols, :],
-                in1=adj_bank[c, G][:].bitcast(BF16).rearrange("p (u n e) -> p u n e", u=2, e=2)[:, :, cols, :],
+                out=diff[c][:, :, :, G, :, :],
+                in0=prob[c, G].rearrange("p (u e) (b n) -> p u b n e", u=2, b=parts),
+                in1=adj_bank[c, G][:].bitcast(BF16).rearrange("p (u b n e) -> p u b n e", u=2, b=parts, e=2),
                 op=ALU.subtract,
             )
 
-        def multiply_v(dst, src, G, width):
+        def minus_last(G, b):
+            if (G, b) == (0, 0):
+                diff[LAST] = tile([P, 2, 2, 2, P, 2], F32, "diff_1")
             nc.vector.tensor_tensor(
-                out=dst.rearrange("p n (u e) -> p n u e", u=2),
-                in0=src.rearrange("p u n e -> p n u e"),
-                in1=turned_vec(G).unsqueeze(1).to_broadcast([P, width, 2, 2]),
+                out=diff[LAST][:, :, b, G, :, :],
+                in0=prob[LAST, G].rearrange("p (u e) n -> p u n e", u=2)[:, :, block(b), :],
+                in1=adj_bank[LAST, G][:].bitcast(BF16).rearrange("p (u n e) -> p u n e", u=2, e=2)[:, :, block(b), :],
+                op=ALU.subtract,
+            )
+
+        def times_v(c, b=0):
+            src = diff[c][:, :, b, :, :, :]
+            width = src.shape[3]
+            res_bf[c, b] = tile([P, 2, width, 4], BF16, "res_last_%d" % b)
+            nc.vector.tensor_tensor(
+                out=res_bf[c, b][:].rearrange("p G n (u e) -> p G n u e", u=2),
+                in0=src.rearrange("p u G n e -> p G n u e"),
+                in1=turned_vec(0, 2).unsqueeze(2).to_broadcast([P, 2, width, 4]).rearrange("p G n (u e) -> p G n u e", u=2),
                 op=ALU.mult,
             )
 
-        def times_v(c, G, cols=slice(0, CH)):
-            if G == 0 and cols.start == 0:
-                res_bf[c] = tile([P, 2, CH, 4], BF16, "res_bf_%d" % (c % 2))
-            multiply_v(res_bf[c][:, G, cols, :], diff[c, G][:, :, cols, :], G, cols.stop - cols.start)
+        def new_res(c):
+            res_bf[c, 0] = tile([P, 2, CH, 4], BF16, "res_bf_%d" % (len(res_bf) % 2))
 
-        def quantize_res(c):
-            codes = tile([P, 2, CH], U32, "res_codes_%d" % c)
-            scales = tile([P, 2, CH], U8, "res_scales_%d" % c)
+        def times_v_part(engine, factor, c, G, cols):
+            engine.tensor_tensor(
+                out=res_bf[c, 0][:, G, cols, :].rearrange("p n (u e) -> p n u e", u=2),
+                in0=diff[c][:, :, 0, G, cols, :].rearrange("p u n e -> p n u e"),
+                in1=factor[:, G, :].unsqueeze(1).to_broadcast([P, cols.stop - cols.start, 4]).rearrange("p n (u e) -> p n u e", u=2),
+                op=ALU.mult,
+            )
+
+        def times_v_vector(c, G, first=0):
+            times_v_part(nc.vector, turned_vec(0, 2), c, G, slice(first, CH))
+
+        def times_v_gpsimd(c, G, last):
+            times_v_part(nc.gpsimd, vecs["v"], c, G, slice(0, last))
+
+        def times_v_final(G):
+            if G == 0:
+                res_bf[LAST, 1] = tile([P, 2, P, 4], BF16, "res_last_1")
+            nc.vector.tensor_tensor(
+                out=res_bf[LAST, 1][:, G, :, :].rearrange("p n (u e) -> p n u e", u=2),
+                in0=diff[LAST][:, :, 1, G, :, :].rearrange("p u n e -> p n u e"),
+                in1=turned_vec(0, 2)[:, G, :].unsqueeze(1).to_broadcast([P, P, 4]).rearrange("p n (u e) -> p n u e", u=2),
+                op=ALU.mult,
+            )
+
+        def quantize_res_halves(c):
+            codes = tile([P, 2, CH], U32, "res_codes_%d_0" % c)
+            scales = tile([P, 2, CH], U8, "res_scales_%d_0" % c)
             for G in range(2):
-                quantize(codes[:, G, :], scales[:, G, :], res_bf[c][:, G, :, :].rearrange("p n t -> p (n t)"))
+                quantize(codes[:, G, :], scales[:, G, :], res_bf[c, 0][:, G, :, :].rearrange("p n t -> p (n t)"))
             for i in range(2):
                 res_mx[c, i] = (codes[:, :, block(i)], scales[:, :, block(i)])
 
-        def times_v_last(G, i):
-            if G == 0:
-                res_bf[LAST, i] = tile([P, 2, P, 4], BF16, "res_last_%d" % i)
-            multiply_v(res_bf[LAST, i][:, G, :, :], diff[LAST, G][:, :, P * i : P * i + P, :], G, P)
-
-        def quantize_res_last(i):
-            codes = tile([P, 2, P], U32, "res_codes_last_%d" % i)
-            scales = tile([P, 2, P], U8, "res_scales_last_%d" % i)
-            quantize_pair(codes, scales, res_bf[LAST, i])
-            res_mx[LAST, i] = (codes[:], scales[:])
+        def quantize_res(c, b=0):
+            width = res_bf[c, b].shape[2]
+            codes = tile([P, 2, width], U32, "res_codes_%d_%d" % (c, b))
+            scales = tile([P, 2, width], U8, "res_scales_%d_%d" % (c, b))
+            quantize_pair(codes, scales, res_bf[c, b])
+            for k in range(width // P):
+                res_mx[c, b + k] = (codes[:, :, block(k)], scales[:, :, block(k)])
 
         def product(c, i, h):
             out_bank[c, i, h] = ring_bank()
@@ -319,9 +371,13 @@ def tile_innerproductsigmoidresidualprojection_kernel(tc, z, y, adj, g, bj, v, r
             for i in range(2):
                 turn_out_block(c, i, new_bank)
 
+        def plane_rows(c, f, first, width):
+            if (c, f) not in plane_bf:
+                plane_bf[c, f] = tile([P, PLANE_ROWS[c], 4], BF16, ("plane_bf_0_%d", "plane_bf_1_%d", "y_scaled_%d", "yr_bf_%d")[c] % f)
+            return plane_bf[c, f][:, first : first + width, :].rearrange("p n t -> p (n t)")
+
         def copy_plane(c, f, copy):
-            plane_bf[c, f] = tile([P, CH, 4], BF16, "plane_bf_%d" % (2 * (c % 2) + f))
-            dst = plane_bf[c, f][:].rearrange("p n t -> p (n t)").bitcast(F32).rearrange("p (q i u) -> p q i u", i=2, u=2)
+            dst = plane_rows(c, f, 0, CH).bitcast(F32).rearrange("p (q i u) -> p q i u", i=2, u=2)
             copy(out=dst, in_=plane_bank[c, f][:].rearrange("p (u i q) -> p q i u", u=2, i=2))
 
         def turn_out_last(i, f, bank):
@@ -332,24 +388,18 @@ def tile_innerproductsigmoidresidualprojection_kernel(tc, z, y, adj, g, bj, v, r
                 nc.tensor.transpose(bank[:, P * u : P * u + P], words[:, first : first + P], ident[:])
 
         def copy_plane_last(i, f, copy):
-            plane_bf[LAST, i, f] = tile([P, P, 4], BF16, "plane_last_%d" % (2 * i + f))
-            dst = plane_bf[LAST, i, f][:].rearrange("p n t -> p (n t)").bitcast(F32).rearrange("p (n u) -> p n u", u=2)
-            copy(out=dst, in_=plane_bank[LAST, i, f][:, 0:CH].rearrange("p (u n) -> p n u", u=2))
-
-        def quantize_plane_last(i, f):
-            if f == 0:
-                plane_codes[LAST, i] = tile([P, 2, P], U32, "plane_codes_last_%d" % i)
-            rows = slice(CH * LAST + P * i, CH * LAST + P * i + P)
-            quantize(plane_codes[LAST, i][:, f, :], out_scales[:, f, rows], plane_bf[LAST, i, f][:].rearrange("p n t -> p (n t)"))
-            if f == 1:
-                nc.sync.dma_start(out=out_1[:, :, rows, :].rearrange("f p n t -> p f (n t)").bitcast(I32), in_=plane_codes[LAST, i][:].bitcast(I32))
+            rows = plane_rows(LAST, f, P * i, P)
+            copy(out=rows.bitcast(F32).rearrange("p (n u) -> p n u", u=2), in_=plane_bank[LAST, i, f][:, 0:CH].rearrange("p (u n) -> p n u", u=2))
 
         def quantize_plane(c, f):
-            if f == 0:
-                plane_codes[c] = tile([P, 2, CH], U32, "plane_codes_%d" % c)
-            quantize(plane_codes[c][:, f, :], out_scales[:, f, chunk(c)], plane_bf[c, f][:].rearrange("p n t -> p (n t)"))
-            if f == 1:
-                nc.sync.dma_start(out=out_1[:, :, chunk(c), :].rearrange("f p n t -> p f (n t)").bitcast(I32), in_=plane_codes[c][:].bitcast(I32))
+            first_half = c not in plane_codes
+            if first_half:
+                plane_codes[c] = tile([P, 2, PLANE_ROWS[c]], U32, "plane_codes_%d" % c)
+            first = sum(PLANE_ROWS[:c])
+            rows = slice(first, first + PLANE_ROWS[c])
+            quantize(plane_codes[c][:, f, :], out_scales[:, f, rows], plane_rows(c, f, 0, PLANE_ROWS[c]))
+            if not first_half:
+                nc.sync.dma_start(out=out_1[:, :, rows, :].rearrange("f p n t -> p f (n t)").bitcast(I32), in_=plane_codes[c][:].bitcast(I32))
 
         with tc.manual_schedule():
             load_vec("r", r)
@@ -358,77 +408,79 @@ def tile_innerproductsigmoidresidualprojection_kernel(tc, z, y, adj, g, bj, v, r
             make_identity(nc, ident[:])
             nc.scalar.activation(out=table_probe[:], in_=ident[:, 0:1], func=ACT.Sigmoid)
 
-            for jp in range(2):
-                load_y(0, jp)
+            for j in range(2):
+                load_y(0, j, 1)
+            load_y(0, 2, 2)
             load_rows(z_raw, z, "z", 0)
             load_vec_rows(0, v)
             load_vec_rows(2, bj)
             for jp in range(2):
-                load_y(1, jp)
+                load_y(1, 2 * jp, 2)
             load_rows(adj_raw, adj, "adj", 0)
             for c in range(1, 4):
                 load_rows(z_raw, z, "z", c)
-                if c > 1:
-                    load_rows(adj_raw, adj, "adj", c - 1)
-            load_rows(adj_raw, adj, "adj", LAST)
+            for c in range(1, 4):
+                load_rows(adj_raw, adj, "adj", c)
 
-            for h in range(2):
-                yr_bf[0, h] = tile([P, HALF, 4], BF16, "yr_bf_%d" % h)
-            for jp in range(2):
-                for f in range(2):
-                    turn_y(0, jp, f)
+            nc.scalar.copy(out=r_f32[:], in_=vecs["r"][:])
+            yr_bf[0] = tile([P, D, 4], BF16, "yr_bf_0")
+            for j in range(4):
+                turn_y(0, j)
             for j in range(2):
                 times_r(0, j)
-            times_g(0, 0, 0)
+                times_g(0, j)
+            times_r(0, 2)
+            times_r_scalar(0, 3)
+            interleave(interleave_gpsimd, 0, 0, G0)
+            interleave(interleave_scalar, 0, G0, S1)
             for j in range(2, 4):
-                times_r(0, j)
-            interleave(interleave_scalar, 0, 0, S1)
-            times_g(0, 0, 1)
-            for f in range(2):
-                times_g(0, 1, f)
+                times_g(0, j)
             turn_z(0)
+            copy_z(0)
             vec_words = vec_rows[:].bitcast(F32)
             for u in range(2):
-                nc.tensor.transpose(v_bank[:, P * u : P * u + P], vec_words[:, u:256:2], ident[:])
-            nc.scalar.copy(out=vecs["bj"][:].rearrange("p G (u e) -> p G u e", u=2), in_=turned_vec(slice(2, 4)))
-            interleave(interleave_scalar, 0, S1, HALF)
-            interleave(interleave_scalar, 0, HALF, D)
+                nc.tensor.transpose(v_bank[:, u : 2 * P : 2], vec_words[:, u:256:2], ident[:])
+            nc.scalar.copy(out=vec_pair[:], in_=turned_vec(0, 4))
+            interleave(interleave_scalar, 0, S1, D)
 
-            for jp in range(2):
-                for f in range(2):
-                    turn_y(1, jp, f)
+            for j in range(4):
+                turn_y(1, j)
             times_r(1, 0)
             quantize_yg(0)
             times_r(1, 1)
             quantize_z(0)
             for j in range(2, 4):
                 times_r(1, j)
-            yr_bf[1, 0] = tile([P, HALF, 4], BF16, "yr_bf_2")
+            yr_bf[1, 0] = tile([P, HALF, 4], BF16, "yr_bf_1")
             interleave(interleave_gpsimd, 1, 0, G1)
-            for jp in range(2):
-                for f in range(2):
-                    times_g(1, jp, f)
+            for j in range(4):
+                times_g(1, j)
             scores(0, 0, 0)
             for G in range(2):
                 turn_adj(0, G)
             interleave(interleave_scalar, 1, G1, HALF)
             scores(0, 0, 1)
-            quantize_yr(0, 0)
+            quantize_yr_first(0)
             quantize_yg(1)
             turn_z(1)
+            copy_z(1)
+            turn_z(2)
+            copy_z(2)
             for tp in range(2):
                 scores(0, 1, tp)
 
-            quantize_yr(0, 1)
+            quantize_yr_first(1)
             minus_adj(0, 0)
             quantize_z(1)
             yr_bf[1, 1] = tile([P, HALF, 4], BF16, "z_bf_1")
             interleave(interleave_gpsimd, 1, HALF, HALF + G2)
-            times_v(0, 0)
+            new_res(0)
+            times_v_vector(0, 0)
             minus_adj(0, 1)
-            turn_z(2)
+            turn_z(LAST)
+            copy_z(LAST)
             quantize_z(2)
-            times_v(0, 1)
+            times_v_vector(0, 1)
             for G in range(2):
                 for tp in range(2):
                     scores(1, G, tp)
@@ -438,91 +490,85 @@ def tile_innerproductsigmoidresidualprojection_kernel(tc, z, y, adj, g, bj, v, r
             quantize_yr(1, 0)
             quantize_res(0)
             quantize_yr(1, 1)
-            sort_adj(2, "z_bf_1")
-            for tp in range(2):
-                scores(2, 0, tp)
+            for t in range(4):
+                scores_wide(0, t)
 
             for G in range(2):
                 minus_adj(1, G)
-            for G in range(2):
-                times_v(1, G)
+            new_res(1)
+            times_v_gpsimd(1, 0, X1)
+            times_v_vector(1, 0, X1)
+            times_v_vector(1, 1)
             row_block(0, 0)
             round_gpsimd(0, 0)
-            row_block(0, 1)
-            turn_z(LAST)
-            for tp in range(2):
-                scores(2, 1, tp)
+            for t in range(4):
+                scores_wide(1, t)
             for G in range(2):
-                turn_sorted_adj(2, G)
-            quantize_z(LAST)
-            quantize_res(1)
-            sort_adj(LAST, "res_bf_1")
-            round_gpsimd(0, 1)
-            for tp in range(2):
-                scores(LAST, 0, tp)
+                turn_adj(2, G)
+            row_block(0, 1)
+            quantize_res_halves(1)
 
             for G in range(2):
                 minus_adj(2, G)
-            for G in range(2):
-                times_v(2, G)
+            new_res(2)
+            times_v_gpsimd(2, 0, X2)
+            round_gpsimd(0, 1)
+            times_v_vector(2, 0, X2)
+            times_v_vector(2, 1)
             for i in range(2):
                 row_block(1, i)
-            for tp in range(2):
-                scores(LAST, 1, tp)
             for G in range(2):
-                turn_sorted_adj(LAST, G)
+                turn_adj(LAST, G)
             turn_out(0, ring_bank)
             for f in range(2):
                 copy_plane(0, f, nc.scalar.copy)
-            quantize_res(2)
+            quantize_res_halves(2)
             round_gpsimd(1, 0, "res_bf_0")
             round_gpsimd(1, 1)
 
             for G in range(2):
-                minus_adj(LAST, G, block(0))
-            for G in range(2):
-                times_v_last(G, 0)
-            minus_adj(LAST, 0, block(1))
-            quantize_res_last(0)
+                minus_last(G, 0)
+            minus_last(0, 1)
+            times_v(LAST, 0)
+            quantize_plane(0, 0)
+            quantize_res(LAST, 0)
             row_block(2, 0)
             round_gpsimd(2, 0, "res_last_0")
             row_block(2, 1)
             turn_out(1, ring_bank)
             for f in range(2):
                 copy_plane(1, f, nc.scalar.copy)
-            minus_adj(LAST, 1, block(1))
+            minus_last(1, 1)
             for G in range(2):
-                times_v_last(G, 1)
-            quantize_plane(0, 0)
-            quantize_res_last(1)
+                times_v_final(G)
+            round_vector(2, 1)
+            quantize_res(LAST, 1)
             quantize_plane(0, 1)
             row_block(LAST, 0)
-            round_vector(2, 1)
+            for h in range(2):
+                round_from_psum(LAST, 0, h)
             for f in range(2):
                 quantize_plane(1, f)
-            turn_out_block(2, 0, side_bank)
+            turn_out(2, side_bank)
             for h in range(2):
                 product(LAST, 1, h)
-            turn_out_block(2, 1, side_bank)
-            round_vector(LAST, 0)
+            copy_plane(2, 0, nc.scalar.copy)
+            copy_plane(2, 1, nc.vector.tensor_copy)
             round_from_psum(LAST, 1, 0)
-            copy_out(LAST, 1, 0)
             round_from_psum(LAST, 1, 1, "vector")
             for i in range(2):
                 for f in range(2):
-                    turn_out_last(i, f, ring_bank())
-            copy_plane(2, 0, nc.scalar.copy)
-            copy_out(LAST, 1, 1)
-            copy_plane(2, 1, nc.vector.tensor_copy)
+                    turn_out_last(i, f, ring_bank() if i == 0 else side_bank())
+            for f in range(2):
+                quantize_plane(2, 1 - f)
+            for h in range(2):
+                copy_out(LAST, 1, h)
             for f in range(2):
                 copy_plane_last(0, f, nc.vector.tensor_copy)
             for f in range(2):
                 copy_plane_last(1, f, nc.scalar.copy)
             for f in range(2):
-                quantize_plane(2, f)
-            for i in range(2):
-                for f in range(2):
-                    quantize_plane_last(i, f)
+                quantize_plane(LAST, f)
 
             for Q in range(4):
                 queue = nc.scalar if Q % 2 == 0 else nc.sync

@@ -23,12 +23,12 @@ INV_SQRT = 1.0 / 32.0
 RING_BANKS = 5
 SIDE_BANKS = 2
 G0 = 128
-G1 = 352
-G2 = 384
+G1 = 400
+G2 = 416
 S1 = 256
-X1 = 96
-X2 = 96
-PLANE_ROWS = (256, 256, 256, 256)
+X1 = 112
+X2 = 128
+PLANE_ROWS = (256, 256, 256, 128, 128)
 
 
 def tile_innerproductsigmoidresidualprojection_kernel(tc, z, y, adj, g, bj, v, r, out_0, out_1, out_2):
@@ -373,7 +373,7 @@ def tile_innerproductsigmoidresidualprojection_kernel(tc, z, y, adj, g, bj, v, r
 
         def plane_rows(c, f, first, width):
             if (c, f) not in plane_bf:
-                plane_bf[c, f] = tile([P, PLANE_ROWS[c], 4], BF16, ("plane_bf_0_%d", "plane_bf_1_%d", "y_scaled_%d", "yr_bf_%d")[c] % f)
+                plane_bf[c, f] = tile([P, PLANE_ROWS[c], 4], BF16, ("plane_bf_0_%d", "plane_bf_1_%d", "y_scaled_%d", "yr_bf_%d", "plane_bf_0_%d")[c] % f)
             return plane_bf[c, f][:, first : first + width, :].rearrange("p n t -> p (n t)")
 
         def copy_plane(c, f, copy):
@@ -388,7 +388,7 @@ def tile_innerproductsigmoidresidualprojection_kernel(tc, z, y, adj, g, bj, v, r
                 nc.tensor.transpose(bank[:, P * u : P * u + P], words[:, first : first + P], ident[:])
 
         def copy_plane_last(i, f, copy):
-            rows = plane_rows(LAST, f, P * i, P)
+            rows = plane_rows(LAST + i, f, 0, P)
             copy(out=rows.bitcast(F32).rearrange("p (n u) -> p n u", u=2), in_=plane_bank[LAST, i, f][:, 0:CH].rearrange("p (u n) -> p n u", u=2))
 
         def quantize_plane(c, f):
@@ -534,41 +534,42 @@ def tile_innerproductsigmoidresidualprojection_kernel(tc, z, y, adj, g, bj, v, r
             quantize_res(LAST, 0)
             row_block(2, 0)
             round_gpsimd(2, 0, "res_last_0")
-            row_block(2, 1)
+            for h in range(2):
+                product(2, 1, h)
+                round_from_psum(2, 1, h)
+                copy_out(2, 1, h)
             turn_out(1, ring_bank)
-            for f in range(2):
-                copy_plane(1, f, nc.scalar.copy)
             minus_last(1, 1)
             for G in range(2):
                 times_v_final(G)
-            round_vector(2, 1)
-            quantize_res(LAST, 1)
             quantize_plane(0, 1)
+            quantize_res(LAST, 1)
             row_block(LAST, 0)
-            for h in range(2):
-                round_from_psum(LAST, 0, h)
             for f in range(2):
-                quantize_plane(1, f)
+                copy_plane(1, f, nc.vector.tensor_copy)
             turn_out(2, side_bank)
             for h in range(2):
                 product(LAST, 1, h)
+            round_gpsimd(LAST, 0)
             copy_plane(2, 0, nc.scalar.copy)
             copy_plane(2, 1, nc.vector.tensor_copy)
-            round_from_psum(LAST, 1, 0)
-            round_from_psum(LAST, 1, 1, "vector")
+            for h in range(2):
+                round_from_psum(LAST, 1, h)
+            for f in range(2):
+                quantize_plane(1, f)
+            copy_out(LAST, 1, 0)
+            for f in range(2):
+                quantize_plane(2, f)
+            copy_out(LAST, 1, 1)
             for i in range(2):
                 for f in range(2):
                     turn_out_last(i, f, ring_bank() if i == 0 else side_bank())
-            for f in range(2):
-                quantize_plane(2, 1 - f)
-            for h in range(2):
-                copy_out(LAST, 1, h)
-            for f in range(2):
-                copy_plane_last(0, f, nc.vector.tensor_copy)
-            for f in range(2):
-                copy_plane_last(1, f, nc.scalar.copy)
-            for f in range(2):
-                quantize_plane(LAST, f)
+            for i in range(2):
+                copy_plane_last(i, 0, nc.vector.tensor_copy)
+                copy_plane_last(i, 1, nc.scalar.copy)
+            for c in range(LAST, LAST + 2):
+                for f in range(2):
+                    quantize_plane(c, f)
 
             for Q in range(4):
                 queue = nc.scalar if Q % 2 == 0 else nc.sync

@@ -22,12 +22,11 @@ LAST = N // CH - 1
 INV_SQRT = 1.0 / 32.0
 RING_BANKS = 5
 SIDE_BANKS = 2
-G0 = 128
-G1 = 400
-G2 = 416
+G0 = 96
+G1 = 336
+G2 = 320
 S1 = 256
-X1 = 112
-X2 = 128
+X1 = 176
 PLANE_ROWS = (256, 256, 256, 128, 128)
 
 
@@ -68,7 +67,6 @@ def tile_innerproductsigmoidresidualprojection_kernel(tc, z, y, adj, g, bj, v, r
         yg_codes = [tile([P, 4, 2, P], U32, "yg_codes_%d" % G) for G in range(2)]
         yg_scales = [tile([P, 4, 2, P], U8, "yg_scales_%d" % G) for G in range(2)]
         out_scales = tile([P, 2, N], U8, "out_scales")
-        r_f32 = tile([P, 2, 4], F32, "r_f32")
         ident = tile([P, P], F32, "ident")
         vec_rows = tile([P, HALF], BF16, "vec_rows")
         v_bank = psum.tile([P, HALF], F32, name="v_bank", tag="v_bank")
@@ -77,6 +75,7 @@ def tile_innerproductsigmoidresidualprojection_kernel(tc, z, y, adj, g, bj, v, r
         y_raw, y_row, adj_sorted, z_raw, adj_raw, yg_bf = {}, {}, {}, {}, {}, {}
         y_bank, z_bank, adj_bank, out_bank, plane_bank = {}, {}, {}, {}, {}
         yr_bf, z_bf, z_codes, z_scales, prob, diff = {}, {}, {}, {}, {}, {}
+        out_pair, pair_bf = {}, {}
         res_bf, res_mx, out_f32, out_bf, plane_bf, plane_codes = {}, {}, {}, {}, {}, {}
 
         def load_vec(name, src):
@@ -142,7 +141,7 @@ def tile_innerproductsigmoidresidualprojection_kernel(tc, z, y, adj, g, bj, v, r
             src = y_bank[G, j][:].bitcast(BF16).rearrange("p (u f m e) -> p f m u e", u=2, f=2, e=2)
             dst = yg_bf[G][:, j, :, :, :].rearrange("p f m (u e) -> p f m u e", u=2)
             factor = vecs["g"][:].unsqueeze(2).to_broadcast([P, 2, P, 4]).rearrange("p f m (u e) -> p f m u e", u=2)
-            nc.vector.tensor_tensor(out=dst, in0=src, in1=factor, op=ALU.mult)
+            nc.vector.tensor_tensor(out=dst, in0=factor, in1=src, op=ALU.mult)
 
         def quantize_yg(G):
             quantize(
@@ -174,9 +173,6 @@ def tile_innerproductsigmoidresidualprojection_kernel(tc, z, y, adj, g, bj, v, r
 
         def times_r(G, j):
             nc.vector.tensor_scalar_mul(y_scaled[G][:, j, :], y_row[G, j], vecs["r"][:, G, j : j + 1])
-
-        def times_r_scalar(G, j):
-            nc.scalar.activation(out=y_scaled[G][:, j, :], in_=y_row[G, j], func=ACT.Copy, scale=r_f32[:, G, j : j + 1])
 
         def interleave_scalar(dst, src):
             nc.scalar.copy(out=dst.rearrange("p (c i) t -> p c t i", i=4), in_=src.rearrange("p t (c i) -> p c t i", i=4))
@@ -321,7 +317,11 @@ def tile_innerproductsigmoidresidualprojection_kernel(tc, z, y, adj, g, bj, v, r
             )
 
         def copy_out(c, i, h, scale=nc.scalar.mul):
-            if h == 0:
+            if c == 1:
+                if (i, h) == (0, 0):
+                    out_pair[c] = tile([P, 2, D], F32, "yg_bf")
+                out_f32[c, i] = out_pair[c][:, i, :]
+            elif h == 0:
                 out_f32[c, i] = tile([P, D], F32, "raw_%s_%d" % (("z", "adj")[i], c))
             dst = out_f32[c, i][:, half(h)]
             scale(dst, out_bank[c, i, h][:], INV_SQRT)
@@ -349,6 +349,11 @@ def tile_innerproductsigmoidresidualprojection_kernel(tc, z, y, adj, g, bj, v, r
         def round_gpsimd(c, i, tag=None):
             gpsimd_scale(new_out_bf(c, i, tag), by_words(out_f32[c, i][:]), 1.0)
 
+        def round_pair_gpsimd(c, tag):
+            both = tile([P, 2, 2 * CH, 2], BF16, tag)
+            gpsimd_scale(both[:], out_pair[c][:].rearrange("p i (q u e) -> p u (i q) e", u=2, e=2), 1.0)
+            pair_bf[c] = both
+
         def round_from_psum(c, i, h, engine="scalar"):
             if h == 0:
                 new_out_bf(c, i)
@@ -359,13 +364,15 @@ def tile_innerproductsigmoidresidualprojection_kernel(tc, z, y, adj, g, bj, v, r
                 nc.vector.tensor_scalar_mul(dst, by_words(out_bank[c, i, h][:]), INV_SQRT)
 
         def turn_out_block(c, i, new_bank):
-            words = out_bf[c, i][:].bitcast(F32)
             for f in range(2):
                 if i == 0:
                     plane_bank[c, f] = new_bank()
                 for u in range(2):
-                    first = CH * u + P * f
-                    nc.tensor.transpose(plane_bank[c, f][:, CH * u + P * i : CH * u + P * i + P], words[:, first : first + P], ident[:])
+                    if c in pair_bf:
+                        words = pair_bf[c][:, u, block(2 * i + f), :].rearrange("p q e -> p (q e)").bitcast(F32)
+                    else:
+                        words = out_bf[c, i][:].bitcast(F32)[:, block(2 * u + f)]
+                    nc.tensor.transpose(plane_bank[c, f][:, CH * u + P * i : CH * u + P * i + P], words, ident[:])
 
         def turn_out(c, new_bank):
             for i in range(2):
@@ -422,15 +429,14 @@ def tile_innerproductsigmoidresidualprojection_kernel(tc, z, y, adj, g, bj, v, r
             for c in range(1, 4):
                 load_rows(adj_raw, adj, "adj", c)
 
-            nc.scalar.copy(out=r_f32[:], in_=vecs["r"][:])
             yr_bf[0] = tile([P, D, 4], BF16, "yr_bf_0")
             for j in range(4):
                 turn_y(0, j)
             for j in range(2):
                 times_r(0, j)
                 times_g(0, j)
-            times_r(0, 2)
-            times_r_scalar(0, 3)
+            for j in range(2, 4):
+                times_r(0, j)
             interleave(interleave_gpsimd, 0, 0, G0)
             interleave(interleave_scalar, 0, G0, S1)
             for j in range(2, 4):
@@ -455,24 +461,24 @@ def tile_innerproductsigmoidresidualprojection_kernel(tc, z, y, adj, g, bj, v, r
             interleave(interleave_gpsimd, 1, 0, G1)
             for j in range(4):
                 times_g(1, j)
-            scores(0, 0, 0)
             for G in range(2):
                 turn_adj(0, G)
             interleave(interleave_scalar, 1, G1, HALF)
+            scores(0, 0, 0)
+            turn_z(1)
+            copy_z(1)
             scores(0, 0, 1)
             quantize_yr_first(0)
             quantize_yg(1)
-            turn_z(1)
-            copy_z(1)
             turn_z(2)
             copy_z(2)
             for tp in range(2):
                 scores(0, 1, tp)
 
-            quantize_yr_first(1)
-            minus_adj(0, 0)
             quantize_z(1)
-            yr_bf[1, 1] = tile([P, HALF, 4], BF16, "z_bf_1")
+            minus_adj(0, 0)
+            quantize_yr_first(1)
+            yr_bf[1, 1] = tile([P, HALF, 4], BF16, "yr_bf_0")
             interleave(interleave_gpsimd, 1, HALF, HALF + G2)
             new_res(0)
             times_v_vector(0, 0)
@@ -500,21 +506,20 @@ def tile_innerproductsigmoidresidualprojection_kernel(tc, z, y, adj, g, bj, v, r
             times_v_vector(1, 0, X1)
             times_v_vector(1, 1)
             row_block(0, 0)
-            round_gpsimd(0, 0)
             for t in range(4):
                 scores_wide(1, t)
             for G in range(2):
                 turn_adj(2, G)
             row_block(0, 1)
             quantize_res_halves(1)
+            round_gpsimd(0, 0, "res_bf_1")
 
             for G in range(2):
                 minus_adj(2, G)
             new_res(2)
-            times_v_gpsimd(2, 0, X2)
             round_gpsimd(0, 1)
-            times_v_vector(2, 0, X2)
-            times_v_vector(2, 1)
+            for G in range(2):
+                times_v_vector(2, G)
             for i in range(2):
                 row_block(1, i)
             for G in range(2):
@@ -523,8 +528,7 @@ def tile_innerproductsigmoidresidualprojection_kernel(tc, z, y, adj, g, bj, v, r
             for f in range(2):
                 copy_plane(0, f, nc.scalar.copy)
             quantize_res_halves(2)
-            round_gpsimd(1, 0, "res_bf_0")
-            round_gpsimd(1, 1)
+            round_pair_gpsimd(1, "res_bf_0")
 
             for G in range(2):
                 minus_last(G, 0)

@@ -22,11 +22,12 @@ LAST = N // CH - 1
 INV_SQRT = 1.0 / 32.0
 RING_BANKS = 5
 SIDE_BANKS = 2
-G0 = 96
-G1 = 336
-G2 = 320
-S1 = 256
-X1 = 176
+G0 = 112
+G1 = 352
+G2 = 336
+S1 = 336
+X1 = 160
+X2 = 64
 PLANE_ROWS = (256, 256, 256, 128, 128)
 
 
@@ -67,6 +68,7 @@ def tile_innerproductsigmoidresidualprojection_kernel(tc, z, y, adj, g, bj, v, r
         yg_codes = [tile([P, 4, 2, P], U32, "yg_codes_%d" % G) for G in range(2)]
         yg_scales = [tile([P, 4, 2, P], U8, "yg_scales_%d" % G) for G in range(2)]
         out_scales = tile([P, 2, N], U8, "out_scales")
+        r_f32 = tile([P, 2, 4], F32, "r_f32")
         ident = tile([P, P], F32, "ident")
         vec_rows = tile([P, HALF], BF16, "vec_rows")
         v_bank = psum.tile([P, HALF], F32, name="v_bank", tag="v_bank")
@@ -75,7 +77,7 @@ def tile_innerproductsigmoidresidualprojection_kernel(tc, z, y, adj, g, bj, v, r
         y_raw, y_row, adj_sorted, z_raw, adj_raw, yg_bf = {}, {}, {}, {}, {}, {}
         y_bank, z_bank, adj_bank, out_bank, plane_bank = {}, {}, {}, {}, {}
         yr_bf, z_bf, z_codes, z_scales, prob, diff = {}, {}, {}, {}, {}, {}
-        out_pair, pair_bf = {}, {}
+        out_pair, pair_bf, copied = {}, {}, set()
         res_bf, res_mx, out_f32, out_bf, plane_bf, plane_codes = {}, {}, {}, {}, {}, {}
 
         def load_vec(name, src):
@@ -136,7 +138,7 @@ def tile_innerproductsigmoidresidualprojection_kernel(tc, z, y, adj, g, bj, v, r
                     nc.tensor.transpose(bank[:, CH * u + P * f : CH * u + P * f + P], words[:, CH * f + u : CH * f + CH : 2], ident[:])
 
         def times_g(G, j):
-            if j == 0:
+            if G not in yg_bf:
                 yg_bf[G] = tile([P, 4, 2, P, 4], BF16, "yg_bf")
             src = y_bank[G, j][:].bitcast(BF16).rearrange("p (u f m e) -> p f m u e", u=2, f=2, e=2)
             dst = yg_bf[G][:, j, :, :, :].rearrange("p f m (u e) -> p f m u e", u=2)
@@ -158,9 +160,9 @@ def tile_innerproductsigmoidresidualprojection_kernel(tc, z, y, adj, g, bj, v, r
                 z_bank[c, f] = ring_bank()
                 turn(z_bank[c, f], z_raw[c][:, :, half(f)])
 
-        def copy_z(c):
+        def copy_z(c, order=(0, 1)):
             first = min(c, 2)
-            for f in range(2):
+            for f in order:
                 bank = z_bank[c, f]
                 dst = z_bf[first][:, f, chunk(c - first), :].rearrange("p n t -> p (n t)").bitcast(F32).rearrange("p (n u) -> p n u", u=2)
                 nc.scalar.copy(out=dst, in_=bank[:].rearrange("p (u n) -> p n u", u=2))
@@ -173,6 +175,9 @@ def tile_innerproductsigmoidresidualprojection_kernel(tc, z, y, adj, g, bj, v, r
 
         def times_r(G, j):
             nc.vector.tensor_scalar_mul(y_scaled[G][:, j, :], y_row[G, j], vecs["r"][:, G, j : j + 1])
+
+        def times_r_scalar(G, j):
+            nc.scalar.activation(out=y_scaled[G][:, j, :], in_=y_row[G, j], func=ACT.Copy, scale=r_f32[:, G, j : j + 1])
 
         def interleave_scalar(dst, src):
             nc.scalar.copy(out=dst.rearrange("p (c i) t -> p c t i", i=4), in_=src.rearrange("p t (c i) -> p c t i", i=4))
@@ -223,52 +228,80 @@ def tile_innerproductsigmoidresidualprojection_kernel(tc, z, y, adj, g, bj, v, r
             score_product(bank[:], G, t, z_codes[2], z_scales[2])
             sigmoid(prob["wide", G][:, t, :], bank[:], G, t)
 
+        def scores_both(c, G):
+            prob[c, G] = tile([P, 4, CH], F32, "prob_%d_%d" % (c, G))[:]
+            banks = [ring_bank(), ring_bank()]
+            for t in range(4):
+                score_product(banks[t // 2][:, chunk(t % 2)], G, t, z_codes[c], z_scales[c])
+            for t in reversed(range(4)):
+                sigmoid(prob[c, G][:, t, :], banks[t // 2][:, chunk(t % 2)], G, t)
+
+        def scores_wide_pair(G, tp):
+            if tp == 0:
+                prob["wide", G] = tile([P, 4, HALF], F32, "prob_wide_%d" % G)
+                for c in range(2, 4):
+                    prob[c, G] = prob["wide", G][:, :, chunk(c - 2)]
+            banks = [ring_bank(), ring_bank()]
+            for e in range(2):
+                score_product(banks[e][:], G, 2 * tp + e, z_codes[2], z_scales[2])
+            for e in reversed(range(2)):
+                sigmoid(prob["wide", G][:, 2 * tp + e, :], banks[e][:], G, 2 * tp + e)
+
         def turn_adj(c, G):
             adj_bank[c, G] = side_bank()
             turn(adj_bank[c, G], adj_raw[c][:, :, half(G)])
 
+        def sort_adj(c, tag):
+            adj_sorted[c] = tile([P, 2, 4 * P], U32, tag)
+            nc.gpsimd.tensor_copy(out=adj_sorted[c][:], in_=adj_raw[c][:].bitcast(U32).rearrange("p i (w u) -> p u (i w)", u=2))
+
+        def turn_sorted_adj(c, G):
+            adj_bank[c, G] = side_bank()
+            for i in range(2):
+                for u in range(2):
+                    words = adj_sorted[c][:, u, block(2 * i + G)].bitcast(F32)
+                    nc.tensor.transpose(adj_bank[c, G][:, CH * u + P * i : CH * u + P * i + P], words, ident[:])
+
         def block(i):
             return slice(P * i, P * i + P)
 
-        def minus_adj(c, G):
-            parts = 2 if c == LAST else 1
-            if G == 0:
-                diff[c] = tile([P, 2, parts, 2, CH // parts, 2], F32, "diff_%d" % (c % 2))
+        def subtract_adj(dst, c, G, cols):
             nc.vector.tensor_tensor(
-                out=diff[c][:, :, :, G, :, :],
-                in0=prob[c, G].rearrange("p (u e) (b n) -> p u b n e", u=2, b=parts),
-                in1=adj_bank[c, G][:].bitcast(BF16).rearrange("p (u b n e) -> p u b n e", u=2, b=parts, e=2),
+                out=dst,
+                in0=prob[c, G].rearrange("p (u e) n -> p u n e", u=2)[:, :, cols, :],
+                in1=adj_bank[c, G][:].bitcast(BF16).rearrange("p (u n e) -> p u n e", u=2, e=2)[:, :, cols, :],
                 op=ALU.subtract,
             )
+
+        def minus_adj(c, G):
+            diff[c, G] = tile([P, 2, CH, 2], F32, "diff_%d" % G)
+            subtract_adj(diff[c, G][:], c, G, slice(0, CH))
 
         def minus_last(G, b):
-            if (G, b) == (0, 0):
-                diff[LAST] = tile([P, 2, 2, 2, P, 2], F32, "diff_1")
-            nc.vector.tensor_tensor(
-                out=diff[LAST][:, :, b, G, :, :],
-                in0=prob[LAST, G].rearrange("p (u e) n -> p u n e", u=2)[:, :, block(b), :],
-                in1=adj_bank[LAST, G][:].bitcast(BF16).rearrange("p (u n e) -> p u n e", u=2, e=2)[:, :, block(b), :],
-                op=ALU.subtract,
-            )
+            if b == 1:
+                diff[LAST, 1, G] = tile([P, 2, P, 2], F32, "diff_last_%d" % G)
+                subtract_adj(diff[LAST, 1, G][:], LAST, G, block(1))
+            else:
+                if (LAST, 0) not in diff:
+                    diff[LAST, 0] = tile([P, 2, 2, P, 2], F32, "diff_0")
+                subtract_adj(diff[LAST, 0][:, :, G, :, :], LAST, G, block(0))
 
-        def times_v(c, b=0):
-            src = diff[c][:, :, b, :, :, :]
-            width = src.shape[3]
-            res_bf[c, b] = tile([P, 2, width, 4], BF16, "res_last_%d" % b)
+        def times_v(c, b):
+            res_bf[c, b] = tile([P, 2, P, 4], BF16, "res_last_%d" % b)
             nc.vector.tensor_tensor(
                 out=res_bf[c, b][:].rearrange("p G n (u e) -> p G n u e", u=2),
-                in0=src.rearrange("p u G n e -> p G n u e"),
-                in1=turned_vec(0, 2).unsqueeze(2).to_broadcast([P, 2, width, 4]).rearrange("p G n (u e) -> p G n u e", u=2),
+                in0=diff[c, b][:].rearrange("p u G n e -> p G n u e"),
+                in1=turned_vec(0, 2).unsqueeze(2).to_broadcast([P, 2, P, 4]).rearrange("p G n (u e) -> p G n u e", u=2),
                 op=ALU.mult,
             )
 
-        def new_res(c):
-            res_bf[c, 0] = tile([P, 2, CH, 4], BF16, "res_bf_%d" % (len(res_bf) % 2))
+        def new_res(c, tag):
+            res_bf[c, 0] = tile([P, 2, CH, 4], BF16, tag)
 
         def times_v_part(engine, factor, c, G, cols):
             engine.tensor_tensor(
                 out=res_bf[c, 0][:, G, cols, :].rearrange("p n (u e) -> p n u e", u=2),
-                in0=diff[c][:, :, 0, G, cols, :].rearrange("p u n e -> p n u e"),
+                in0=diff[c, G][:, :, cols, :].rearrange("p u n e -> p n u e"),
                 in1=factor[:, G, :].unsqueeze(1).to_broadcast([P, cols.stop - cols.start, 4]).rearrange("p n (u e) -> p n u e", u=2),
                 op=ALU.mult,
             )
@@ -284,15 +317,15 @@ def tile_innerproductsigmoidresidualprojection_kernel(tc, z, y, adj, g, bj, v, r
                 res_bf[LAST, 1] = tile([P, 2, P, 4], BF16, "res_last_1")
             nc.vector.tensor_tensor(
                 out=res_bf[LAST, 1][:, G, :, :].rearrange("p n (u e) -> p n u e", u=2),
-                in0=diff[LAST][:, :, 1, G, :, :].rearrange("p u n e -> p n u e"),
+                in0=diff[LAST, 1, G][:].rearrange("p u n e -> p n u e"),
                 in1=turned_vec(0, 2)[:, G, :].unsqueeze(1).to_broadcast([P, P, 4]).rearrange("p n (u e) -> p n u e", u=2),
                 op=ALU.mult,
             )
 
-        def quantize_res_halves(c):
+        def quantize_res_halves(c, order=(0, 1)):
             codes = tile([P, 2, CH], U32, "res_codes_%d_0" % c)
             scales = tile([P, 2, CH], U8, "res_scales_%d_0" % c)
-            for G in range(2):
+            for G in order:
                 quantize(codes[:, G, :], scales[:, G, :], res_bf[c, 0][:, G, :, :].rearrange("p n t -> p (n t)"))
             for i in range(2):
                 res_mx[c, i] = (codes[:, :, block(i)], scales[:, :, block(i)])
@@ -318,22 +351,29 @@ def tile_innerproductsigmoidresidualprojection_kernel(tc, z, y, adj, g, bj, v, r
 
         def copy_out(c, i, h, scale=nc.scalar.mul):
             if c == 1:
-                if (i, h) == (0, 0):
+                if c not in out_pair:
                     out_pair[c] = tile([P, 2, D], F32, "yg_bf")
                 out_f32[c, i] = out_pair[c][:, i, :]
-            elif h == 0:
+            elif (c, i) not in out_f32:
                 out_f32[c, i] = tile([P, D], F32, "raw_%s_%d" % (("z", "adj")[i], c))
             dst = out_f32[c, i][:, half(h)]
             scale(dst, out_bank[c, i, h][:], INV_SQRT)
             rows = slots(out_0, c)[:, i, :]
             if (c, i) == (LAST, 1):
                 nc.sync.dma_start(out=rows[:, half(h)], in_=dst)
-            elif h == 1:
+            elif (c, i, 1 - h) in copied:
                 nc.sync.dma_start(out=rows, in_=out_f32[c, i][:])
+            copied.add((c, i, h))
 
         def row_block(c, i):
             for h in range(2):
                 product(c, i, h)
+                copy_out(c, i, h)
+
+        def row_block_reversed(c, i):
+            for h in range(2):
+                product(c, i, h)
+            for h in reversed(range(2)):
                 copy_out(c, i, h)
 
         def new_out_bf(c, i, tag=None):
@@ -355,7 +395,7 @@ def tile_innerproductsigmoidresidualprojection_kernel(tc, z, y, adj, g, bj, v, r
             pair_bf[c] = both
 
         def round_from_psum(c, i, h, engine="scalar"):
-            if h == 0:
+            if (c, i) not in out_bf:
                 new_out_bf(c, i)
             dst = out_bf[c, i][:].rearrange("p (u q e) -> p u q e", u=2, e=2)[:, :, P * h : P * h + P, :]
             if engine == "scalar":
@@ -429,11 +469,13 @@ def tile_innerproductsigmoidresidualprojection_kernel(tc, z, y, adj, g, bj, v, r
             for c in range(1, 4):
                 load_rows(adj_raw, adj, "adj", c)
 
+            nc.scalar.copy(out=r_f32[:], in_=vecs["r"][:])
             yr_bf[0] = tile([P, D, 4], BF16, "yr_bf_0")
             for j in range(4):
                 turn_y(0, j)
+            times_r(0, 0)
+            times_r_scalar(0, 1)
             for j in range(2):
-                times_r(0, j)
                 times_g(0, j)
             for j in range(2, 4):
                 times_r(0, j)
@@ -480,7 +522,7 @@ def tile_innerproductsigmoidresidualprojection_kernel(tc, z, y, adj, g, bj, v, r
             quantize_yr_first(1)
             yr_bf[1, 1] = tile([P, HALF, 4], BF16, "yr_bf_0")
             interleave(interleave_gpsimd, 1, HALF, HALF + G2)
-            new_res(0)
+            new_res(0, "res_bf_0")
             times_v_vector(0, 0)
             minus_adj(0, 1)
             turn_z(LAST)
@@ -496,12 +538,13 @@ def tile_innerproductsigmoidresidualprojection_kernel(tc, z, y, adj, g, bj, v, r
             quantize_yr(1, 0)
             quantize_res(0)
             quantize_yr(1, 1)
+            sort_adj(2, "yr_bf_0")
             for t in range(4):
                 scores_wide(0, t)
 
             for G in range(2):
                 minus_adj(1, G)
-            new_res(1)
+            new_res(1, "res_bf_1")
             times_v_gpsimd(1, 0, X1)
             times_v_vector(1, 0, X1)
             times_v_vector(1, 1)
@@ -509,17 +552,18 @@ def tile_innerproductsigmoidresidualprojection_kernel(tc, z, y, adj, g, bj, v, r
             for t in range(4):
                 scores_wide(1, t)
             for G in range(2):
-                turn_adj(2, G)
+                turn_sorted_adj(2, G)
             row_block(0, 1)
             quantize_res_halves(1)
             round_gpsimd(0, 0, "res_bf_1")
 
             for G in range(2):
                 minus_adj(2, G)
-            new_res(2)
+            new_res(2, "res_bf_0")
+            times_v_gpsimd(2, 0, X2)
             round_gpsimd(0, 1)
-            for G in range(2):
-                times_v_vector(2, G)
+            times_v_vector(2, 0, X2)
+            times_v_vector(2, 1)
             for i in range(2):
                 row_block(1, i)
             for G in range(2):

from contextlib import ExitStack

import concourse.mybir as mybir
from concourse.masks import make_identity

N, M, D = 1024, 1024, 1024
FLOPS = 2 * N * M * D + 2 * N * M * D

F32 = mybir.dt.float32
BF16 = mybir.dt.bfloat16
U32 = mybir.dt.uint32
I32 = mybir.dt.int32
U8 = mybir.dt.uint8
FP8X4 = mybir.dt.float8_e4m3fn_x4
ACT = mybir.ActivationFunctionType
ALU = mybir.AluOpType

P = 128
HALF = 512
CH = 256
LAST = N // CH - 1
INV_SQRT = 1.0 / 32.0
RING_BANKS = 5
SIDE_BANKS = 2
G0 = 112
G1 = 352
G2 = 336
S1 = 336
X1 = 160
X2 = 64
PLANE_ROWS = (256, 256, 256, 128, 128)


def tile_innerproductsigmoidresidualprojection_kernel(tc, z, y, adj, g, bj, v, r, out_0, out_1, out_2):
    nc = tc.nc
    with ExitStack() as ctx:
        sbuf = ctx.enter_context(tc.tile_pool(name="sbuf", bufs=1))
        psum = ctx.enter_context(tc.psum_pool(name="psum", bufs=1))

        def tile(shape, dtype, tag):
            return sbuf.tile(shape, dtype, name=tag, tag=tag, align_bytes=64)

        ring_taken, side_taken = [], []

        def next_bank(taken, name, count):
            tag = "%s_%d" % (name, len(taken) % count)
            taken.append(tag)
            return psum.tile([P, HALF], F32, name=tag, tag=tag)

        def ring_bank():
            return next_bank(ring_taken, "ring", RING_BANKS)

        def side_bank():
            return next_bank(side_taken, "side", SIDE_BANKS)

        def half(h):
            return slice(HALF * h, HALF * h + HALF)

        def chunk(c):
            return slice(CH * c, CH * c + CH)

        vecs = {name: tile([P, 2, 4], BF16, "vec_" + name) for name in ("r", "g")}
        vec_pair = tile([P, 4, 4], BF16, "vec_pair")
        vecs["v"], vecs["bj"] = vec_pair[:, 0:2, :], vec_pair[:, 2:4, :]
        y_scaled = [tile([P, 4, D], BF16, "y_scaled_%d" % G) for G in range(2)]
        yr_codes = [tile([P, D], U32, "yr_codes_%d" % G) for G in range(2)]
        yr_scales = [tile([P, D], U8, "yr_scales_%d" % G) for G in range(2)]
        yg_codes = [tile([P, 4, 2, P], U32, "yg_codes_%d" % G) for G in range(2)]
        yg_scales = [tile([P, 4, 2, P], U8, "yg_scales_%d" % G) for G in range(2)]
        out_scales = tile([P, 2, N], U8, "out_scales")
        r_f32 = tile([P, 2, 4], F32, "r_f32")
        ident = tile([P, P], F32, "ident")
        vec_rows = tile([P, HALF], BF16, "vec_rows")
        v_bank = psum.tile([P, HALF], F32, name="v_bank", tag="v_bank")
        table_probe = tile([P, 1], F32, "table_probe")

        y_raw, y_row, adj_sorted, z_raw, adj_raw, yg_bf = {}, {}, {}, {}, {}, {}
        y_bank, z_bank, adj_bank, out_bank, plane_bank = {}, {}, {}, {}, {}
        yr_bf, z_bf, z_codes, z_scales, prob, diff = {}, {}, {}, {}, {}, {}
        out_pair, pair_bf, copied = {}, {}, set()
        res_bf, res_mx, out_f32, out_bf, plane_bf, plane_codes = {}, {}, {}, {}, {}, {}

        def load_vec(name, src):
            nc.scalar.dma_start(out=vecs[name][:], in_=src.rearrange("(G p t) -> p G t", p=P, t=4))

        def load_vec_rows(first, src):
            nc.sync.dma_start(out=vec_rows[first : first + 2, :], in_=src.rearrange("(G k) -> G k", G=2))

        def turned_vec(first, count):
            return v_bank[:, 0 : 2 * P].bitcast(BF16).rearrange("p (k t) -> p k t", t=4)[:, first : first + count, :]

        def load_y(G, first, count):
            raw = tile([P, count, D], BF16, "raw_y_%d_%d" % (G, first))
            nc.sync.dma_start(out=raw[:], in_=y[half(G), :].rearrange("(p j) d -> p j d", j=4)[:, first : first + count, :])
            for j in range(count):
                y_row[G, first + j] = raw[:, j, :]

        def slots(rows, c):
            return rows[chunk(c), :].rearrange("(i p) k -> p i k" if c == LAST else "(p i) k -> p i k", i=2)

        def load_rows(dst, src, name, c):
            dst[c] = tile([P, 2, D], BF16, "raw_%s_%d" % (name, c))
            nc.sync.dma_start(out=dst[c][:], in_=slots(src, c))

        def turn(bank, rows):
            for i in range(2):
                words = rows[:, i, :].bitcast(F32)
                for u in range(2):
                    nc.tensor.transpose(bank[:, CH * u + P * i : CH * u + P * i + P], words[:, u:256:2], ident[:])

        def quantize(codes, scales, src):
            nc.vector.quantize_mx(out=codes.bitcast(FP8X4), scales=scales, in_=src)

        def quantize_pair(codes, scales, src):
            quantize(codes[:].rearrange("p a n -> p (a n)"), scales[:].rearrange("p a n -> p (a n)"), src[:].rearrange("p a n t -> p (a n t)"))

        def gpsimd_scale(dst, src, factor):
            nc.gpsimd.tensor_scalar(out=dst, in0=src, scalar1=factor, scalar2=0.0, op0=ALU.mult, op1=ALU.add)

        def mx_product(bank, lhs_codes, lhs_scales, rhs_codes, rhs_scales):
            for k in range(2):
                nc.tensor.matmul_mx(
                    out=bank,
                    lhsT=lhs_codes[k].bitcast(FP8X4),
                    lhsT_scale=lhs_scales[k],
                    rhs=rhs_codes[k].bitcast(FP8X4),
                    rhs_scale=rhs_scales[k],
                    start=(k == 0),
                    stop=(k == 1),
                )

        def turn_y(G, j):
            bank = ring_bank()
            y_bank[G, j] = bank
            words = y_row[G, j].bitcast(F32)
            for f in range(2):
                for u in range(2):
                    nc.tensor.transpose(bank[:, CH * u + P * f : CH * u + P * f + P], words[:, CH * f + u : CH * f + CH : 2], ident[:])

        def times_g(G, j):
            if G not in yg_bf:
                yg_bf[G] = tile([P, 4, 2, P, 4], BF16, "yg_bf")
            src = y_bank[G, j][:].bitcast(BF16).rearrange("p (u f m e) -> p f m u e", u=2, f=2, e=2)
            dst = yg_bf[G][:, j, :, :, :].rearrange("p f m (u e) -> p f m u e", u=2)
            factor = vecs["g"][:].unsqueeze(2).to_broadcast([P, 2, P, 4]).rearrange("p f m (u e) -> p f m u e", u=2)
            nc.vector.tensor_tensor(out=dst, in0=factor, in1=src, op=ALU.mult)

        def quantize_yg(G):
            quantize(
                yg_codes[G][:].rearrange("p j f m -> p (j f m)"),
                yg_scales[G][:].rearrange("p j f m -> p (j f m)"),
                yg_bf[G][:].rearrange("p j f m t -> p (j f m t)"),
            )

        def turn_z(c):
            first = min(c, 2)
            if c == first:
                z_bf[first] = tile([P, 2, CH if c < 2 else HALF, 4], BF16, "z_bf_%d" % first)
            for f in range(2):
                z_bank[c, f] = ring_bank()
                turn(z_bank[c, f], z_raw[c][:, :, half(f)])

        def copy_z(c, order=(0, 1)):
            first = min(c, 2)
            for f in order:
                bank = z_bank[c, f]
                dst = z_bf[first][:, f, chunk(c - first), :].rearrange("p n t -> p (n t)").bitcast(F32).rearrange("p (n u) -> p n u", u=2)
                nc.scalar.copy(out=dst, in_=bank[:].rearrange("p (u n) -> p n u", u=2))

        def quantize_z(c):
            width = z_bf[c].shape[2]
            z_codes[c] = tile([P, 2, width], U32, "z_codes_%d" % c)
            z_scales[c] = tile([P, 2, width], U8, "z_scales_%d" % c)
            quantize_pair(z_codes[c], z_scales[c], z_bf[c])

        def times_r(G, j):
            nc.vector.tensor_scalar_mul(y_scaled[G][:, j, :], y_row[G, j], vecs["r"][:, G, j : j + 1])

        def times_r_scalar(G, j):
            nc.scalar.activation(out=y_scaled[G][:, j, :], in_=y_row[G, j], func=ACT.Copy, scale=r_f32[:, G, j : j + 1])

        def interleave_scalar(dst, src):
            nc.scalar.copy(out=dst.rearrange("p (c i) t -> p c t i", i=4), in_=src.rearrange("p t (c i) -> p c t i", i=4))

        def interleave_vector(dst, src):
            nc.vector.tensor_copy(out=dst.rearrange("p (c i) t -> p c t i", i=4), in_=src.rearrange("p t (c i) -> p c t i", i=4))

        def interleave(engine, G, first, last):
            dst, col = (yr_bf[0], first) if G == 0 else (yr_bf[1, first // HALF], first % HALF)
            engine(dst[:, col : col + last - first, :], y_scaled[G][:, :, first:last])

        def interleave_gpsimd(dst, src):
            gpsimd_scale(dst, src.rearrange("p t d -> p d t"), 1.0)

        def quantize_yr_first(h):
            quantize(yr_codes[0][:, half(h)], yr_scales[0][:, half(h)], yr_bf[0][:, half(h), :].rearrange("p d t -> p (d t)"))

        def quantize_yr(G, h):
            quantize(yr_codes[G][:, half(h)], yr_scales[G][:, half(h)], yr_bf[G, h][:].rearrange("p d t -> p (d t)"))

        def sigmoid(dst, src, G, t):
            nc.scalar.activation(out=dst, in_=src, func=ACT.Sigmoid, bias=vecs["bj"][:, G, t : t + 1], scale=INV_SQRT)

        def score_product(out, G, t, codes, scales):
            mx_product(
                out,
                [yg_codes[G][:, t, f, :] for f in range(2)],
                [yg_scales[G][:, t, f, :] for f in range(2)],
                [codes[:, f, :] for f in range(2)],
                [scales[:, f, :] for f in range(2)],
            )

        def scores(c, G, tp):
            if tp == 0:
                prob[c, G] = tile([P, 4, CH], F32, "prob_%d_%d" % (c, G))[:]
            bank = ring_bank()
            for e in range(2):
                score_product(bank[:, chunk(e)], G, 2 * tp + e, z_codes[c], z_scales[c])
            for e in range(2):
                sigmoid(prob[c, G][:, 2 * tp + e, :], bank[:, chunk(e)], G, 2 * tp + e)

        def scores_wide(G, t):
            if t == 0:
                prob["wide", G] = tile([P, 4, HALF], F32, "prob_wide_%d" % G)
                for c in range(2, 4):
                    prob[c, G] = prob["wide", G][:, :, chunk(c - 2)]
            bank = ring_bank()
            score_product(bank[:], G, t, z_codes[2], z_scales[2])
            sigmoid(prob["wide", G][:, t, :], bank[:], G, t)

        def scores_both(c, G):
            prob[c, G] = tile([P, 4, CH], F32, "prob_%d_%d" % (c, G))[:]
            banks = [ring_bank(), ring_bank()]
            for t in range(4):
                score_product(banks[t // 2][:, chunk(t % 2)], G, t, z_codes[c], z_scales[c])
            for t in reversed(range(4)):
                sigmoid(prob[c, G][:, t, :], banks[t // 2][:, chunk(t % 2)], G, t)

        def scores_wide_pair(G, tp):
            if tp == 0:
                prob["wide", G] = tile([P, 4, HALF], F32, "prob_wide_%d" % G)
                for c in range(2, 4):
                    prob[c, G] = prob["wide", G][:, :, chunk(c - 2)]
            banks = [ring_bank(), ring_bank()]
            for e in range(2):
                score_product(banks[e][:], G, 2 * tp + e, z_codes[2], z_scales[2])
            for e in reversed(range(2)):
                sigmoid(prob["wide", G][:, 2 * tp + e, :], banks[e][:], G, 2 * tp + e)

        def turn_adj(c, G):
            adj_bank[c, G] = side_bank()
            turn(adj_bank[c, G], adj_raw[c][:, :, half(G)])

        def sort_adj(c, tag):
            adj_sorted[c] = tile([P, 2, 4 * P], U32, tag)
            nc.gpsimd.tensor_copy(out=adj_sorted[c][:], in_=adj_raw[c][:].bitcast(U32).rearrange("p i (w u) -> p u (i w)", u=2))

        def turn_sorted_adj(c, G):
            adj_bank[c, G] = side_bank()
            for i in range(2):
                for u in range(2):
                    words = adj_sorted[c][:, u, block(2 * i + G)].bitcast(F32)
                    nc.tensor.transpose(adj_bank[c, G][:, CH * u + P * i : CH * u + P * i + P], words, ident[:])

        def block(i):
            return slice(P * i, P * i + P)

        def subtract_adj(dst, c, G, cols):
            nc.vector.tensor_tensor(
                out=dst,
                in0=prob[c, G].rearrange("p (u e) n -> p u n e", u=2)[:, :, cols, :],
                in1=adj_bank[c, G][:].bitcast(BF16).rearrange("p (u n e) -> p u n e", u=2, e=2)[:, :, cols, :],
                op=ALU.subtract,
            )

        def minus_adj(c, G):
            diff[c, G] = tile([P, 2, CH, 2], F32, "diff_%d" % G)
            subtract_adj(diff[c, G][:], c, G, slice(0, CH))

        def minus_last(G, b):
            if b == 1:
                diff[LAST, 1, G] = tile([P, 2, P, 2], F32, "diff_last_%d" % G)
                subtract_adj(diff[LAST, 1, G][:], LAST, G, block(1))
            else:
                if (LAST, 0) not in diff:
                    diff[LAST, 0] = tile([P, 2, 2, P, 2], F32, "diff_0")
                subtract_adj(diff[LAST, 0][:, :, G, :, :], LAST, G, block(0))

        def times_v(c, b):
            res_bf[c, b] = tile([P, 2, P, 4], BF16, "res_last_%d" % b)
            nc.vector.tensor_tensor(
                out=res_bf[c, b][:].rearrange("p G n (u e) -> p G n u e", u=2),
                in0=diff[c, b][:].rearrange("p u G n e -> p G n u e"),
                in1=turned_vec(0, 2).unsqueeze(2).to_broadcast([P, 2, P, 4]).rearrange("p G n (u e) -> p G n u e", u=2),
                op=ALU.mult,
            )

        def new_res(c, tag):
            res_bf[c, 0] = tile([P, 2, CH, 4], BF16, tag)

        def times_v_part(engine, factor, c, G, cols):
            engine.tensor_tensor(
                out=res_bf[c, 0][:, G, cols, :].rearrange("p n (u e) -> p n u e", u=2),
                in0=diff[c, G][:, :, cols, :].rearrange("p u n e -> p n u e"),
                in1=factor[:, G, :].unsqueeze(1).to_broadcast([P, cols.stop - cols.start, 4]).rearrange("p n (u e) -> p n u e", u=2),
                op=ALU.mult,
            )

        def times_v_vector(c, G, first=0):
            times_v_part(nc.vector, turned_vec(0, 2), c, G, slice(first, CH))

        def times_v_gpsimd(c, G, last):
            times_v_part(nc.gpsimd, vecs["v"], c, G, slice(0, last))

        def times_v_final(G):
            if G == 0:
                res_bf[LAST, 1] = tile([P, 2, P, 4], BF16, "res_last_1")
            nc.vector.tensor_tensor(
                out=res_bf[LAST, 1][:, G, :, :].rearrange("p n (u e) -> p n u e", u=2),
                in0=diff[LAST, 1, G][:].rearrange("p u n e -> p n u e"),
                in1=turned_vec(0, 2)[:, G, :].unsqueeze(1).to_broadcast([P, P, 4]).rearrange("p n (u e) -> p n u e", u=2),
                op=ALU.mult,
            )

        def quantize_res_halves(c, order=(0, 1)):
            codes = tile([P, 2, CH], U32, "res_codes_%d_0" % c)
            scales = tile([P, 2, CH], U8, "res_scales_%d_0" % c)
            for G in order:
                quantize(codes[:, G, :], scales[:, G, :], res_bf[c, 0][:, G, :, :].rearrange("p n t -> p (n t)"))
            for i in range(2):
                res_mx[c, i] = (codes[:, :, block(i)], scales[:, :, block(i)])

        def quantize_res(c, b=0):
            width = res_bf[c, b].shape[2]
            codes = tile([P, 2, width], U32, "res_codes_%d_%d" % (c, b))
            scales = tile([P, 2, width], U8, "res_scales_%d_%d" % (c, b))
            quantize_pair(codes, scales, res_bf[c, b])
            for k in range(width // P):
                res_mx[c, b + k] = (codes[:, :, block(k)], scales[:, :, block(k)])

        def product(c, i, h):
            out_bank[c, i, h] = ring_bank()
            codes, scales = res_mx[c, i]
            mx_product(
                out_bank[c, i, h][:],
                [codes[:, G, :] for G in range(2)],
                [scales[:, G, :] for G in range(2)],
                [yr_codes[G][:, half(h)] for G in range(2)],
                [yr_scales[G][:, half(h)] for G in range(2)],
            )

        def copy_out(c, i, h, scale=nc.scalar.mul):
            if c == 1:
                if c not in out_pair:
                    out_pair[c] = tile([P, 2, D], F32, "yg_bf")
                out_f32[c, i] = out_pair[c][:, i, :]
            elif (c, i) not in out_f32:
                out_f32[c, i] = tile([P, D], F32, "raw_%s_%d" % (("z", "adj")[i], c))
            dst = out_f32[c, i][:, half(h)]
            scale(dst, out_bank[c, i, h][:], INV_SQRT)
            rows = slots(out_0, c)[:, i, :]
            if (c, i) == (LAST, 1):
                nc.sync.dma_start(out=rows[:, half(h)], in_=dst)
            elif (c, i, 1 - h) in copied:
                nc.sync.dma_start(out=rows, in_=out_f32[c, i][:])
            copied.add((c, i, h))

        def row_block(c, i):
            for h in range(2):
                product(c, i, h)
                copy_out(c, i, h)

        def row_block_reversed(c, i):
            for h in range(2):
                product(c, i, h)
            for h in reversed(range(2)):
                copy_out(c, i, h)

        def new_out_bf(c, i, tag=None):
            out_bf[c, i] = tile([P, D], BF16, tag or "out_bf_%d" % (2 * c + i))
            return out_bf[c, i][:].rearrange("p (u q e) -> p u q e", u=2, e=2)

        def by_words(src):
            return src.rearrange("p (q u e) -> p u q e", u=2, e=2)

        def round_vector(c, i):
            nc.vector.tensor_copy(out=new_out_bf(c, i), in_=by_words(out_f32[c, i][:]))

        def round_gpsimd(c, i, tag=None):
            gpsimd_scale(new_out_bf(c, i, tag), by_words(out_f32[c, i][:]), 1.0)

        def round_pair_gpsimd(c, tag):
            both = tile([P, 2, 2 * CH, 2], BF16, tag)
            gpsimd_scale(both[:], out_pair[c][:].rearrange("p i (q u e) -> p u (i q) e", u=2, e=2), 1.0)
            pair_bf[c] = both

        def round_from_psum(c, i, h, engine="scalar"):
            if (c, i) not in out_bf:
                new_out_bf(c, i)
            dst = out_bf[c, i][:].rearrange("p (u q e) -> p u q e", u=2, e=2)[:, :, P * h : P * h + P, :]
            if engine == "scalar":
                nc.scalar.mul(dst, by_words(out_bank[c, i, h][:]), INV_SQRT)
            else:
                nc.vector.tensor_scalar_mul(dst, by_words(out_bank[c, i, h][:]), INV_SQRT)

        def turn_out_block(c, i, new_bank):
            for f in range(2):
                if i == 0:
                    plane_bank[c, f] = new_bank()
                for u in range(2):
                    if c in pair_bf:
                        words = pair_bf[c][:, u, block(2 * i + f), :].rearrange("p q e -> p (q e)").bitcast(F32)
                    else:
                        words = out_bf[c, i][:].bitcast(F32)[:, block(2 * u + f)]
                    nc.tensor.transpose(plane_bank[c, f][:, CH * u + P * i : CH * u + P * i + P], words, ident[:])

        def turn_out(c, new_bank):
            for i in range(2):
                turn_out_block(c, i, new_bank)

        def plane_rows(c, f, first, width):
            if (c, f) not in plane_bf:
                plane_bf[c, f] = tile([P, PLANE_ROWS[c], 4], BF16, ("plane_bf_0_%d", "plane_bf_1_%d", "y_scaled_%d", "yr_bf_%d", "plane_bf_0_%d")[c] % f)
            return plane_bf[c, f][:, first : first + width, :].rearrange("p n t -> p (n t)")

        def copy_plane(c, f, copy):
            dst = plane_rows(c, f, 0, CH).bitcast(F32).rearrange("p (q i u) -> p q i u", i=2, u=2)
            copy(out=dst, in_=plane_bank[c, f][:].rearrange("p (u i q) -> p q i u", u=2, i=2))

        def turn_out_last(i, f, bank):
            plane_bank[LAST, i, f] = bank
            words = out_bf[LAST, i][:].bitcast(F32)
            for u in range(2):
                first = CH * u + P * f
                nc.tensor.transpose(bank[:, P * u : P * u + P], words[:, first : first + P], ident[:])

        def copy_plane_last(i, f, copy):
            rows = plane_rows(LAST + i, f, 0, P)
            copy(out=rows.bitcast(F32).rearrange("p (n u) -> p n u", u=2), in_=plane_bank[LAST, i, f][:, 0:CH].rearrange("p (u n) -> p n u", u=2))

        def quantize_plane(c, f):
            first_half = c not in plane_codes
            if first_half:
                plane_codes[c] = tile([P, 2, PLANE_ROWS[c]], U32, "plane_codes_%d" % c)
            first = sum(PLANE_ROWS[:c])
            rows = slice(first, first + PLANE_ROWS[c])
            quantize(plane_codes[c][:, f, :], out_scales[:, f, rows], plane_rows(c, f, 0, PLANE_ROWS[c]))
            if not first_half:
                nc.sync.dma_start(out=out_1[:, :, rows, :].rearrange("f p n t -> p f (n t)").bitcast(I32), in_=plane_codes[c][:].bitcast(I32))

        with tc.manual_schedule():
            load_vec("r", r)
            load_vec("g", g)
            nc.vector.memset(vec_rows[:], 0.0)
            make_identity(nc, ident[:])
            nc.scalar.activation(out=table_probe[:], in_=ident[:, 0:1], func=ACT.Sigmoid)

            for j in range(2):
                load_y(0, j, 1)
            load_y(0, 2, 2)
            load_rows(z_raw, z, "z", 0)
            load_vec_rows(0, v)
            load_vec_rows(2, bj)
            for jp in range(2):
                load_y(1, 2 * jp, 2)
            load_rows(adj_raw, adj, "adj", 0)
            for c in range(1, 4):
                load_rows(z_raw, z, "z", c)
            for c in range(1, 4):
                load_rows(adj_raw, adj, "adj", c)

            nc.scalar.copy(out=r_f32[:], in_=vecs["r"][:])
            yr_bf[0] = tile([P, D, 4], BF16, "yr_bf_0")
            for j in range(4):
                turn_y(0, j)
            times_r(0, 0)
            times_r_scalar(0, 1)
            for j in range(2):
                times_g(0, j)
            for j in range(2, 4):
                times_r(0, j)
            interleave(interleave_gpsimd, 0, 0, G0)
            interleave(interleave_scalar, 0, G0, S1)
            for j in range(2, 4):
                times_g(0, j)
            turn_z(0)
            copy_z(0)
            vec_words = vec_rows[:].bitcast(F32)
            for u in range(2):
                nc.tensor.transpose(v_bank[:, u : 2 * P : 2], vec_words[:, u:256:2], ident[:])
            nc.scalar.copy(out=vec_pair[:], in_=turned_vec(0, 4))
            interleave(interleave_scalar, 0, S1, D)

            for j in range(4):
                turn_y(1, j)
            times_r(1, 0)
            quantize_yg(0)
            times_r(1, 1)
            quantize_z(0)
            for j in range(2, 4):
                times_r(1, j)
            yr_bf[1, 0] = tile([P, HALF, 4], BF16, "yr_bf_1")
            interleave(interleave_gpsimd, 1, 0, G1)
            for j in range(4):
                times_g(1, j)
            for G in range(2):
                turn_adj(0, G)
            interleave(interleave_scalar, 1, G1, HALF)
            scores(0, 0, 0)
            turn_z(1)
            copy_z(1)
            scores(0, 0, 1)
            quantize_yr_first(0)
            quantize_yg(1)
            turn_z(2)
            copy_z(2)
            for tp in range(2):
                scores(0, 1, tp)

            quantize_z(1)
            minus_adj(0, 0)
            quantize_yr_first(1)
            yr_bf[1, 1] = tile([P, HALF, 4], BF16, "yr_bf_0")
            interleave(interleave_gpsimd, 1, HALF, HALF + G2)
            new_res(0, "res_bf_0")
            times_v_vector(0, 0)
            minus_adj(0, 1)
            turn_z(LAST)
            copy_z(LAST)
            quantize_z(2)
            times_v_vector(0, 1)
            for G in range(2):
                for tp in range(2):
                    scores(1, G, tp)
            interleave(interleave_scalar, 1, HALF + G2, D)
            for G in range(2):
                turn_adj(1, G)
            quantize_yr(1, 0)
            quantize_res(0)
            quantize_yr(1, 1)
            sort_adj(2, "yr_bf_0")
            for t in range(4):
                scores_wide(0, t)

            for G in range(2):
                minus_adj(1, G)
            new_res(1, "res_bf_1")
            times_v_gpsimd(1, 0, X1)
            times_v_vector(1, 0, X1)
            times_v_vector(1, 1)
            row_block(0, 0)
            for t in range(4):
                scores_wide(1, t)
            for G in range(2):
                turn_sorted_adj(2, G)
            row_block(0, 1)
            quantize_res_halves(1)
            round_gpsimd(0, 0, "res_bf_1")

            for G in range(2):
                minus_adj(2, G)
            new_res(2, "res_bf_0")
            times_v_gpsimd(2, 0, X2)
            round_gpsimd(0, 1)
            times_v_vector(2, 0, X2)
            times_v_vector(2, 1)
            for i in range(2):
                row_block(1, i)
            for G in range(2):
                turn_adj(LAST, G)
            turn_out(0, ring_bank)
            for f in range(2):
                copy_plane(0, f, nc.scalar.copy)
            quantize_res_halves(2)
            round_pair_gpsimd(1, "res_bf_0")

            for G in range(2):
                minus_last(G, 0)
            minus_last(0, 1)
            times_v(LAST, 0)
            quantize_plane(0, 0)
            quantize_res(LAST, 0)
            row_block(2, 0)
            round_gpsimd(2, 0, "res_last_0")
            for h in range(2):
                product(2, 1, h)
                round_from_psum(2, 1, h)
                copy_out(2, 1, h)
            turn_out(1, ring_bank)
            minus_last(1, 1)
            for G in range(2):
                times_v_final(G)
            quantize_plane(0, 1)
            quantize_res(LAST, 1)
            row_block(LAST, 0)
            for f in range(2):
                copy_plane(1, f, nc.vector.tensor_copy)
            turn_out(2, side_bank)
            for h in range(2):
                product(LAST, 1, h)
            round_gpsimd(LAST, 0)
            copy_plane(2, 0, nc.scalar.copy)
            copy_plane(2, 1, nc.vector.tensor_copy)
            for h in range(2):
                round_from_psum(LAST, 1, h)
            for f in range(2):
                quantize_plane(1, f)
            copy_out(LAST, 1, 0)
            for f in range(2):
                quantize_plane(2, f)
            copy_out(LAST, 1, 1)
            for i in range(2):
                for f in range(2):
                    turn_out_last(i, f, ring_bank() if i == 0 else side_bank())
            for i in range(2):
                copy_plane_last(i, 0, nc.vector.tensor_copy)
                copy_plane_last(i, 1, nc.scalar.copy)
            for c in range(LAST, LAST + 2):
                for f in range(2):
                    quantize_plane(c, f)

            for Q in range(4):
                queue = nc.scalar if Q % 2 == 0 else nc.sync
                queue.dma_start(out=out_2[:, 4 * Q : 4 * Q + 4, :].rearrange("f q n -> q f n").bitcast(I32), in_=out_scales[32 * Q : 32 * Q + 4, :, :].bitcast(I32))
